import numpy as np
import ml_dtypes


def mxq(x, axis, fmt="e4m3"):
    dtype, down = {"e4m3": (ml_dtypes.float8_e4m3fn, 7), "e5m2": (ml_dtypes.float8_e5m2, 14)}[fmt]
    v = np.moveaxis(np.asarray(x, np.float32).astype(ml_dtypes.bfloat16).astype(np.float64), axis, -1)
    blocks = v.reshape(v.shape[:-1] + (-1, 32))
    amax = np.abs(blocks).max(-1, keepdims=True)
    byte = np.maximum(np.where(amax > 0, np.frexp(amax)[1] - 1 + 127, 0) - down, 1)
    scale = np.exp2(byte - 127.0)
    codes = (blocks / scale).astype(np.float32).astype(dtype).astype(np.float64)
    return np.moveaxis((codes * scale).reshape(v.shape), -1, axis)


WIDE = False


def mx_kscale(k):
    if not WIDE:
        return np.ones(k)
    levels = np.array([24, -24, 12, -12, 0])
    if k % 512:
        return np.exp2(np.random.permutation(np.resize(levels, k // 32))).repeat(32)
    a = np.empty((k // 512, 16))
    for p in range(k // 512):
        a[p, :8] = np.random.permutation(np.resize(levels, 8))
        for g in range(8):
            far = levels[np.abs(levels - a[p, g]) >= 10]
            a[p, g + 8] = far[np.random.randint(len(far))]
    return np.exp2(a.ravel()).repeat(32)


def f64(x):
    return np.asarray(x).astype(np.float64)


def striped(idx):
    return np.tile(idx.reshape(-1, 16).T, (8, 1)).astype(np.uint16)


def unstriped(offs):
    return offs[:16].T.reshape(-1).astype(np.int64)


E2M1 = np.array([0.0, 0.5, 1.0, 1.5, 2.0, 3.0, 4.0, 6.0, -0.0, -0.5, -1.0, -1.5, -2.0, -3.0, -4.0, -6.0])


def pack_weight(w, fmt):
    k, n = w.shape
    w = f64(np.asarray(w, np.float32).astype(ml_dtypes.bfloat16)).reshape(k // 32, 32, n)
    amax = np.abs(w).max(1)
    if fmt == "e4m3":
        byte = np.frexp(amax)[1] - 1 + 127 - 7
    else:
        mant, ex = np.frexp(amax / 6.0)
        byte = np.where(mant > 0.5, ex, ex - 1) + 127
    byte = np.clip(np.where(amax > 0, byte, 1), 1, 254)
    scaled = (w * np.exp2(127.0 - byte)[:, None, :]).reshape(k, n).astype(np.float32)
    by_word = np.ascontiguousarray(scaled.reshape(k // 512, 128, 4, n).transpose(0, 1, 3, 2))
    if fmt == "e4m3":
        words = by_word.astype(ml_dtypes.float8_e4m3fn).view(np.uint8)
    else:
        c = by_word.astype(ml_dtypes.float4_e2m1fn).view(np.uint8) & 0xF
        words = (c[..., 0::2] | (c[..., 1::2] << 4)).reshape(k // 512, 128, 2 * n)
    return np.ascontiguousarray(words), np.ascontiguousarray(byte.astype(np.uint8).reshape(k // 512, 16, n))


def unpack_weight(words, scales, fmt):
    g, _, n = scales.shape
    words = np.ascontiguousarray(words).reshape(g, 128, n, -1)
    if fmt == "e4m3":
        vals = words.view(ml_dtypes.float8_e4m3fn).astype(np.float64)
    else:
        nib = np.empty((g, 128, n, 4), np.uint8)
        nib[..., 0::2] = words & 0xF
        nib[..., 1::2] = words >> 4
        vals = E2M1[nib]
    vals = vals * np.repeat(np.exp2(scales.astype(np.float64) - 127.0), 8, axis=1)[..., None]
    return vals.transpose(0, 1, 3, 2).reshape(g * 512, n)


def pack_table4(v):
    words, scales = pack_weight(v, "e2m1")
    g, t = words.shape[0] // 2, v.shape[1]
    return np.ascontiguousarray(words.reshape(g, 2, 128, t, 2).transpose(0, 2, 3, 1, 4).reshape(g, 128, t, 4)), scales


def unpack_table4(words, scales):
    g, _, t, _ = words.shape
    return unpack_weight(words.reshape(g, 128, t, 2, 2).transpose(0, 3, 1, 2, 4).reshape(2 * g, 128, 2 * t), scales, "e2m1")


def sigm(f):
    return 1.0 / (1.0 + np.exp(-np.maximum(f, -700.0)))


K, L, N, T, J = 1024, 512, 512, 2048, 1024


def setup_inputs():
    n = np.random.standard_normal
    s = mx_kscale(K)[:, None]
    s2 = mx_kscale(L)[:, None]
    p_tab = pack_table4(n((K, T)) * s)
    p_tab2 = pack_weight(n((L, T)) * s2, "e4m3")
    p_zv = pack_weight(n((K, N)) / np.sqrt(K) / s, "e2m1")
    p_zt = pack_weight(n((L, N)) / np.sqrt(L) / s2, "e2m1")
    p_wt = pack_weight(n((L, N)) / np.sqrt(L) / s2, "e4m3")
    return {
        "tab_words": p_tab[0],
        "tab_scales": p_tab[1],
        "tab2_words": p_tab2[0],
        "tab2_scales": p_tab2[1],
        "zv_words": p_zv[0],
        "zv_scales": p_zv[1],
        "zt_words": p_zt[0],
        "zt_scales": p_zt[1],
        "b": (0.3 * n(N)).astype(np.float32),
        "wv": (n((K, N)) / np.sqrt(K) / s).astype(np.float32),
        "wt_words": p_wt[0],
        "wt_scales": p_wt[1],
        "offs": striped(np.random.permutation(T)[:J]),
        "offs2": striped(np.random.permutation(T)[:J]),
    }


def reference(tab_words, tab_scales, tab2_words, tab2_scales, zv_words, zv_scales, zt_words, zt_scales, b, wv, wt_words, wt_scales, offs, offs2):
    idx = unstriped(offs)
    idx2 = unstriped(offs2)
    tab_ = unpack_table4(tab_words, tab_scales)[:, idx]
    tab2_ = unpack_weight(tab2_words, tab2_scales, "e4m3")[:, idx2]
    zv_ = unpack_weight(zv_words, zv_scales, "e2m1")
    zt_ = unpack_weight(zt_words, zt_scales, "e2m1")
    z = zv_.T @ tab_ + zt_.T @ tab2_
    gate = sigm(z + f64(b)[:, None])
    wv_ = mxq(f64(wv), 0, "e4m3")
    wt_ = unpack_weight(wt_words, wt_scales, "e4m3")
    hv = wv_.T @ tab_
    ht = wt_.T @ tab2_
    av = np.maximum(hv, 0.0)
    at = np.maximum(ht, 0.0)
    return at + gate * (av - at)

@@ -1,0 +1,210 @@
+from contextlib import ExitStack
+
+import concourse.mybir as mybir
+
+K, L, N, T, J = 1024, 512, 512, 2048, 1024
+FLOPS = 2 * N * J * (2 * K + 2 * L)
+
+F32 = mybir.dt.float32
+BF16 = mybir.dt.bfloat16
+I32 = mybir.dt.int32
+U32 = mybir.dt.uint32
+U16 = mybir.dt.uint16
+U8 = mybir.dt.uint8
+FP8X4 = mybir.dt.float8_e4m3fn_x4
+FP4X4 = mybir.dt.float4_e2m1fn_x4
+ACT = mybir.ActivationFunctionType
+ALU = mybir.AluOpType
+
+P = 128
+CH = 512
+NCH = J // CH
+NT = N // P
+NH = N // 2
+
+
+def tile_list_gmu_relu_none_kernel(
+    tc, tab_words, tab_scales, tab2_words, tab2_scales, zv_words, zv_scales, zt_words, zt_scales,
+    b, wv, wt_words, wt_scales, offs, offs2, out,
+):
+    nc = tc.nc
+    with ExitStack() as ctx:
+        keep = ctx.enter_context(tc.tile_pool(name="keep", bufs=1))
+        lap = ctx.enter_context(tc.tile_pool(name="lap", bufs=1))
+        work = ctx.enter_context(tc.tile_pool(name="work", bufs=1))
+        psum = ctx.enter_context(tc.psum_pool(name="psum", bufs=1))
+
+        def kept(name, shape, dtype):
+            return keep.tile(shape, dtype, name=name, align_bytes=64)
+
+        list1 = kept("list1", [P, J // 16], U16)
+        list2 = kept("list2", [P, J // 16], U16)
+        tab_w = kept("tab_w", [P, T], I32)
+        tab2_w = kept("tab2_w", [P, T], I32)
+        tab_s = kept("tab_s", [P, T], U8)
+        tab2_s = kept("tab2_s", [P, T], U8)
+        zv_w = kept("zv_w", [P, 2, 2 * N], U8)
+        zt_w = kept("zt_w", [P, 2 * N], U8)
+        wt_w = kept("wt_w", [P, N], I32)
+        zv_s = kept("zv_s", [P, 2, N], U8)
+        zt_s = kept("zt_s", [P, N], U8)
+        wt_s = kept("wt_s", [P, N], U8)
+        bias = kept("bias", [P, NT], F32)
+        nbias = kept("nbias", [P, NT], F32)
+        warm = kept("warm", [P, 8], F32)
+        warm_o = kept("warm_o", [P, 8], F32)
+        pieces = [(h, a) for h in range(2) for a in range(2)]
+        wv_raw = {k: kept("wv_raw%d%d" % k, [P, 4, NH], F32) for k in pieces}
+        wv_bf = {k: kept("wv_bf%d%d" % k, [P, NH, 4], BF16) for k in pieces}
+        wv_c = {k: kept("wv_c%d%d" % k, [P, NH], U32) for k in pieces}
+        wv_s = {k: kept("wv_s%d%d" % k, [P, NH], U8) for k in pieces}
+        g_s = kept("g_s", [P, J], U8)
+        g_s1 = kept("g_s1", [P, J], U8)
+        def placed(name, dtype, offset):
+            return lap.tile([P, CH], dtype, name=name, align_bytes=64, offset=offset)
+
+        g_w = [placed("g_w0", U32, 2048), placed("g_w1", U32, 64)]
+        g2_s = [kept("g2_s0", [P, CH], U8), placed("g2_s1", U8, 2112)]
+        g2_w = [kept("g2_w0", [P, CH], U32), placed("g2_w1", U32, 2624)]
+        parted = [kept("parted%d" % c, [P, 2, 2 * CH], U8) for c in range(NCH)]
+
+        nc.gpsimd.memset(tab_s[:].bitcast(I32), 0)
+        nc.vector.memset(wt_s[:].bitcast(I32), 0)
+        nc.vector.memset(warm[:], 0.0)
+        nc.vector.memset(tab2_s[:].bitcast(I32), 0)
+        nc.vector.memset(zt_s[:].bitcast(I32), 0)
+        nc.vector.memset(zv_s[:].rearrange("p a n -> p (a n)").bitcast(I32), 0)
+        nc.vector.memset(g_s1[:].bitcast(I32), 0)
+        nc.scalar.activation(out=warm_o[:], in_=warm[:], func=ACT.Sigmoid)
+
+        def load_scales(eng, tile, src):
+            for q in range(4):
+                eng.dma_start(out=tile[32 * q : 32 * q + 4, :].bitcast(I32), in_=src[4 * q : 4 * q + 4, :].bitcast(I32))
+
+        def load_wv(h, a):
+            nc.sync.dma_start(out=wv_raw[h, a][:], in_=wv[512 * a : 512 * (a + 1), NH * h : NH * (h + 1)].rearrange("(p j) n -> p j n", j=4))
+
+        nc.sync.dma_start(list1[:], offs)
+        for q in range(4):
+            nc.sync.dma_start(out=tab_s[32 * q : 32 * q + 8, :].bitcast(I32), in_=tab_scales[:, 4 * q : 4 * q + 4, :].bitcast(I32))
+        nc.sync.dma_start(list2[:], offs2)
+        load_scales(nc.gpsimd, wt_s, wt_scales[0])
+        nc.sync.dma_start(out=tab2_w[:], in_=tab2_words[0].rearrange("p t i -> p (t i)").bitcast(I32))
+        nc.sync.dma_start(out=wt_w[:], in_=wt_words[0].rearrange("p n i -> p (n i)").bitcast(I32))
+        load_scales(nc.sync, tab2_s, tab2_scales[0])
+        nc.sync.dma_start(out=tab_w[:], in_=tab_words[0].rearrange("p t i -> p (t i)").bitcast(I32))
+        nc.sync.dma_start(out=zt_w[:].bitcast(I32), in_=zt_words[0].bitcast(I32))
+        nc.sync.dma_start(out=zv_w[:].bitcast(I32), in_=zv_words.rearrange("a p n -> p a n").bitcast(I32))
+        load_wv(0, 0)
+        load_scales(nc.sync, zt_s, zt_scales[0])
+        load_wv(0, 1)
+        load_wv(1, 0)
+        load_wv(1, 1)
+
+        def lcols(c):
+            return slice(c * CH // 16, (c + 1) * CH // 16)
+
+        nc.vector.tensor_copy(g_s[:], tab_s[:].indirect(list1[:]))
+        nc.gpsimd.dma_start(out=g_s1[0:100, :].bitcast(I32), in_=g_s[4:104, :].bitcast(I32))
+        for q in range(4):
+            nc.gpsimd.dma_start(
+                out=zv_s[32 * q : 32 * q + 4, :, :].bitcast(I32),
+                in_=zv_scales[:, 4 * q : 4 * q + 4, :].rearrange("a r n -> r a n").bitcast(I32),
+            )
+
+        with nc.allow_non_contiguous_dma(reason="one bias value to a partition"):
+            nc.gpsimd.dma_start(out=bias[:], in_=b.rearrange("(t p) -> p t", p=P))
+        nc.scalar.activation(out=nbias[:], in_=bias[:], func=ACT.Copy, scale=-1.0)
+
+        def gather2s(c):
+            nc.vector.tensor_copy(g2_s[c][:], tab2_s[:].indirect(list2[:, lcols(c)]))
+
+        def gather2w(c):
+            nc.vector.tensor_copy(g2_w[c][:], tab2_w[:].bitcast(U32).indirect(list2[:, lcols(c)]))
+
+        def gather1(c):
+            nc.vector.tensor_copy(g_w[c][:], tab_w[:].bitcast(U32).indirect(list1[:, lcols(c)]))
+
+        def part(c):
+            nc.vector.tensor_copy(parted[c][:].bitcast(U16), g_w[c][:].bitcast(U16).rearrange("p (j d) -> p d j", d=2))
+
+        def cast(a):
+            nc.scalar.copy(
+                out=wv_bf[a][:].rearrange("p (c i) t -> p c t i", i=4),
+                in_=wv_raw[a][:].rearrange("p t (c i) -> p c t i", i=4),
+            )
+
+        def quant(a):
+            nc.vector.quantize_mx(out=wv_c[a][:].bitcast(FP8X4), scales=wv_s[a][:], in_=wv_bf[a][:].rearrange("p n t -> p (n t)"))
+
+        tab_plane = [g_s, g_s1]
+        ht, hv, gate, gbar, t1, t2 = {}, {}, {}, {}, {}, {}
+
+        def mm_ht(c, t):
+            cols = slice(t * P, (t + 1) * P)
+            ht[c, t] = psum.tile([P, CH], F32, name="ht", bufs=4)
+            nc.tensor.matmul_mx(out=ht[c, t][:], lhsT=wt_w[:, cols].bitcast(FP8X4), lhsT_scale=wt_s[:, cols],
+                                rhs=g2_w[c][:].bitcast(FP8X4), rhs_scale=g2_s[c][:], start=True, stop=True)
+
+        def mm_z(c, t):
+            cols = slice(t * P, (t + 1) * P)
+            cols2 = slice(2 * t * P, 2 * (t + 1) * P)
+            jc = slice(c * CH, (c + 1) * CH)
+            z = psum.tile([P, CH], F32, name="z", bufs=2)
+            nc.tensor.matmul_mx(out=z[:], lhsT=zt_w[:, cols2].bitcast(FP4X4), lhsT_scale=zt_s[:, cols],
+                                rhs=g2_w[c][:].bitcast(FP8X4), rhs_scale=g2_s[c][:], start=True, stop=False)
+            for a in range(2):
+                nc.tensor.matmul_mx(out=z[:], lhsT=zv_w[:, a, cols2].bitcast(FP4X4), lhsT_scale=zv_s[:, a, cols],
+                                    rhs=parted[c][:, a, :].bitcast(FP4X4), rhs_scale=tab_plane[a][:, jc], start=False, stop=(a == 1))
+            gbar[c, t] = work.tile([P, CH], F32, name="gbar", bufs=8)
+            gate[c, t] = work.tile([P, CH], F32, name="gate", bufs=8)
+            nc.scalar.activation(out=gbar[c, t][:], in_=z[:], func=ACT.Sigmoid, bias=nbias[:, t : t + 1], scale=-1.0)
+            nc.scalar.activation(out=gate[c, t][:], in_=z[:], func=ACT.Sigmoid, bias=bias[:, t : t + 1], scale=1.0)
+
+        def mm_hv(c, t):
+            cols = slice((t % 2) * P, (t % 2 + 1) * P)
+            jc = slice(c * CH, (c + 1) * CH)
+            hv[c, t] = psum.tile([P, CH], F32, name="hv", bufs=2)
+            for a in range(2):
+                nc.tensor.matmul_mx(out=hv[c, t][:], lhsT=wv_c[t // 2, a][:, cols].bitcast(FP8X4), lhsT_scale=wv_s[t // 2, a][:, cols],
+                                    rhs=parted[c][:, a, :].bitcast(FP4X4), rhs_scale=tab_plane[a][:, jc], start=(a == 0), stop=(a == 1))
+
+        def finish(c, t, eng):
+            t2[c, t] = work.tile([P, CH], F32, name="t2", bufs=4)
+            t1[c, t] = work.tile([P, CH], F32, name="t1", bufs=4)
+            res = work.tile([P, CH], F32, name="res", bufs=8)
+            nc.vector.scalar_tensor_tensor(out=t2[c, t][:], in0=ht[c, t][:], scalar=0.0, in1=gbar[c, t][:], op0=ALU.max, op1=ALU.mult)
+            nc.vector.scalar_tensor_tensor(out=t1[c, t][:], in0=hv[c, t][:], scalar=0.0, in1=gate[c, t][:], op0=ALU.max, op1=ALU.mult)
+            eng.tensor_tensor(out=res[:], in0=t1[c, t][:], in1=t2[c, t][:], op=ALU.add)
+            nc.sync.dma_start(out=out[t * P : (t + 1) * P, c * CH : (c + 1) * CH], in_=res[:])
+
+        gather2w(0)
+        gather2s(0)
+        gather1(0)
+        for t in range(NT):
+            mm_ht(0, t)
+        part(0)
+        cast((0, 0))
+        cast((0, 1))
+        gather1(1)
+        gather2s(1)
+        part(1)
+        mm_z(0, 0)
+        quant((0, 0))
+        quant((0, 1))
+        cast((1, 0))
+        gather2w(1)
+        mm_z(0, 1)
+        cast((1, 1))
+        quant((1, 0))
+        mm_z(0, 2)
+        quant((1, 1))
+        mm_z(0, 3)
+        for t in range(NT):
+            mm_hv(0, t)
+            finish(0, t, nc.gpsimd)
+        for t in range(NT):
+            mm_z(1, t)
+            mm_ht(1, t)
+            mm_hv(1, t)
+            finish(1, t, nc.vector if t == NT - 1 else nc.gpsimd)

@@ -17,10 +17,14 @@ ACT = mybir.ActivationFunctionType
 ALU = mybir.AluOpType
 
 P = 128
-CH = 512
-NCH = J // CH
-NT = N // P
-NH = N // 2
+K_PASS = 512
+PASSES = K // K_PASS
+CHUNK = 512
+N_TILES = N // P
+HALF = N // 2
+QUADS = 4
+PASS1_SHIFT = 16
+BANKS = 8
 
 
 def tile_list_gmu_relu_none_kernel(
@@ -30,8 +34,8 @@ def tile_list_gmu_relu_none_kernel(
     nc = tc.nc
     with ExitStack() as ctx:
         keep = ctx.enter_context(tc.tile_pool(name="keep", bufs=1))
-        lap = ctx.enter_context(tc.tile_pool(name="lap", bufs=1))
-        work = ctx.enter_context(tc.tile_pool(name="work", bufs=1))
+        lapped = ctx.enter_context(tc.tile_pool(name="lapped", bufs=1))
+        work = ctx.enter_context(tc.tile_pool(name="work", bufs=2 * N_TILES))
         psum = ctx.enter_context(tc.psum_pool(name="psum", bufs=1))
 
         def kept(name, shape, dtype):
@@ -43,168 +47,222 @@ def tile_list_gmu_relu_none_kernel(
         tab2_w = kept("tab2_w", [P, T], I32)
         tab_s = kept("tab_s", [P, T], U8)
         tab2_s = kept("tab2_s", [P, T], U8)
-        zv_w = kept("zv_w", [P, 2, 2 * N], U8)
+        zv_w = kept("zv_w", [P, PASSES, 2 * N], U8)
         zt_w = kept("zt_w", [P, 2 * N], U8)
         wt_w = kept("wt_w", [P, N], I32)
-        zv_s = kept("zv_s", [P, 2, N], U8)
-        zt_s = kept("zt_s", [P, N], U8)
-        wt_s = kept("wt_s", [P, N], U8)
-        bias = kept("bias", [P, NT], F32)
-        nbias = kept("nbias", [P, NT], F32)
-        warm = kept("warm", [P, 8], F32)
-        warm_o = kept("warm_o", [P, 8], F32)
-        pieces = [(h, a) for h in range(2) for a in range(2)]
-        wv_raw = {k: kept("wv_raw%d%d" % k, [P, 4, NH], F32) for k in pieces}
-        wv_bf = {k: kept("wv_bf%d%d" % k, [P, NH, 4], BF16) for k in pieces}
-        wv_c = {k: kept("wv_c%d%d" % k, [P, NH], U32) for k in pieces}
-        wv_s = {k: kept("wv_s%d%d" % k, [P, NH], U8) for k in pieces}
-        g_s = kept("g_s", [P, J], U8)
-        g_s1 = kept("g_s1", [P, J], U8)
-        def placed(name, dtype, offset):
-            return lap.tile([P, CH], dtype, name=name, align_bytes=64, offset=offset)
+        weight_s = kept("weight_s", [P, 4 * N], U8)
+        zv_s = [weight_s[:, 0:N], weight_s[:, N : 2 * N]]
+        zt_s = weight_s[:, 2 * N : 3 * N]
+        wt_s = weight_s[:, 3 * N : 4 * N]
+        bias = kept("bias", [P, N_TILES], F32)
+        neg_bias = kept("neg_bias", [P, N_TILES], F32)
+        warm_in = kept("warm_in", [P, 8], F32)
+        warm_out = kept("warm_out", [P, 8], F32)
+        wv_raw = [[kept("wv_raw%d%d" % (h, a), [P, 4, HALF], F32) for a in range(PASSES)] for h in range(2)]
+        wv_bf = [kept("wv_bf%d" % h, [P, PASSES, HALF, 4], BF16) for h in range(2)]
+        wv_w = [kept("wv_w%d" % h, [P, PASSES, HALF], U32) for h in range(2)]
+        wv_s = [kept("wv_s%d" % h, [P, PASSES, HALF], U8) for h in range(2)]
+        picked_s = kept("picked_s", [P, J], U8)
+        picked_s_pass1 = kept("picked_s_pass1", [P, J], U8)
+        picked_planes = [picked_s, picked_s_pass1]
+        picked2_s = [kept("picked2_s%d" % c, [P, CHUNK], U8) for c in range(2)]
+        parted = [kept("parted%d" % c, [P, PASSES, 2 * CHUNK], U8) for c in range(2)]
 
-        g_w = [placed("g_w0", U32, 2048), placed("g_w1", U32, 64)]
-        g2_s = [kept("g2_s0", [P, CH], U8), placed("g2_s1", U8, 2112)]
-        g2_w = [kept("g2_w0", [P, CH], U32), placed("g2_w1", U32, 2624)]
-        parted = [kept("parted%d" % c, [P, 2, 2 * CH], U8) for c in range(NCH)]
+        word_bytes = 4 * CHUNK
 
-        nc.gpsimd.memset(tab_s[:].bitcast(I32), 0)
-        nc.vector.memset(wt_s[:].bitcast(I32), 0)
-        nc.vector.memset(warm[:], 0.0)
-        nc.vector.memset(tab2_s[:].bitcast(I32), 0)
-        nc.vector.memset(zt_s[:].bitcast(I32), 0)
-        nc.vector.memset(zv_s[:].rearrange("p a n -> p (a n)").bitcast(I32), 0)
-        nc.vector.memset(g_s1[:].bitcast(I32), 0)
-        nc.scalar.activation(out=warm_o[:], in_=warm[:], func=ACT.Sigmoid)
+        def placed(name, offset):
+            return lapped.tile([P, CHUNK], U32, name=name, align_bytes=64, offset=offset)
 
-        def load_scales(eng, tile, src):
-            for q in range(4):
-                eng.dma_start(out=tile[32 * q : 32 * q + 4, :].bitcast(I32), in_=src[4 * q : 4 * q + 4, :].bitcast(I32))
+        picked_w = [placed("picked_w0", word_bytes // 2), placed("picked_w1", 0)]
+        picked2_w = [kept("picked2_w0", [P, CHUNK], U32), placed("picked2_w1", word_bytes)]
+
+        for tile in (tab_s, weight_s, tab2_s, picked_s_pass1):
+            nc.vector.memset(tile[:].bitcast(I32), 0)
+        nc.vector.memset(warm_in[:], 0.0)
+        nc.scalar.activation(out=warm_out[:], in_=warm_in[:], func=ACT.Sigmoid)
+
+        def load_bytes(dst, src):
+            nc.sync.dma_start(out=dst.bitcast(I32), in_=src.bitcast(I32))
 
         def load_wv(h, a):
-            nc.sync.dma_start(out=wv_raw[h, a][:], in_=wv[512 * a : 512 * (a + 1), NH * h : NH * (h + 1)].rearrange("(p j) n -> p j n", j=4))
+            rows = wv[K_PASS * a : K_PASS * (a + 1), HALF * h : HALF * (h + 1)]
+            nc.sync.dma_start(out=wv_raw[h][a][:], in_=rows.rearrange("(p i) n -> p i n", i=4))
+
+        def list_cols(c):
+            return slice(c * CHUNK // 16, (c + 1) * CHUNK // 16)
+
+        def chunk_cols(c):
+            return slice(c * CHUNK, (c + 1) * CHUNK)
 
         nc.sync.dma_start(list1[:], offs)
-        for q in range(4):
-            nc.sync.dma_start(out=tab_s[32 * q : 32 * q + 8, :].bitcast(I32), in_=tab_scales[:, 4 * q : 4 * q + 4, :].bitcast(I32))
+        for r in range(4):
+            load_bytes(tab_s[r:P:PASS1_SHIFT, :], tab_scales[:, r:16:4, :].rearrange("a g t -> g a t"))
         nc.sync.dma_start(list2[:], offs2)
-        load_scales(nc.gpsimd, wt_s, wt_scales[0])
-        nc.sync.dma_start(out=tab2_w[:], in_=tab2_words[0].rearrange("p t i -> p (t i)").bitcast(I32))
-        nc.sync.dma_start(out=wt_w[:], in_=wt_words[0].rearrange("p n i -> p (n i)").bitcast(I32))
-        load_scales(nc.sync, tab2_s, tab2_scales[0])
-        nc.sync.dma_start(out=tab_w[:], in_=tab_words[0].rearrange("p t i -> p (t i)").bitcast(I32))
-        nc.sync.dma_start(out=zt_w[:].bitcast(I32), in_=zt_words[0].bitcast(I32))
-        nc.sync.dma_start(out=zv_w[:].bitcast(I32), in_=zv_words.rearrange("a p n -> p a n").bitcast(I32))
+        load_bytes(wt_s[0:16, :], wt_scales[0])
+        load_bytes(tab2_w[:], tab2_words[0].rearrange("p t i -> p (t i)"))
+        for g in range(QUADS):
+            load_bytes(tab2_s[32 * g : 32 * g + 4, :], tab2_scales[0, 4 * g : 4 * g + 4, :])
+        load_bytes(zt_s[0:16, :], zt_scales[0])
+        load_bytes(weight_s[0:16, 0 : 2 * N].rearrange("q (a n) -> q a n", a=PASSES), zv_scales.rearrange("a q n -> q a n"))
+        load_bytes(tab_w[:], tab_words[0].rearrange("p t i -> p (t i)"))
+        for g in range(1, QUADS):
+            load_bytes(weight_s[32 * g : 32 * g + 4, :], weight_s[4 * g : 4 * g + 4, :])
+        load_bytes(zt_w[:], zt_words[0])
         load_wv(0, 0)
-        load_scales(nc.sync, zt_s, zt_scales[0])
+        load_bytes(zv_w[:], zv_words.rearrange("a p n -> p a n"))
         load_wv(0, 1)
+        nc.vector.tensor_copy(picked_s[:], tab_s[:].indirect(list1[:]))
+        load_bytes(picked_s_pass1[0 : P - PASS1_SHIFT, :], picked_s[PASS1_SHIFT:P, :])
+        with nc.allow_non_contiguous_dma(reason="one bias value to a partition"):
+            nc.sync.dma_start(out=bias[:], in_=b.rearrange("(t p) -> p t", p=P))
+        nc.scalar.activation(out=neg_bias[:], in_=bias[:], func=ACT.Copy, scale=-1.0)
+        load_bytes(wt_w[:], wt_words[0].rearrange("p n i -> p (n i)"))
         load_wv(1, 0)
         load_wv(1, 1)
 
-        def lcols(c):
-            return slice(c * CH // 16, (c + 1) * CH // 16)
+        def gather_tab2_scales(c):
+            nc.vector.tensor_copy(picked2_s[c][:], tab2_s[:].indirect(list2[:, list_cols(c)]))
 
-        nc.vector.tensor_copy(g_s[:], tab_s[:].indirect(list1[:]))
-        nc.gpsimd.dma_start(out=g_s1[0:100, :].bitcast(I32), in_=g_s[4:104, :].bitcast(I32))
-        for q in range(4):
-            nc.gpsimd.dma_start(
-                out=zv_s[32 * q : 32 * q + 4, :, :].bitcast(I32),
-                in_=zv_scales[:, 4 * q : 4 * q + 4, :].rearrange("a r n -> r a n").bitcast(I32),
-            )
+        def gather_tab2_words(c):
+            nc.vector.tensor_copy(picked2_w[c][:], tab2_w[:].bitcast(U32).indirect(list2[:, list_cols(c)]))
 
-        with nc.allow_non_contiguous_dma(reason="one bias value to a partition"):
-            nc.gpsimd.dma_start(out=bias[:], in_=b.rearrange("(t p) -> p t", p=P))
-        nc.scalar.activation(out=nbias[:], in_=bias[:], func=ACT.Copy, scale=-1.0)
+        def gather_tab_words(c):
+            nc.vector.tensor_copy(picked_w[c][:], tab_w[:].bitcast(U32).indirect(list1[:, list_cols(c)]))
 
-        def gather2s(c):
-            nc.vector.tensor_copy(g2_s[c][:], tab2_s[:].indirect(list2[:, lcols(c)]))
+        def part_passes(c):
+            nc.vector.tensor_copy(parted[c][:].bitcast(U16), picked_w[c][:].bitcast(U16).rearrange("p (j a) -> p a j", a=PASSES))
 
-        def gather2w(c):
-            nc.vector.tensor_copy(g2_w[c][:], tab2_w[:].bitcast(U32).indirect(list2[:, lcols(c)]))
-
-        def gather1(c):
-            nc.vector.tensor_copy(g_w[c][:], tab_w[:].bitcast(U32).indirect(list1[:, lcols(c)]))
-
-        def part(c):
-            nc.vector.tensor_copy(parted[c][:].bitcast(U16), g_w[c][:].bitcast(U16).rearrange("p (j d) -> p d j", d=2))
-
-        def cast(a):
+        def round_wv(h, a):
             nc.scalar.copy(
-                out=wv_bf[a][:].rearrange("p (c i) t -> p c t i", i=4),
-                in_=wv_raw[a][:].rearrange("p t (c i) -> p c t i", i=4),
+                out=wv_bf[h][:, a].rearrange("p (n m) i -> p n i m", m=4),
+                in_=wv_raw[h][a][:].rearrange("p i (n m) -> p n i m", m=4),
             )
 
-        def quant(a):
-            nc.vector.quantize_mx(out=wv_c[a][:].bitcast(FP8X4), scales=wv_s[a][:], in_=wv_bf[a][:].rearrange("p n t -> p (n t)"))
+        def quantise_wv(h):
+            nc.vector.quantize_mx(
+                out=wv_w[h][:].rearrange("p a n -> p (a n)").bitcast(FP8X4),
+                scales=wv_s[h][:].rearrange("p a n -> p (a n)"),
+                in_=wv_bf[h][:].rearrange("p a n i -> p (a n i)"),
+            )
 
-        tab_plane = [g_s, g_s1]
-        ht, hv, gate, gbar, t1, t2 = {}, {}, {}, {}, {}, {}
+        free_banks = list(range(BANKS))
+        sums, gate, rest, from_v, from_t = {}, {}, {}, {}, {}
 
-        def mm_ht(c, t):
+        def new_sum(kind, c, t):
+            bank = free_banks.pop(0)
+            acc = psum.tile([P, CHUNK], F32, name=kind, tag="bank%d" % bank)
+            sums[kind, c, t] = (acc, bank)
+            return acc
+
+        def release(kind, c, t):
+            free_banks.append(sums[kind, c, t][1])
+
+        def sum_ht(c, t):
             cols = slice(t * P, (t + 1) * P)
-            ht[c, t] = psum.tile([P, CH], F32, name="ht", bufs=4)
-            nc.tensor.matmul_mx(out=ht[c, t][:], lhsT=wt_w[:, cols].bitcast(FP8X4), lhsT_scale=wt_s[:, cols],
-                                rhs=g2_w[c][:].bitcast(FP8X4), rhs_scale=g2_s[c][:], start=True, stop=True)
+            nc.tensor.matmul_mx(
+                out=new_sum("ht", c, t)[:], lhsT=wt_w[:, cols].bitcast(FP8X4), lhsT_scale=wt_s[:, cols],
+                rhs=picked2_w[c][:].bitcast(FP8X4), rhs_scale=picked2_s[c][:], start=True, stop=True,
+            )
 
-        def mm_z(c, t):
+        def sum_hv(c, t):
+            h, cols = t // 2, slice(t % 2 * P, (t % 2 + 1) * P)
+            acc = new_sum("hv", c, t)
+            for a in range(PASSES):
+                nc.tensor.matmul_mx(
+                    out=acc[:], lhsT=wv_w[h][:, a, cols].bitcast(FP8X4), lhsT_scale=wv_s[h][:, a, cols],
+                    rhs=parted[c][:, a, :].bitcast(FP4X4), rhs_scale=picked_planes[a][:, chunk_cols(c)],
+                    start=(a == 0), stop=(a == PASSES - 1),
+                )
+
+        def make_gate(c, t, rest_on_gpsimd):
             cols = slice(t * P, (t + 1) * P)
-            cols2 = slice(2 * t * P, 2 * (t + 1) * P)
-            jc = slice(c * CH, (c + 1) * CH)
-            z = psum.tile([P, CH], F32, name="z", bufs=2)
-            nc.tensor.matmul_mx(out=z[:], lhsT=zt_w[:, cols2].bitcast(FP4X4), lhsT_scale=zt_s[:, cols],
-                                rhs=g2_w[c][:].bitcast(FP8X4), rhs_scale=g2_s[c][:], start=True, stop=False)
-            for a in range(2):
-                nc.tensor.matmul_mx(out=z[:], lhsT=zv_w[:, a, cols2].bitcast(FP4X4), lhsT_scale=zv_s[:, a, cols],
-                                    rhs=parted[c][:, a, :].bitcast(FP4X4), rhs_scale=tab_plane[a][:, jc], start=False, stop=(a == 1))
-            gbar[c, t] = work.tile([P, CH], F32, name="gbar", bufs=8)
-            gate[c, t] = work.tile([P, CH], F32, name="gate", bufs=8)
-            nc.scalar.activation(out=gbar[c, t][:], in_=z[:], func=ACT.Sigmoid, bias=nbias[:, t : t + 1], scale=-1.0)
+            byte_cols = slice(2 * t * P, 2 * (t + 1) * P)
+            z = new_sum("z", c, t)
+            nc.tensor.matmul_mx(
+                out=z[:], lhsT=zt_w[:, byte_cols].bitcast(FP4X4), lhsT_scale=zt_s[:, cols],
+                rhs=picked2_w[c][:].bitcast(FP8X4), rhs_scale=picked2_s[c][:], start=True, stop=False,
+            )
+            for a in range(PASSES):
+                nc.tensor.matmul_mx(
+                    out=z[:], lhsT=zv_w[:, a, byte_cols].bitcast(FP4X4), lhsT_scale=zv_s[a][:, cols],
+                    rhs=parted[c][:, a, :].bitcast(FP4X4), rhs_scale=picked_planes[a][:, chunk_cols(c)],
+                    start=False, stop=(a == PASSES - 1),
+                )
+            gate[c, t] = work.tile([P, CHUNK], F32, name="gate")
+            rest[c, t] = work.tile([P, CHUNK], F32, name="rest")
+            if not rest_on_gpsimd:
+                nc.scalar.activation(out=rest[c, t][:], in_=z[:], func=ACT.Sigmoid, bias=neg_bias[:, t : t + 1], scale=-1.0)
             nc.scalar.activation(out=gate[c, t][:], in_=z[:], func=ACT.Sigmoid, bias=bias[:, t : t + 1], scale=1.0)
+            if rest_on_gpsimd:
+                nc.gpsimd.tensor_scalar(out=rest[c, t][:], in0=gate[c, t][:], scalar1=-1.0, scalar2=1.0, op0=ALU.mult, op1=ALU.add)
+            release("z", c, t)
 
-        def mm_hv(c, t):
-            cols = slice((t % 2) * P, (t % 2 + 1) * P)
-            jc = slice(c * CH, (c + 1) * CH)
-            hv[c, t] = psum.tile([P, CH], F32, name="hv", bufs=2)
-            for a in range(2):
-                nc.tensor.matmul_mx(out=hv[c, t][:], lhsT=wv_c[t // 2, a][:, cols].bitcast(FP8X4), lhsT_scale=wv_s[t // 2, a][:, cols],
-                                    rhs=parted[c][:, a, :].bitcast(FP4X4), rhs_scale=tab_plane[a][:, jc], start=(a == 0), stop=(a == 1))
+        def spans(parts):
+            return [slice(i * CHUNK // parts, (i + 1) * CHUNK // parts) for i in range(parts)]
 
-        def finish(c, t, eng):
-            t2[c, t] = work.tile([P, CH], F32, name="t2", bufs=4)
-            t1[c, t] = work.tile([P, CH], F32, name="t1", bufs=4)
-            res = work.tile([P, CH], F32, name="res", bufs=8)
-            nc.vector.scalar_tensor_tensor(out=t2[c, t][:], in0=ht[c, t][:], scalar=0.0, in1=gbar[c, t][:], op0=ALU.max, op1=ALU.mult)
-            nc.vector.scalar_tensor_tensor(out=t1[c, t][:], in0=hv[c, t][:], scalar=0.0, in1=gate[c, t][:], op0=ALU.max, op1=ALU.mult)
-            eng.tensor_tensor(out=res[:], in0=t1[c, t][:], in1=t2[c, t][:], op=ALU.add)
-            nc.sync.dma_start(out=out[t * P : (t + 1) * P, c * CH : (c + 1) * CH], in_=res[:])
+        def products(c, t, parts=1):
+            from_t[c, t] = work.tile([P, CHUNK], F32, name="from_t")
+            from_v[c, t] = work.tile([P, CHUNK], F32, name="from_v")
+            nc.vector.scalar_tensor_tensor(
+                out=from_t[c, t][:], in0=sums["ht", c, t][0][:], scalar=0.0, in1=rest[c, t][:], op0=ALU.max, op1=ALU.mult
+            )
+            release("ht", c, t)
+            for s in spans(parts):
+                nc.vector.scalar_tensor_tensor(
+                    out=from_v[c, t][:, s], in0=sums["hv", c, t][0][:, s], scalar=0.0, in1=gate[c, t][:, s], op0=ALU.max, op1=ALU.mult
+                )
+            release("hv", c, t)
 
-        gather2w(0)
-        gather2s(0)
-        gather1(0)
-        for t in range(NT):
-            mm_ht(0, t)
-        part(0)
-        cast((0, 0))
-        cast((0, 1))
-        gather1(1)
-        gather2s(1)
-        part(1)
-        mm_z(0, 0)
-        quant((0, 0))
-        quant((0, 1))
-        cast((1, 0))
-        gather2w(1)
-        mm_z(0, 1)
-        cast((1, 1))
-        quant((1, 0))
-        mm_z(0, 2)
-        quant((1, 1))
-        mm_z(0, 3)
-        for t in range(NT):
-            mm_hv(0, t)
-            finish(0, t, nc.gpsimd)
-        for t in range(NT):
-            mm_z(1, t)
-            mm_ht(1, t)
-            mm_hv(1, t)
-            finish(1, t, nc.vector if t == NT - 1 else nc.gpsimd)
+        def add_and_store(c, t, engine, parts=1):
+            result = work.tile([P, CHUNK], F32, name="result")
+            for s in spans(parts):
+                engine.tensor_tensor(out=result[:, s], in0=from_v[c, t][:, s], in1=from_t[c, t][:, s], op=ALU.add)
+                nc.sync.dma_start(out=out[t * P : (t + 1) * P, chunk_cols(c)][:, s], in_=result[:, s])
+
+        def finish(c, t):
+            products(c, t)
+            add_and_store(c, t, nc.gpsimd)
+
+        gather_tab2_words(0)
+        gather_tab2_scales(0)
+        gather_tab2_scales(1)
+        gather_tab_words(0)
+        part_passes(0)
+        round_wv(0, 0)
+        gather_tab_words(1)
+        part_passes(1)
+        gather_tab2_words(1)
+        round_wv(0, 1)
+        quantise_wv(0)
+
+        for t in range(N_TILES):
+            make_gate(0, t, rest_on_gpsimd=True)
+        for t in range(N_TILES):
+            sum_ht(0, t)
+        for t in (0, 1):
+            sum_hv(0, t)
+            finish(0, t)
+        round_wv(1, 0)
+        round_wv(1, 1)
+        make_gate(1, 0, False)
+        sum_ht(1, 0)
+        sum_hv(1, 0)
+        finish(1, 0)
+        quantise_wv(1)
+        make_gate(1, 1, False)
+        for t in (2, 3):
+            sum_hv(0, t)
+            finish(0, t)
+        make_gate(1, 2, False)
+        sum_ht(1, 1)
+        sum_hv(1, 1)
+        finish(1, 1)
+        make_gate(1, 3, False)
+        sum_ht(1, 2)
+        sum_hv(1, 2)
+        products(1, 2)
+        sum_ht(1, 3)
+        sum_hv(1, 3)
+        products(1, 3, parts=2)
+        add_and_store(1, 2, nc.vector)
+        add_and_store(1, 3, nc.vector, parts=2)

@@ -70,11 +70,14 @@ def tile_list_gmu_relu_none_kernel(
 
         word_bytes = 4 * CHUNK
 
-        def placed(name, offset):
-            return lapped.tile([P, CHUNK], U32, name=name, align_bytes=64, offset=offset)
+        def placed(name, entries, offset):
+            return lapped.tile([P, entries], U32, name=name, align_bytes=64, offset=offset)
 
-        picked_w = [placed("picked_w0", word_bytes // 2), placed("picked_w1", 0)]
-        picked2_w = [kept("picked2_w0", [P, CHUNK], U32), placed("picked2_w1", word_bytes)]
+        picked_w = [
+            [(0, CHUNK // 2, placed("picked_w0a", CHUNK // 2, word_bytes // 2)), (CHUNK // 2, CHUNK // 2, placed("picked_w0b", CHUNK // 2, word_bytes))],
+            [(CHUNK, CHUNK, placed("picked_w1", CHUNK, 0))],
+        ]
+        picked2_w = [kept("picked2_w0", [P, CHUNK], U32), placed("picked2_w1", CHUNK, word_bytes)]
 
         for tile in (tab_s, weight_s, tab2_s, picked_s_pass1):
             nc.vector.memset(tile[:].bitcast(I32), 0)
@@ -127,10 +130,15 @@ def tile_list_gmu_relu_none_kernel(
             nc.vector.tensor_copy(picked2_w[c][:], tab2_w[:].bitcast(U32).indirect(list2[:, list_cols(c)]))
 
         def gather_tab_words(c):
-            nc.vector.tensor_copy(picked_w[c][:], tab_w[:].bitcast(U32).indirect(list1[:, list_cols(c)]))
+            for first, entries, tile in picked_w[c]:
+                nc.vector.tensor_copy(tile[:], tab_w[:].bitcast(U32).indirect(list1[:, first // 16 : (first + entries) // 16]))
 
         def part_passes(c):
-            nc.vector.tensor_copy(parted[c][:].bitcast(U16), picked_w[c][:].bitcast(U16).rearrange("p (j a) -> p a j", a=PASSES))
+            for first, entries, tile in picked_w[c]:
+                at = first % CHUNK
+                nc.vector.tensor_copy(
+                    parted[c][:].bitcast(U16)[:, :, at : at + entries], tile[:].bitcast(U16).rearrange("p (j a) -> p a j", a=PASSES)
+                )
 
         def round_wv(h, a):
             nc.scalar.copy(
@@ -230,8 +238,8 @@ def tile_list_gmu_relu_none_kernel(
         part_passes(0)
         round_wv(0, 0)
         gather_tab_words(1)
-        part_passes(1)
         gather_tab2_words(1)
+        part_passes(1)
         round_wv(0, 1)
         quantise_wv(0)
 

@@ -55,37 +55,43 @@ def tile_list_gmu_relu_none_kernel(
         zt_s = weight_s[:, 2 * N : 3 * N]
         wt_s = weight_s[:, 3 * N : 4 * N]
         bias = kept("bias", [P, N_TILES], F32)
-        neg_bias = kept("neg_bias", [P, N_TILES], F32)
         warm_in = kept("warm_in", [P, 8], F32)
         warm_out = kept("warm_out", [P, 8], F32)
-        wv_raw = [[kept("wv_raw%d%d" % (h, a), [P, 4, HALF], F32) for a in range(PASSES)] for h in range(2)]
-        wv_bf = [kept("wv_bf%d" % h, [P, PASSES, HALF, 4], BF16) for h in range(2)]
         wv_w = [kept("wv_w%d" % h, [P, PASSES, HALF], U32) for h in range(2)]
         wv_s = [kept("wv_s%d" % h, [P, PASSES, HALF], U8) for h in range(2)]
         picked_s = kept("picked_s", [P, J], U8)
-        picked_s_pass1 = kept("picked_s_pass1", [P, J], U8)
-        picked_planes = [picked_s, picked_s_pass1]
-        picked2_s = [kept("picked2_s%d" % c, [P, CHUNK], U8) for c in range(2)]
-        parted = [kept("parted%d" % c, [P, PASSES, 2 * CHUNK], U8) for c in range(2)]
-
+        planes = kept("planes", [P, PASSES, J], U8)
+        picked_planes = [planes[:, a, :] for a in range(PASSES)]
         word_bytes = 4 * CHUNK
 
-        def placed(name, entries, offset):
-            return lapped.tile([P, entries], U32, name=name, align_bytes=64, offset=offset)
+        def placed(name, shape, dtype, offset):
+            return lapped.tile(shape, dtype, name=name, align_bytes=64, offset=offset)
 
         picked_w = [
-            [(0, CHUNK // 2, placed("picked_w0a", CHUNK // 2, word_bytes // 2)), (CHUNK // 2, CHUNK // 2, placed("picked_w0b", CHUNK // 2, word_bytes))],
-            [(CHUNK, CHUNK, placed("picked_w1", CHUNK, 0))],
+            [(0, CHUNK // 2, placed("picked_w0a", [P, CHUNK // 2], U32, word_bytes - 256)),
+             (CHUNK // 2, CHUNK // 2, kept("picked_w0b", [P, CHUNK // 2], U32))],
+            [(CHUNK, CHUNK, placed("picked_w1", [P, CHUNK], U32, 0))],
         ]
-        picked2_w = [kept("picked2_w0", [P, CHUNK], U32), placed("picked2_w1", CHUNK, word_bytes)]
+        picked2_s = [kept("picked2_s0", [P, CHUNK], U8), placed("picked2_s1", [P, CHUNK], U8, word_bytes)]
+        picked2_w = [kept("picked2_w0", [P, CHUNK], U32), placed("picked2_w1", [P, CHUNK], U32, word_bytes + CHUNK)]
+        bf_at = 3 * word_bytes
+        wv_bf = [placed("wv_bf0", [P, PASSES, HALF, 4], BF16, bf_at), kept("wv_bf1", [P, PASSES, HALF, 4], BF16)]
+        parted = [kept("parted0", [P, PASSES, 2 * CHUNK], U8), placed("parted1", [P, PASSES, 2 * CHUNK], U8, bf_at + word_bytes // 2)]
 
-        for tile in (tab_s, weight_s, tab2_s, picked_s_pass1):
-            nc.vector.memset(tile[:].bitcast(I32), 0)
+        raw_at = 6 * word_bytes
+        wv_raw = [[kept("wv_raw00", [P, 4, HALF], F32), placed("wv_raw01", [P, 4, HALF], F32, raw_at)],
+                  [kept("wv_raw1%d" % a, [P, 4, HALF], F32) for a in range(PASSES)]]
+        signed_bias = placed("signed_bias", [P, 2, N_TILES], F32, raw_at)
+
+        nc.vector.memset(weight_s[:].bitcast(I32), 0)
+        nc.vector.memset(tab2_s[:].bitcast(I32), 0)
+        nc.vector.memset(tab_s[0:96, :].bitcast(I32), 0)
+        nc.vector.memset(planes[:].rearrange("p a j -> p (a j)").bitcast(I32), 0)
         nc.vector.memset(warm_in[:], 0.0)
         nc.scalar.activation(out=warm_out[:], in_=warm_in[:], func=ACT.Sigmoid)
 
-        def load_bytes(dst, src):
-            nc.sync.dma_start(out=dst.bitcast(I32), in_=src.bitcast(I32))
+        def load_bytes(dst, src, queue=nc.sync):
+            queue.dma_start(out=dst.bitcast(I32), in_=src.bitcast(I32))
 
         def load_wv(h, a):
             rows = wv[K_PASS * a : K_PASS * (a + 1), HALF * h : HALF * (h + 1)]
@@ -98,29 +104,30 @@ def tile_list_gmu_relu_none_kernel(
             return slice(c * CHUNK, (c + 1) * CHUNK)
 
         nc.sync.dma_start(list1[:], offs)
-        for r in range(4):
-            load_bytes(tab_s[r:P:PASS1_SHIFT, :], tab_scales[:, r:16:4, :].rearrange("a g t -> g a t"))
+        load_bytes(tab_s[96:128, :], tab_scales.rearrange("a q t -> q a t"))
         nc.sync.dma_start(list2[:], offs2)
         load_bytes(wt_s[0:16, :], wt_scales[0])
         load_bytes(tab2_w[:], tab2_words[0].rearrange("p t i -> p (t i)"))
-        for g in range(QUADS):
-            load_bytes(tab2_s[32 * g : 32 * g + 4, :], tab2_scales[0, 4 * g : 4 * g + 4, :])
         load_bytes(zt_s[0:16, :], zt_scales[0])
         load_bytes(weight_s[0:16, 0 : 2 * N].rearrange("q (a n) -> q a n", a=PASSES), zv_scales.rearrange("a q n -> q a n"))
+        load_bytes(tab2_s[0 : 4, :], tab2_scales[0, 0 : 4, :])
+        load_bytes(tab2_s[32 : 36, :], tab2_scales[0, 4 : 8, :])
+        load_bytes(tab2_s[64 : 68, :], tab2_scales[0, 8 : 12, :])
+        load_bytes(tab2_s[96 : 100, :], tab2_scales[0, 12 : 16, :])
         load_bytes(tab_w[:], tab_words[0].rearrange("p t i -> p (t i)"))
+        load_bytes(wt_w[:], wt_words[0].rearrange("p n i -> p (n i)"))
         for g in range(1, QUADS):
             load_bytes(weight_s[32 * g : 32 * g + 4, :], weight_s[4 * g : 4 * g + 4, :])
         load_bytes(zt_w[:], zt_words[0])
-        load_wv(0, 0)
         load_bytes(zv_w[:], zv_words.rearrange("a p n -> p a n"))
-        load_wv(0, 1)
+        load_wv(0, 0)
         nc.vector.tensor_copy(picked_s[:], tab_s[:].indirect(list1[:]))
-        load_bytes(picked_s_pass1[0 : P - PASS1_SHIFT, :], picked_s[PASS1_SHIFT:P, :])
+        for g in range(QUADS):
+            load_bytes(planes[32 * g : 32 * g + 4, :, :], picked_s[96 + 8 * g : 104 + 8 * g, :])
+        load_wv(0, 1)
+        load_wv(1, 0)
         with nc.allow_non_contiguous_dma(reason="one bias value to a partition"):
             nc.sync.dma_start(out=bias[:], in_=b.rearrange("(t p) -> p t", p=P))
-        nc.scalar.activation(out=neg_bias[:], in_=bias[:], func=ACT.Copy, scale=-1.0)
-        load_bytes(wt_w[:], wt_words[0].rearrange("p n i -> p (n i)"))
-        load_wv(1, 0)
         load_wv(1, 1)
 
         def gather_tab2_scales(c):
@@ -140,11 +147,18 @@ def tile_list_gmu_relu_none_kernel(
                     parted[c][:].bitcast(U16)[:, :, at : at + entries], tile[:].bitcast(U16).rearrange("p (j a) -> p a j", a=PASSES)
                 )
 
-        def round_wv(h, a):
-            nc.scalar.copy(
-                out=wv_bf[h][:, a].rearrange("p (n m) i -> p n i m", m=4),
-                in_=wv_raw[h][a][:].rearrange("p i (n m) -> p n i m", m=4),
-            )
+        def round_wv(h, a, parts=1):
+            for s in range(parts):
+                cols = slice(s * HALF // parts, (s + 1) * HALF // parts)
+                nc.scalar.activation(
+                    out=wv_bf[h][:, a, cols].rearrange("p (n m) i -> p n i m", m=4),
+                    in_=wv_raw[h][a][:, :, cols].rearrange("p i (n m) -> p n i m", m=4),
+                    func=ACT.Copy, scale=-1.0,
+                )
+
+        def sign_bias():
+            for side, factor in enumerate((1.0, -1.0)):
+                nc.gpsimd.tensor_scalar(out=signed_bias[:, side, :], in0=bias[:], scalar1=factor, scalar2=0.0, op0=ALU.mult, op1=ALU.add)
 
         def quantise_wv(h):
             nc.vector.quantize_mx(
@@ -182,95 +196,181 @@ def tile_list_gmu_relu_none_kernel(
                     start=(a == 0), stop=(a == PASSES - 1),
                 )
 
-        def make_gate(c, t, rest_on_gpsimd):
+        at = {}
+
+        def open_z(c, t):
             cols = slice(t * P, (t + 1) * P)
-            byte_cols = slice(2 * t * P, 2 * (t + 1) * P)
-            z = new_sum("z", c, t)
             nc.tensor.matmul_mx(
-                out=z[:], lhsT=zt_w[:, byte_cols].bitcast(FP4X4), lhsT_scale=zt_s[:, cols],
+                out=new_sum("z", c, t)[:], lhsT=zt_w[:, 2 * t * P : 2 * (t + 1) * P].bitcast(FP4X4), lhsT_scale=zt_s[:, cols],
                 rhs=picked2_w[c][:].bitcast(FP8X4), rhs_scale=picked2_s[c][:], start=True, stop=False,
             )
+
+        def close_z(c, t):
+            cols = slice(t * P, (t + 1) * P)
             for a in range(PASSES):
                 nc.tensor.matmul_mx(
-                    out=z[:], lhsT=zv_w[:, a, byte_cols].bitcast(FP4X4), lhsT_scale=zv_s[a][:, cols],
+                    out=sums["z", c, t][0][:], lhsT=zv_w[:, a, 2 * t * P : 2 * (t + 1) * P].bitcast(FP4X4), lhsT_scale=zv_s[a][:, cols],
                     rhs=parted[c][:, a, :].bitcast(FP4X4), rhs_scale=picked_planes[a][:, chunk_cols(c)],
                     start=False, stop=(a == PASSES - 1),
                 )
+
+        def sum_z(c, t):
+            open_z(c, t)
+            close_z(c, t)
+
+        def make_gate(c, t, last):
             gate[c, t] = work.tile([P, CHUNK], F32, name="gate")
+            nc.scalar.activation(out=gate[c, t][:], in_=sums["z", c, t][0][:], func=ACT.Sigmoid, bias=signed_bias[:, 0, t : t + 1], scale=1.0)
+            if last:
+                release("z", c, t)
+
+        def make_rest(c, t, last):
             rest[c, t] = work.tile([P, CHUNK], F32, name="rest")
-            if not rest_on_gpsimd:
-                nc.scalar.activation(out=rest[c, t][:], in_=z[:], func=ACT.Sigmoid, bias=neg_bias[:, t : t + 1], scale=-1.0)
-            nc.scalar.activation(out=gate[c, t][:], in_=z[:], func=ACT.Sigmoid, bias=bias[:, t : t + 1], scale=1.0)
-            if rest_on_gpsimd:
-                nc.gpsimd.tensor_scalar(out=rest[c, t][:], in0=gate[c, t][:], scalar1=-1.0, scalar2=1.0, op0=ALU.mult, op1=ALU.add)
-            release("z", c, t)
+            nc.scalar.activation(out=rest[c, t][:], in_=sums["z", c, t][0][:], func=ACT.Sigmoid, bias=signed_bias[:, 1, t : t + 1], scale=-1.0)
+            if last:
+                release("z", c, t)
+
+        def rest_from_gate(c, t):
+            rest[c, t] = work.tile([P, CHUNK], F32, name="rest")
+            nc.gpsimd.tensor_scalar(out=rest[c, t][:], in0=gate[c, t][:], scalar1=-1.0, scalar2=1.0, op0=ALU.mult, op1=ALU.add)
 
         def spans(parts):
             return [slice(i * CHUNK // parts, (i + 1) * CHUNK // parts) for i in range(parts)]
 
-        def products(c, t, parts=1):
+        def relu_ht(c, t):
+            at[c, t] = work.tile([P, CHUNK], F32, name="at")
+            nc.scalar.activation(out=at[c, t][:], in_=sums["ht", c, t][0][:], func=ACT.Relu)
+            release("ht", c, t)
+
+        def t_on_gpsimd(c, t):
             from_t[c, t] = work.tile([P, CHUNK], F32, name="from_t")
-            from_v[c, t] = work.tile([P, CHUNK], F32, name="from_v")
+            nc.gpsimd.tensor_tensor(out=from_t[c, t][:], in0=at[c, t][:], in1=rest[c, t][:], op=ALU.mult)
+
+        def t_on_vector(c, t):
+            from_t[c, t] = work.tile([P, CHUNK], F32, name="from_t")
             nc.vector.scalar_tensor_tensor(
                 out=from_t[c, t][:], in0=sums["ht", c, t][0][:], scalar=0.0, in1=rest[c, t][:], op0=ALU.max, op1=ALU.mult
             )
             release("ht", c, t)
+
+        def v_by_gate(c, t):
+            from_v[c, t] = work.tile([P, CHUNK], F32, name="from_v")
+            nc.vector.scalar_tensor_tensor(
+                out=from_v[c, t][:], in0=sums["hv", c, t][0][:], scalar=0.0, in1=gate[c, t][:], op0=ALU.min, op1=ALU.mult
+            )
+            release("hv", c, t)
+
+        def join_on_gpsimd(c, t):
+            result = work.tile([P, CHUNK], F32, name="result")
+            nc.gpsimd.tensor_tensor(out=result[:], in0=from_t[c, t][:], in1=from_v[c, t][:], op=ALU.subtract)
+            nc.sync.dma_start(out=out[t * P : (t + 1) * P, chunk_cols(c)], in_=result[:])
+
+        def v_by_rest(c, t, parts=1):
+            from_v[c, t] = work.tile([P, CHUNK], F32, name="from_v")
             for s in spans(parts):
                 nc.vector.scalar_tensor_tensor(
-                    out=from_v[c, t][:, s], in0=sums["hv", c, t][0][:, s], scalar=0.0, in1=gate[c, t][:, s], op0=ALU.max, op1=ALU.mult
+                    out=from_v[c, t][:, s], in0=rest[c, t][:, s], scalar=1.0, in1=sums["hv", c, t][0][:, s], op0=ALU.subtract, op1=ALU.mult
                 )
             release("hv", c, t)
 
-        def add_and_store(c, t, engine, parts=1):
+        def join_on_vector(c, t, parts=1):
             result = work.tile([P, CHUNK], F32, name="result")
             for s in spans(parts):
-                engine.tensor_tensor(out=result[:, s], in0=from_v[c, t][:, s], in1=from_t[c, t][:, s], op=ALU.add)
+                nc.vector.scalar_tensor_tensor(
+                    out=result[:, s], in0=from_v[c, t][:, s], scalar=0.0, in1=from_t[c, t][:, s], op0=ALU.max, op1=ALU.add
+                )
                 nc.sync.dma_start(out=out[t * P : (t + 1) * P, chunk_cols(c)][:, s], in_=result[:, s])
 
-        def finish(c, t):
-            products(c, t)
-            add_and_store(c, t, nc.gpsimd)
+        def v_by_difference(c, t):
+            from_v[c, t] = work.tile([P, CHUNK], F32, name="from_v")
+            nc.vector.scalar_tensor_tensor(
+                out=from_v[c, t][:], in0=sums["hv", c, t][0][:], scalar=0.0, in1=at[c, t][:], op0=ALU.min, op1=ALU.add
+            )
+            release("hv", c, t)
+
+        def gate_difference(c, t):
+            gated = work.tile([P, CHUNK], F32, name="gated")
+            nc.gpsimd.tensor_tensor(out=gated[:], in0=from_v[c, t][:], in1=gate[c, t][:], op=ALU.mult)
+            from_t[c, t], from_v[c, t] = at[c, t], gated
 
         gather_tab2_words(0)
         gather_tab2_scales(0)
-        gather_tab2_scales(1)
         gather_tab_words(0)
         part_passes(0)
-        round_wv(0, 0)
-        gather_tab_words(1)
+        sum_ht(0, 0)
+        relu_ht(0, 0)
+        sum_ht(0, 1)
+        open_z(0, 1)
+        open_z(0, 2)
+        open_z(0, 3)
+        open_z(0, 0)
+        sum_ht(0, 2)
+        sum_ht(0, 3)
+        close_z(0, 1)
+        close_z(0, 2)
+        close_z(0, 3)
+        close_z(0, 0)
+        gather_tab2_scales(1)
         gather_tab2_words(1)
-        part_passes(1)
-        round_wv(0, 1)
+        gather_tab_words(1)
+        round_wv(0, 0)
+        round_wv(0, 1, parts=2)
+        sign_bias()
         quantise_wv(0)
-
-        for t in range(N_TILES):
-            make_gate(0, t, rest_on_gpsimd=True)
-        for t in range(N_TILES):
-            sum_ht(0, t)
-        for t in (0, 1):
-            sum_hv(0, t)
-            finish(0, t)
+        part_passes(1)
+        make_gate(0, 1, True)
+        rest_from_gate(0, 1)
+        make_gate(0, 2, True)
+        rest_from_gate(0, 2)
+        make_gate(0, 0, True)
+        make_rest(0, 3, False)
+        sum_hv(0, 0)
+        sum_hv(0, 1)
+        v_by_difference(0, 0)
+        t_on_vector(0, 1)
+        gate_difference(0, 0)
+        join_on_gpsimd(0, 0)
+        v_by_gate(0, 1)
+        join_on_gpsimd(0, 1)
+        t_on_vector(0, 2)
+        t_on_vector(0, 3)
         round_wv(1, 0)
+        sum_z(1, 0)
+        make_rest(1, 0, False)
+        make_gate(1, 0, True)
         round_wv(1, 1)
-        make_gate(1, 0, False)
         sum_ht(1, 0)
         sum_hv(1, 0)
-        finish(1, 0)
+        t_on_vector(1, 0)
+        v_by_gate(1, 0)
+        join_on_gpsimd(1, 0)
         quantise_wv(1)
-        make_gate(1, 1, False)
-        for t in (2, 3):
-            sum_hv(0, t)
-            finish(0, t)
-        make_gate(1, 2, False)
+        sum_z(1, 1)
+        make_rest(1, 1, False)
+        make_gate(1, 1, True)
+        make_gate(0, 3, True)
         sum_ht(1, 1)
         sum_hv(1, 1)
-        finish(1, 1)
-        make_gate(1, 3, False)
+        t_on_vector(1, 1)
+        v_by_gate(1, 1)
+        join_on_gpsimd(1, 1)
+        sum_hv(0, 2)
+        v_by_gate(0, 2)
+        join_on_gpsimd(0, 2)
+        sum_hv(0, 3)
+        v_by_gate(0, 3)
+        join_on_gpsimd(0, 3)
+        sum_z(1, 2)
+        make_rest(1, 2, True)
+        sum_z(1, 3)
+        make_rest(1, 3, True)
         sum_ht(1, 2)
         sum_hv(1, 2)
-        products(1, 2)
+        t_on_vector(1, 2)
+        v_by_rest(1, 2)
         sum_ht(1, 3)
         sum_hv(1, 3)
-        products(1, 3, parts=2)
-        add_and_store(1, 2, nc.vector)
-        add_and_store(1, 3, nc.vector, parts=2)
+        t_on_vector(1, 3)
+        v_by_rest(1, 3, parts=2)
+        join_on_vector(1, 2)
+        join_on_vector(1, 3, parts=2)

@@ -76,7 +76,7 @@ def tile_list_gmu_relu_none_kernel(
         picked2_w = [kept("picked2_w0", [P, CHUNK], U32), placed("picked2_w1", [P, CHUNK], U32, word_bytes + CHUNK)]
         bf_at = 3 * word_bytes
         wv_bf = [placed("wv_bf0", [P, PASSES, HALF, 4], BF16, bf_at), kept("wv_bf1", [P, PASSES, HALF, 4], BF16)]
-        parted = [kept("parted0", [P, PASSES, 2 * CHUNK], U8), placed("parted1", [P, PASSES, 2 * CHUNK], U8, bf_at + word_bytes // 2)]
+        parted = [kept("parted0", [P, PASSES, 2 * CHUNK], U8), kept("parted1", [P, PASSES, 2 * CHUNK], U8)]
 
         raw_at = 6 * word_bytes
         wv_raw = [[kept("wv_raw00", [P, 4, HALF], F32), placed("wv_raw01", [P, 4, HALF], F32, raw_at)],
@@ -157,8 +157,8 @@ def tile_list_gmu_relu_none_kernel(
                 )
 
         def sign_bias():
-            for side, factor in enumerate((1.0, -1.0)):
-                nc.gpsimd.tensor_scalar(out=signed_bias[:, side, :], in0=bias[:], scalar1=factor, scalar2=0.0, op0=ALU.mult, op1=ALU.add)
+            for side, factor in ((1, -1.0), (0, 1.0)):
+                nc.scalar.activation(out=signed_bias[:, side, :], in_=bias[:], func=ACT.Copy, scale=factor)
 
         def quantise_wv(h):
             nc.vector.quantize_mx(
@@ -298,78 +298,78 @@ def tile_list_gmu_relu_none_kernel(
         gather_tab_words(0)
         part_passes(0)
         sum_ht(0, 0)
-        relu_ht(0, 0)
         sum_ht(0, 1)
+        open_z(0, 0)
         open_z(0, 1)
         open_z(0, 2)
         open_z(0, 3)
-        open_z(0, 0)
         sum_ht(0, 2)
-        sum_ht(0, 3)
+        close_z(0, 0)
         close_z(0, 1)
         close_z(0, 2)
         close_z(0, 3)
-        close_z(0, 0)
         gather_tab2_scales(1)
         gather_tab2_words(1)
         gather_tab_words(1)
+        part_passes(1)
         round_wv(0, 0)
         round_wv(0, 1, parts=2)
         sign_bias()
         quantise_wv(0)
-        part_passes(1)
-        make_gate(0, 1, True)
-        rest_from_gate(0, 1)
+        make_rest(0, 0, False)
         make_gate(0, 2, True)
         rest_from_gate(0, 2)
         make_gate(0, 0, True)
-        make_rest(0, 3, False)
+        make_gate(0, 1, True)
+        rest_from_gate(0, 1)
+        sum_z(1, 0)
         sum_hv(0, 0)
         sum_hv(0, 1)
-        v_by_difference(0, 0)
-        t_on_vector(0, 1)
-        gate_difference(0, 0)
-        join_on_gpsimd(0, 0)
-        v_by_gate(0, 1)
-        join_on_gpsimd(0, 1)
+        t_on_vector(0, 0)
         t_on_vector(0, 2)
-        t_on_vector(0, 3)
-        round_wv(1, 0)
-        sum_z(1, 0)
-        make_rest(1, 0, False)
-        make_gate(1, 0, True)
-        round_wv(1, 1)
         sum_ht(1, 0)
         sum_hv(1, 0)
+        v_by_gate(0, 0)
+        join_on_gpsimd(0, 0)
+        sum_z(1, 1)
+        make_rest(1, 0, False)
+        make_gate(1, 0, True)
+        v_by_gate(0, 1)
+        t_on_vector(0, 1)
+        join_on_gpsimd(0, 1)
+        sum_ht(1, 1)
+        sum_hv(1, 1)
+        sum_ht(0, 3)
+        round_wv(1, 0)
+        round_wv(1, 1)
         t_on_vector(1, 0)
         v_by_gate(1, 0)
         join_on_gpsimd(1, 0)
         quantise_wv(1)
-        sum_z(1, 1)
+        sum_z(1, 2)
+        sum_hv(0, 2)
         make_rest(1, 1, False)
         make_gate(1, 1, True)
-        make_gate(0, 3, True)
-        sum_ht(1, 1)
-        sum_hv(1, 1)
         t_on_vector(1, 1)
         v_by_gate(1, 1)
         join_on_gpsimd(1, 1)
-        sum_hv(0, 2)
+        sum_hv(0, 3)
+        sum_z(1, 3)
+        sum_ht(1, 2)
+        make_rest(0, 3, False)
+        make_gate(0, 3, True)
         v_by_gate(0, 2)
         join_on_gpsimd(0, 2)
-        sum_hv(0, 3)
+        sum_hv(1, 2)
+        t_on_vector(0, 3)
         v_by_gate(0, 3)
         join_on_gpsimd(0, 3)
-        sum_z(1, 2)
-        make_rest(1, 2, True)
-        sum_z(1, 3)
-        make_rest(1, 3, True)
-        sum_ht(1, 2)
-        sum_hv(1, 2)
-        t_on_vector(1, 2)
-        v_by_rest(1, 2)
         sum_ht(1, 3)
         sum_hv(1, 3)
+        make_rest(1, 2, True)
+        make_rest(1, 3, True)
+        t_on_vector(1, 2)
+        v_by_rest(1, 2)
         t_on_vector(1, 3)
         v_by_rest(1, 3, parts=2)
         join_on_vector(1, 2)

@@ -83,6 +83,7 @@ def tile_list_gmu_relu_none_kernel(
                   [kept("wv_raw1%d" % a, [P, 4, HALF], F32) for a in range(PASSES)]]
         signed_bias = placed("signed_bias", [P, 2, N_TILES], F32, raw_at)
 
+        neg_bias = kept("neg_bias", [P, N_TILES], F32)
         nc.vector.memset(weight_s[:].bitcast(I32), 0)
         nc.vector.memset(tab2_s[:].bitcast(I32), 0)
         nc.vector.memset(tab_s[0:96, :].bitcast(I32), 0)
@@ -106,28 +107,28 @@ def tile_list_gmu_relu_none_kernel(
         nc.sync.dma_start(list1[:], offs)
         load_bytes(tab_s[96:128, :], tab_scales.rearrange("a q t -> q a t"))
         nc.sync.dma_start(list2[:], offs2)
-        load_bytes(wt_s[0:16, :], wt_scales[0])
-        load_bytes(tab2_w[:], tab2_words[0].rearrange("p t i -> p (t i)"))
         load_bytes(zt_s[0:16, :], zt_scales[0])
+        load_bytes(tab2_w[:], tab2_words[0].rearrange("p t i -> p (t i)"))
+        load_bytes(wt_s[0:16, :], wt_scales[0])
         load_bytes(weight_s[0:16, 0 : 2 * N].rearrange("q (a n) -> q a n", a=PASSES), zv_scales.rearrange("a q n -> q a n"))
         load_bytes(tab2_s[0 : 4, :], tab2_scales[0, 0 : 4, :])
         load_bytes(tab2_s[32 : 36, :], tab2_scales[0, 4 : 8, :])
         load_bytes(tab2_s[64 : 68, :], tab2_scales[0, 8 : 12, :])
         load_bytes(tab2_s[96 : 100, :], tab2_scales[0, 12 : 16, :])
         load_bytes(tab_w[:], tab_words[0].rearrange("p t i -> p (t i)"))
-        load_bytes(wt_w[:], wt_words[0].rearrange("p n i -> p (n i)"))
+        load_bytes(zt_w[:], zt_words[0])
         for g in range(1, QUADS):
             load_bytes(weight_s[32 * g : 32 * g + 4, :], weight_s[4 * g : 4 * g + 4, :])
-        load_bytes(zt_w[:], zt_words[0])
         load_bytes(zv_w[:], zv_words.rearrange("a p n -> p a n"))
+        with nc.allow_non_contiguous_dma(reason="one bias value to a partition"):
+            nc.sync.dma_start(out=bias[:], in_=b.rearrange("(t p) -> p t", p=P))
         load_wv(0, 0)
         nc.vector.tensor_copy(picked_s[:], tab_s[:].indirect(list1[:]))
         for g in range(QUADS):
             load_bytes(planes[32 * g : 32 * g + 4, :, :], picked_s[96 + 8 * g : 104 + 8 * g, :])
         load_wv(0, 1)
+        load_bytes(wt_w[:], wt_words[0].rearrange("p n i -> p (n i)"))
         load_wv(1, 0)
-        with nc.allow_non_contiguous_dma(reason="one bias value to a partition"):
-            nc.sync.dma_start(out=bias[:], in_=b.rearrange("(t p) -> p t", p=P))
         load_wv(1, 1)
 
         def gather_tab2_scales(c):
@@ -156,8 +157,11 @@ def tile_list_gmu_relu_none_kernel(
                     func=ACT.Copy, scale=-1.0,
                 )
 
+        def negate_bias():
+            nc.scalar.activation(out=neg_bias[:], in_=bias[:], func=ACT.Copy, scale=-1.0)
+
         def sign_bias():
-            for side, factor in ((1, -1.0), (0, 1.0)):
+            for side, factor in ((0, 1.0), (1, -1.0)):
                 nc.scalar.activation(out=signed_bias[:, side, :], in_=bias[:], func=ACT.Copy, scale=factor)
 
         def quantise_wv(h):
@@ -224,9 +228,10 @@ def tile_list_gmu_relu_none_kernel(
             if last:
                 release("z", c, t)
 
-        def make_rest(c, t, last):
+        def make_rest(c, t, last, early=False):
+            minus_b = neg_bias[:, t : t + 1] if early else signed_bias[:, 1, t : t + 1]
             rest[c, t] = work.tile([P, CHUNK], F32, name="rest")
-            nc.scalar.activation(out=rest[c, t][:], in_=sums["z", c, t][0][:], func=ACT.Sigmoid, bias=signed_bias[:, 1, t : t + 1], scale=-1.0)
+            nc.scalar.activation(out=rest[c, t][:], in_=sums["z", c, t][0][:], func=ACT.Sigmoid, bias=minus_b, scale=-1.0)
             if last:
                 release("z", c, t)
 
@@ -293,21 +298,22 @@ def tile_list_gmu_relu_none_kernel(
             nc.gpsimd.tensor_tensor(out=gated[:], in0=from_v[c, t][:], in1=gate[c, t][:], op=ALU.mult)
             from_t[c, t], from_v[c, t] = at[c, t], gated
 
+        negate_bias()
         gather_tab2_words(0)
         gather_tab2_scales(0)
         gather_tab_words(0)
         part_passes(0)
-        sum_ht(0, 0)
-        sum_ht(0, 1)
         open_z(0, 0)
-        open_z(0, 1)
         open_z(0, 2)
+        open_z(0, 1)
         open_z(0, 3)
-        sum_ht(0, 2)
         close_z(0, 0)
-        close_z(0, 1)
         close_z(0, 2)
+        close_z(0, 1)
         close_z(0, 3)
+        sum_ht(0, 0)
+        sum_ht(0, 2)
+        sum_ht(0, 1)
         gather_tab2_scales(1)
         gather_tab2_words(1)
         gather_tab_words(1)
@@ -316,14 +322,14 @@ def tile_list_gmu_relu_none_kernel(
         round_wv(0, 1, parts=2)
         sign_bias()
         quantise_wv(0)
-        make_rest(0, 0, False)
+        make_rest(0, 0, False, early=True)
         make_gate(0, 2, True)
         rest_from_gate(0, 2)
         make_gate(0, 0, True)
         make_gate(0, 1, True)
         rest_from_gate(0, 1)
-        sum_z(1, 0)
         sum_hv(0, 0)
+        sum_z(1, 0)
         sum_hv(0, 1)
         t_on_vector(0, 0)
         t_on_vector(0, 2)

@@ -41,57 +41,55 @@ def tile_list_gmu_relu_none_kernel(
         def kept(name, shape, dtype):
             return keep.tile(shape, dtype, name=name, align_bytes=64)
 
+        def placed(name, shape, dtype, offset):
+            return lapped.tile(shape, dtype, name=name, align_bytes=64, offset=offset)
+
         list1 = kept("list1", [P, J // 16], U16)
         list2 = kept("list2", [P, J // 16], U16)
         tab_w = kept("tab_w", [P, T], I32)
-        tab2_w = kept("tab2_w", [P, T], I32)
+        tab2_w = placed("tab2_w", [P, T], I32, 8 * 4 * CHUNK)
         tab_s = kept("tab_s", [P, T], U8)
         tab2_s = kept("tab2_s", [P, T], U8)
         zv_w = kept("zv_w", [P, PASSES, 2 * N], U8)
         zt_w = kept("zt_w", [P, 2 * N], U8)
         wt_w = kept("wt_w", [P, N], I32)
-        weight_s = kept("weight_s", [P, 4 * N], U8)
-        zv_s = [weight_s[:, 0:N], weight_s[:, N : 2 * N]]
-        zt_s = weight_s[:, 2 * N : 3 * N]
-        wt_s = weight_s[:, 3 * N : 4 * N]
-        bias = kept("bias", [P, N_TILES], F32)
+        zv_s = kept("zv_s", [P, PASSES, N], U8)
+        weight_s = kept("weight_s", [P, 2 * N], U8)
+        zt_s = weight_s[:, 0:N]
+        wt_s = weight_s[:, N : 2 * N]
+        early_bias = kept("early_bias", [P, 2, N_TILES], F32)
         warm_in = kept("warm_in", [P, 8], F32)
         warm_out = kept("warm_out", [P, 8], F32)
-        wv_w = [kept("wv_w%d" % h, [P, PASSES, HALF], U32) for h in range(2)]
+        wv_w = [placed("wv_w0", [P, PASSES, HALF], U32, 8 * 4 * CHUNK), kept("wv_w1", [P, PASSES, HALF], U32)]
         wv_s = [kept("wv_s%d" % h, [P, PASSES, HALF], U8) for h in range(2)]
+        wv_bf = [kept("wv_bf%d" % h, [P, PASSES, HALF, 4], BF16) for h in range(2)]
         picked_s = kept("picked_s", [P, J], U8)
         planes = kept("planes", [P, PASSES, J], U8)
-        picked_planes = [planes[:, a, :] for a in range(PASSES)]
+        picked2_s = kept("picked2_s", [P, J], U8)
+        parted = [kept("parted%d" % c, [P, PASSES, 2 * CHUNK], U8) for c in range(2)]
         word_bytes = 4 * CHUNK
-
-        def placed(name, shape, dtype, offset):
-            return lapped.tile(shape, dtype, name=name, align_bytes=64, offset=offset)
 
         picked_w = [
             [(0, CHUNK // 2, placed("picked_w0a", [P, CHUNK // 2], U32, word_bytes - 256)),
              (CHUNK // 2, CHUNK // 2, kept("picked_w0b", [P, CHUNK // 2], U32))],
-            [(CHUNK, CHUNK, placed("picked_w1", [P, CHUNK], U32, 0))],
+            [(CHUNK, CHUNK, placed("picked_w1", [P, CHUNK], U32, word_bytes))],
         ]
-        picked2_s = [kept("picked2_s0", [P, CHUNK], U8), placed("picked2_s1", [P, CHUNK], U8, word_bytes)]
-        picked2_w = [kept("picked2_w0", [P, CHUNK], U32), placed("picked2_w1", [P, CHUNK], U32, word_bytes + CHUNK)]
-        bf_at = 3 * word_bytes
-        wv_bf = [placed("wv_bf0", [P, PASSES, HALF, 4], BF16, bf_at), kept("wv_bf1", [P, PASSES, HALF, 4], BF16)]
-        parted = [kept("parted0", [P, PASSES, 2 * CHUNK], U8), kept("parted1", [P, PASSES, 2 * CHUNK], U8)]
+        picked2_w = [kept("picked2_w%d" % c, [P, CHUNK], U32) for c in range(2)]
 
-        raw_at = 6 * word_bytes
-        wv_raw = [[kept("wv_raw00", [P, 4, HALF], F32), placed("wv_raw01", [P, 4, HALF], F32, raw_at)],
-                  [kept("wv_raw1%d" % a, [P, 4, HALF], F32) for a in range(PASSES)]]
-        signed_bias = placed("signed_bias", [P, 2, N_TILES], F32, raw_at)
+        raw_at = 2 * word_bytes
+        wv_raw = [[kept("wv_raw%d0" % h, [P, 4, HALF], F32), placed("wv_raw%d1" % h, [P, 4, HALF], F32, raw_at * (h + 1))]
+                  for h in range(2)]
+        late_bias = placed("late_bias", [P, 2, N_TILES], F32, 2 * raw_at)
+        held_rest = placed("held_rest", [P, CHUNK], F32, raw_at)
 
-        neg_bias = kept("neg_bias", [P, N_TILES], F32)
-        nc.vector.memset(weight_s[:].bitcast(I32), 0)
-        nc.vector.memset(tab2_s[:].bitcast(I32), 0)
+        nc.gpsimd.memset(weight_s[:].bitcast(I32), 0)
+        nc.vector.memset(zv_s[:].rearrange("p a n -> p (a n)").bitcast(I32), 0)
         nc.vector.memset(tab_s[0:96, :].bitcast(I32), 0)
-        nc.vector.memset(planes[:].rearrange("p a j -> p (a j)").bitcast(I32), 0)
+        nc.vector.memset(tab2_s[:].bitcast(I32), 0)
         nc.vector.memset(warm_in[:], 0.0)
         nc.scalar.activation(out=warm_out[:], in_=warm_in[:], func=ACT.Sigmoid)
 
-        def load_bytes(dst, src, queue=nc.sync):
+        def load_bytes(dst, src, queue):
             queue.dma_start(out=dst.bitcast(I32), in_=src.bitcast(I32))
 
         def load_wv(h, a):
@@ -104,35 +102,35 @@ def tile_list_gmu_relu_none_kernel(
         def chunk_cols(c):
             return slice(c * CHUNK, (c + 1) * CHUNK)
 
-        nc.sync.dma_start(list1[:], offs)
-        load_bytes(tab_s[96:128, :], tab_scales.rearrange("a q t -> q a t"))
-        nc.sync.dma_start(list2[:], offs2)
-        load_bytes(zt_s[0:16, :], zt_scales[0])
-        load_bytes(tab2_w[:], tab2_words[0].rearrange("p t i -> p (t i)"))
-        load_bytes(wt_s[0:16, :], wt_scales[0])
-        load_bytes(weight_s[0:16, 0 : 2 * N].rearrange("q (a n) -> q a n", a=PASSES), zv_scales.rearrange("a q n -> q a n"))
-        load_bytes(tab2_s[0 : 4, :], tab2_scales[0, 0 : 4, :])
-        load_bytes(tab2_s[32 : 36, :], tab2_scales[0, 4 : 8, :])
-        load_bytes(tab2_s[64 : 68, :], tab2_scales[0, 8 : 12, :])
-        load_bytes(tab2_s[96 : 100, :], tab2_scales[0, 12 : 16, :])
-        load_bytes(tab_w[:], tab_words[0].rearrange("p t i -> p (t i)"))
-        load_bytes(zt_w[:], zt_words[0])
-        for g in range(1, QUADS):
-            load_bytes(weight_s[32 * g : 32 * g + 4, :], weight_s[4 * g : 4 * g + 4, :])
-        load_bytes(zv_w[:], zv_words.rearrange("a p n -> p a n"))
+        load_bytes(zt_s[0:16, :], zt_scales[0], nc.gpsimd)
+        load_bytes(wt_s[0:16, :], wt_scales[0], nc.gpsimd)
+        nc.gpsimd.memset(planes[:].rearrange("p a j -> p (a j)").bitcast(I32), 0)
         with nc.allow_non_contiguous_dma(reason="one bias value to a partition"):
-            nc.sync.dma_start(out=bias[:], in_=b.rearrange("(t p) -> p t", p=P))
+            nc.gpsimd.dma_start(out=early_bias[:, 0, :], in_=b.rearrange("(t p) -> p t", p=P))
+        nc.sync.dma_start(list1[:], offs)
+        load_bytes(tab_s[96:128, :], tab_scales.rearrange("a q t -> q a t"), nc.sync)
+        load_bytes(tab_w[:], tab_words[0].rearrange("p t i -> p (t i)"), nc.sync)
+        for g in range(QUADS):
+            load_bytes(zv_s[32 * g : 32 * g + 4, :, :], zv_scales[:, 4 * g : 4 * g + 4, :].rearrange("a q n -> q a n"), nc.sync)
+        load_bytes(zv_w[:], zv_words.rearrange("a p n -> p a n"), nc.sync)
+        nc.sync.dma_start(list2[:], offs2)
         load_wv(0, 0)
         nc.vector.tensor_copy(picked_s[:], tab_s[:].indirect(list1[:]))
         for g in range(QUADS):
-            load_bytes(planes[32 * g : 32 * g + 4, :, :], picked_s[96 + 8 * g : 104 + 8 * g, :])
+            load_bytes(planes[32 * g : 32 * g + 4, :, :], picked_s[96 + 8 * g : 104 + 8 * g, :], nc.sync)
         load_wv(0, 1)
-        load_bytes(wt_w[:], wt_words[0].rearrange("p n i -> p (n i)"))
+        for g in range(QUADS):
+            load_bytes(tab2_s[32 * g : 32 * g + 4, :], tab2_scales[0, 4 * g : 4 * g + 4, :], nc.sync)
+        load_bytes(tab2_w[:], tab2_words[0].rearrange("p t i -> p (t i)"), nc.sync)
+        for g in range(1, QUADS):
+            load_bytes(weight_s[32 * g : 32 * g + 4, :], weight_s[4 * g : 4 * g + 4, :], nc.sync)
+        load_bytes(zt_w[:], zt_words[0], nc.sync)
+        load_bytes(wt_w[:], wt_words[0].rearrange("p n i -> p (n i)"), nc.sync)
         load_wv(1, 0)
         load_wv(1, 1)
 
-        def gather_tab2_scales(c):
-            nc.vector.tensor_copy(picked2_s[c][:], tab2_s[:].indirect(list2[:, list_cols(c)]))
+        def gather_tab2_scales():
+            nc.vector.tensor_copy(picked2_s[:], tab2_s[:].indirect(list2[:]))
 
         def gather_tab2_words(c):
             nc.vector.tensor_copy(picked2_w[c][:], tab2_w[:].bitcast(U32).indirect(list2[:, list_cols(c)]))
@@ -148,21 +146,18 @@ def tile_list_gmu_relu_none_kernel(
                     parted[c][:].bitcast(U16)[:, :, at : at + entries], tile[:].bitcast(U16).rearrange("p (j a) -> p a j", a=PASSES)
                 )
 
-        def round_wv(h, a, parts=1):
-            for s in range(parts):
-                cols = slice(s * HALF // parts, (s + 1) * HALF // parts)
-                nc.scalar.activation(
-                    out=wv_bf[h][:, a, cols].rearrange("p (n m) i -> p n i m", m=4),
-                    in_=wv_raw[h][a][:, :, cols].rearrange("p i (n m) -> p n i m", m=4),
-                    func=ACT.Copy, scale=-1.0,
-                )
+        def round_wv(h, a):
+            nc.scalar.activation(
+                out=wv_bf[h][:, a].rearrange("p (n m) i -> p n i m", m=4),
+                in_=wv_raw[h][a][:].rearrange("p i (n m) -> p n i m", m=4),
+                func=ACT.Copy, scale=-1.0,
+            )
 
         def negate_bias():
-            nc.scalar.activation(out=neg_bias[:], in_=bias[:], func=ACT.Copy, scale=-1.0)
+            nc.scalar.activation(out=early_bias[:, 1, :], in_=early_bias[:, 0, :], func=ACT.Copy, scale=-1.0)
 
-        def sign_bias():
-            for side, factor in ((0, 1.0), (1, -1.0)):
-                nc.scalar.activation(out=signed_bias[:, side, :], in_=bias[:], func=ACT.Copy, scale=factor)
+        def carry_bias():
+            nc.scalar.activation(out=late_bias[:], in_=early_bias[:], func=ACT.Copy)
 
         def quantise_wv(h):
             nc.vector.quantize_mx(
@@ -187,7 +182,7 @@ def tile_list_gmu_relu_none_kernel(
             cols = slice(t * P, (t + 1) * P)
             nc.tensor.matmul_mx(
                 out=new_sum("ht", c, t)[:], lhsT=wt_w[:, cols].bitcast(FP8X4), lhsT_scale=wt_s[:, cols],
-                rhs=picked2_w[c][:].bitcast(FP8X4), rhs_scale=picked2_s[c][:], start=True, stop=True,
+                rhs=picked2_w[c][:].bitcast(FP8X4), rhs_scale=picked2_s[:, chunk_cols(c)], start=True, stop=True,
             )
 
         def sum_hv(c, t):
@@ -196,62 +191,50 @@ def tile_list_gmu_relu_none_kernel(
             for a in range(PASSES):
                 nc.tensor.matmul_mx(
                     out=acc[:], lhsT=wv_w[h][:, a, cols].bitcast(FP8X4), lhsT_scale=wv_s[h][:, a, cols],
-                    rhs=parted[c][:, a, :].bitcast(FP4X4), rhs_scale=picked_planes[a][:, chunk_cols(c)],
+                    rhs=parted[c][:, a, :].bitcast(FP4X4), rhs_scale=planes[:, a, chunk_cols(c)],
                     start=(a == 0), stop=(a == PASSES - 1),
                 )
 
-        at = {}
-
         def open_z(c, t):
             cols = slice(t * P, (t + 1) * P)
-            nc.tensor.matmul_mx(
-                out=new_sum("z", c, t)[:], lhsT=zt_w[:, 2 * t * P : 2 * (t + 1) * P].bitcast(FP4X4), lhsT_scale=zt_s[:, cols],
-                rhs=picked2_w[c][:].bitcast(FP8X4), rhs_scale=picked2_s[c][:], start=True, stop=False,
-            )
+            acc = new_sum("z", c, t)
+            for a in range(PASSES):
+                nc.tensor.matmul_mx(
+                    out=acc[:], lhsT=zv_w[:, a, 2 * t * P : 2 * (t + 1) * P].bitcast(FP4X4), lhsT_scale=zv_s[:, a, cols],
+                    rhs=parted[c][:, a, :].bitcast(FP4X4), rhs_scale=planes[:, a, chunk_cols(c)],
+                    start=(a == 0), stop=False,
+                )
 
         def close_z(c, t):
             cols = slice(t * P, (t + 1) * P)
-            for a in range(PASSES):
-                nc.tensor.matmul_mx(
-                    out=sums["z", c, t][0][:], lhsT=zv_w[:, a, 2 * t * P : 2 * (t + 1) * P].bitcast(FP4X4), lhsT_scale=zv_s[a][:, cols],
-                    rhs=parted[c][:, a, :].bitcast(FP4X4), rhs_scale=picked_planes[a][:, chunk_cols(c)],
-                    start=False, stop=(a == PASSES - 1),
-                )
+            nc.tensor.matmul_mx(
+                out=sums["z", c, t][0][:], lhsT=zt_w[:, 2 * t * P : 2 * (t + 1) * P].bitcast(FP4X4), lhsT_scale=zt_s[:, cols],
+                rhs=picked2_w[c][:].bitcast(FP8X4), rhs_scale=picked2_s[:, chunk_cols(c)], start=False, stop=True,
+            )
 
         def sum_z(c, t):
             open_z(c, t)
             close_z(c, t)
 
-        def make_gate(c, t, last):
+        def make_gate(c, t):
             gate[c, t] = work.tile([P, CHUNK], F32, name="gate")
-            nc.scalar.activation(out=gate[c, t][:], in_=sums["z", c, t][0][:], func=ACT.Sigmoid, bias=signed_bias[:, 0, t : t + 1], scale=1.0)
+            nc.scalar.activation(out=gate[c, t][:], in_=sums["z", c, t][0][:], func=ACT.Sigmoid, bias=early_bias[:, 0, t : t + 1], scale=1.0)
+            release("z", c, t)
+
+        def make_rest(c, t, last, biases=late_bias, into=None):
+            rest[c, t] = work.tile([P, CHUNK], F32, name="rest") if into is None else into
+            nc.scalar.activation(out=rest[c, t][:], in_=sums["z", c, t][0][:], func=ACT.Sigmoid, bias=biases[:, 1, t : t + 1], scale=-1.0)
             if last:
                 release("z", c, t)
 
-        def make_rest(c, t, last, early=False):
-            minus_b = neg_bias[:, t : t + 1] if early else signed_bias[:, 1, t : t + 1]
-            rest[c, t] = work.tile([P, CHUNK], F32, name="rest")
-            nc.scalar.activation(out=rest[c, t][:], in_=sums["z", c, t][0][:], func=ACT.Sigmoid, bias=minus_b, scale=-1.0)
-            if last:
-                release("z", c, t)
-
-        def rest_from_gate(c, t):
-            rest[c, t] = work.tile([P, CHUNK], F32, name="rest")
-            nc.gpsimd.tensor_scalar(out=rest[c, t][:], in0=gate[c, t][:], scalar1=-1.0, scalar2=1.0, op0=ALU.mult, op1=ALU.add)
+        def gate_from_rest(c, t):
+            gate[c, t] = work.tile([P, CHUNK], F32, name="gate")
+            nc.gpsimd.tensor_scalar(out=gate[c, t][:], in0=rest[c, t][:], scalar1=-1.0, scalar2=1.0, op0=ALU.mult, op1=ALU.add)
 
         def spans(parts):
             return [slice(i * CHUNK // parts, (i + 1) * CHUNK // parts) for i in range(parts)]
 
-        def relu_ht(c, t):
-            at[c, t] = work.tile([P, CHUNK], F32, name="at")
-            nc.scalar.activation(out=at[c, t][:], in_=sums["ht", c, t][0][:], func=ACT.Relu)
-            release("ht", c, t)
-
-        def t_on_gpsimd(c, t):
-            from_t[c, t] = work.tile([P, CHUNK], F32, name="from_t")
-            nc.gpsimd.tensor_tensor(out=from_t[c, t][:], in0=at[c, t][:], in1=rest[c, t][:], op=ALU.mult)
-
-        def t_on_vector(c, t):
+        def t_by_rest(c, t):
             from_t[c, t] = work.tile([P, CHUNK], F32, name="from_t")
             nc.vector.scalar_tensor_tensor(
                 out=from_t[c, t][:], in0=sums["ht", c, t][0][:], scalar=0.0, in1=rest[c, t][:], op0=ALU.max, op1=ALU.mult
@@ -286,97 +269,86 @@ def tile_list_gmu_relu_none_kernel(
                 )
                 nc.sync.dma_start(out=out[t * P : (t + 1) * P, chunk_cols(c)][:, s], in_=result[:, s])
 
-        def v_by_difference(c, t):
-            from_v[c, t] = work.tile([P, CHUNK], F32, name="from_v")
-            nc.vector.scalar_tensor_tensor(
-                out=from_v[c, t][:], in0=sums["hv", c, t][0][:], scalar=0.0, in1=at[c, t][:], op0=ALU.min, op1=ALU.add
-            )
-            release("hv", c, t)
-
-        def gate_difference(c, t):
-            gated = work.tile([P, CHUNK], F32, name="gated")
-            nc.gpsimd.tensor_tensor(out=gated[:], in0=from_v[c, t][:], in1=gate[c, t][:], op=ALU.mult)
-            from_t[c, t], from_v[c, t] = at[c, t], gated
-
-        negate_bias()
-        gather_tab2_words(0)
-        gather_tab2_scales(0)
         gather_tab_words(0)
         part_passes(0)
-        open_z(0, 0)
-        open_z(0, 2)
-        open_z(0, 1)
-        open_z(0, 3)
-        close_z(0, 0)
-        close_z(0, 2)
-        close_z(0, 1)
-        close_z(0, 3)
-        sum_ht(0, 0)
-        sum_ht(0, 2)
-        sum_ht(0, 1)
-        gather_tab2_scales(1)
-        gather_tab2_words(1)
         gather_tab_words(1)
         part_passes(1)
+        open_z(0, 0)
+        open_z(0, 1)
+        open_z(0, 2)
+        open_z(0, 3)
+        open_z(1, 0)
+        open_z(1, 1)
+        negate_bias()
         round_wv(0, 0)
-        round_wv(0, 1, parts=2)
-        sign_bias()
+        round_wv(0, 1)
+        gather_tab2_scales()
+        gather_tab2_words(0)
+        gather_tab2_words(1)
         quantise_wv(0)
-        make_rest(0, 0, False, early=True)
-        make_gate(0, 2, True)
-        rest_from_gate(0, 2)
-        make_gate(0, 0, True)
-        make_gate(0, 1, True)
-        rest_from_gate(0, 1)
+        close_z(0, 0)
+        sum_ht(0, 0)
+        close_z(0, 1)
+        sum_ht(0, 1)
+        close_z(0, 2)
+        close_z(0, 3)
+        close_z(1, 0)
+        close_z(1, 1)
+        make_rest(0, 0, True, early_bias)
+        gate_from_rest(0, 0)
+        make_rest(0, 1, True, early_bias)
+        gate_from_rest(0, 1)
         sum_hv(0, 0)
-        sum_z(1, 0)
         sum_hv(0, 1)
-        t_on_vector(0, 0)
-        t_on_vector(0, 2)
+        t_by_rest(0, 0)
         sum_ht(1, 0)
+        t_by_rest(0, 1)
         sum_hv(1, 0)
         v_by_gate(0, 0)
         join_on_gpsimd(0, 0)
-        sum_z(1, 1)
-        make_rest(1, 0, False)
-        make_gate(1, 0, True)
-        v_by_gate(0, 1)
-        t_on_vector(0, 1)
-        join_on_gpsimd(0, 1)
         sum_ht(1, 1)
+        v_by_gate(0, 1)
+        join_on_gpsimd(0, 1)
         sum_hv(1, 1)
-        sum_ht(0, 3)
         round_wv(1, 0)
+        make_rest(1, 0, False, early_bias)
+        make_gate(1, 0)
+        open_z(1, 2)
+        close_z(1, 2)
         round_wv(1, 1)
-        t_on_vector(1, 0)
+        t_by_rest(1, 0)
+        sum_ht(0, 2)
         v_by_gate(1, 0)
         join_on_gpsimd(1, 0)
         quantise_wv(1)
-        sum_z(1, 2)
         sum_hv(0, 2)
-        make_rest(1, 1, False)
-        make_gate(1, 1, True)
-        t_on_vector(1, 1)
+        make_rest(1, 1, False, early_bias)
+        make_gate(1, 1)
+        sum_z(1, 3)
+        t_by_rest(1, 1)
+        sum_ht(0, 3)
         v_by_gate(1, 1)
         join_on_gpsimd(1, 1)
         sum_hv(0, 3)
-        sum_z(1, 3)
+        make_rest(0, 2, False, early_bias)
+        make_gate(0, 2)
         sum_ht(1, 2)
-        make_rest(0, 3, False)
-        make_gate(0, 3, True)
+        t_by_rest(0, 2)
+        sum_hv(1, 2)
         v_by_gate(0, 2)
         join_on_gpsimd(0, 2)
-        sum_hv(1, 2)
-        t_on_vector(0, 3)
+        sum_ht(1, 3)
+        make_rest(0, 3, False, early_bias)
+        make_gate(0, 3)
+        sum_hv(1, 3)
+        t_by_rest(0, 3)
         v_by_gate(0, 3)
         join_on_gpsimd(0, 3)
-        sum_ht(1, 3)
-        sum_hv(1, 3)
-        make_rest(1, 2, True)
-        make_rest(1, 3, True)
-        t_on_vector(1, 2)
+        make_rest(1, 2, True, early_bias)
+        make_rest(1, 3, True, early_bias)
+        t_by_rest(1, 2)
         v_by_rest(1, 2)
-        t_on_vector(1, 3)
+        t_by_rest(1, 3)
         v_by_rest(1, 3, parts=2)
         join_on_vector(1, 2)
         join_on_vector(1, 3, parts=2)

@@ -111,18 +111,18 @@ def tile_list_gmu_relu_none_kernel(
         load_bytes(tab_s[96:128, :], tab_scales.rearrange("a q t -> q a t"), nc.sync)
         load_bytes(tab_w[:], tab_words[0].rearrange("p t i -> p (t i)"), nc.sync)
         for g in range(QUADS):
-            load_bytes(zv_s[32 * g : 32 * g + 4, :, :], zv_scales[:, 4 * g : 4 * g + 4, :].rearrange("a q n -> q a n"), nc.sync)
+            load_bytes(zv_s[g : P : 32, :, :], zv_scales[:, g : 16 : 4, :].rearrange("a q n -> q a n"), nc.sync)
         load_bytes(zv_w[:], zv_words.rearrange("a p n -> p a n"), nc.sync)
         nc.sync.dma_start(list2[:], offs2)
         load_wv(0, 0)
         nc.vector.tensor_copy(picked_s[:], tab_s[:].indirect(list1[:]))
-        for g in range(QUADS):
+        for g in (0, 2, 1, 3):
             load_bytes(planes[32 * g : 32 * g + 4, :, :], picked_s[96 + 8 * g : 104 + 8 * g, :], nc.sync)
         load_wv(0, 1)
         for g in range(QUADS):
-            load_bytes(tab2_s[32 * g : 32 * g + 4, :], tab2_scales[0, 4 * g : 4 * g + 4, :], nc.sync)
+            load_bytes(tab2_s[g : P : 32, :], tab2_scales[0, g : 16 : 4, :], nc.sync)
         load_bytes(tab2_w[:], tab2_words[0].rearrange("p t i -> p (t i)"), nc.sync)
-        for g in range(1, QUADS):
+        for g in (2, 1, 3):
             load_bytes(weight_s[32 * g : 32 * g + 4, :], weight_s[4 * g : 4 * g + 4, :], nc.sync)
         load_bytes(zt_w[:], zt_words[0], nc.sync)
         load_bytes(wt_w[:], wt_words[0].rearrange("p n i -> p (n i)"), nc.sync)

@@ -47,9 +47,9 @@ def tile_list_gmu_relu_none_kernel(
         list1 = kept("list1", [P, J // 16], U16)
         list2 = kept("list2", [P, J // 16], U16)
         tab_w = kept("tab_w", [P, T], I32)
-        tab2_w = placed("tab2_w", [P, T], I32, 8 * 4 * CHUNK)
+        tab2_w = kept("tab2_w", [P, T], I32)
         tab_s = kept("tab_s", [P, T], U8)
-        tab2_s = kept("tab2_s", [P, T], U8)
+        tab2_s = placed("tab2_s", [P, T], U8, 8 * 4 * CHUNK)
         zv_w = kept("zv_w", [P, PASSES, 2 * N], U8)
         zt_w = kept("zt_w", [P, 2 * N], U8)
         wt_w = kept("wt_w", [P, N], I32)
@@ -65,7 +65,7 @@ def tile_list_gmu_relu_none_kernel(
         wv_bf = [kept("wv_bf%d" % h, [P, PASSES, HALF, 4], BF16) for h in range(2)]
         picked_s = kept("picked_s", [P, J], U8)
         planes = kept("planes", [P, PASSES, J], U8)
-        picked2_s = kept("picked2_s", [P, J], U8)
+        picked2_s = [kept("picked2_s%d" % c, [P, CHUNK], U8) for c in range(2)]
         parted = [kept("parted%d" % c, [P, PASSES, 2 * CHUNK], U8) for c in range(2)]
         word_bytes = 4 * CHUNK
 
@@ -102,6 +102,9 @@ def tile_list_gmu_relu_none_kernel(
         def chunk_cols(c):
             return slice(c * CHUNK, (c + 1) * CHUNK)
 
+        def load_tab2_scales(r):
+            load_bytes(tab2_s[r : P : 32, :], tab2_scales[0, r : 16 : 4, :], nc.sync)
+
         load_bytes(zt_s[0:16, :], zt_scales[0], nc.gpsimd)
         load_bytes(wt_s[0:16, :], wt_scales[0], nc.gpsimd)
         nc.gpsimd.memset(planes[:].rearrange("p a j -> p (a j)").bitcast(I32), 0)
@@ -110,27 +113,28 @@ def tile_list_gmu_relu_none_kernel(
         nc.sync.dma_start(list1[:], offs)
         load_bytes(tab_s[96:128, :], tab_scales.rearrange("a q t -> q a t"), nc.sync)
         load_bytes(tab_w[:], tab_words[0].rearrange("p t i -> p (t i)"), nc.sync)
-        for g in range(QUADS):
-            load_bytes(zv_s[g : P : 32, :, :], zv_scales[:, g : 16 : 4, :].rearrange("a q n -> q a n"), nc.sync)
-        load_bytes(zv_w[:], zv_words.rearrange("a p n -> p a n"), nc.sync)
+        for r in range(4):
+            load_bytes(zv_s[r : P : 32, :, :], zv_scales[:, r : 16 : 4, :].rearrange("a q n -> q a n"), nc.sync)
         nc.sync.dma_start(list2[:], offs2)
-        load_wv(0, 0)
+        load_bytes(tab2_w[:], tab2_words[0].rearrange("p t i -> p (t i)"), nc.sync)
+        load_bytes(zv_w[:], zv_words.rearrange("a p n -> p a n"), nc.sync)
         nc.vector.tensor_copy(picked_s[:], tab_s[:].indirect(list1[:]))
         for g in (0, 2, 1, 3):
             load_bytes(planes[32 * g : 32 * g + 4, :, :], picked_s[96 + 8 * g : 104 + 8 * g, :], nc.sync)
+        load_wv(0, 0)
+        load_tab2_scales(0)
         load_wv(0, 1)
-        for g in range(QUADS):
-            load_bytes(tab2_s[g : P : 32, :], tab2_scales[0, g : 16 : 4, :], nc.sync)
-        load_bytes(tab2_w[:], tab2_words[0].rearrange("p t i -> p (t i)"), nc.sync)
-        for g in (2, 1, 3):
-            load_bytes(weight_s[32 * g : 32 * g + 4, :], weight_s[4 * g : 4 * g + 4, :], nc.sync)
+        for r in range(1, 4):
+            load_tab2_scales(r)
         load_bytes(zt_w[:], zt_words[0], nc.sync)
         load_bytes(wt_w[:], wt_words[0].rearrange("p n i -> p (n i)"), nc.sync)
+        for g in (2, 1, 3):
+            load_bytes(weight_s[32 * g : 32 * g + 4, :], weight_s[4 * g : 4 * g + 4, :], nc.sync)
         load_wv(1, 0)
         load_wv(1, 1)
 
-        def gather_tab2_scales():
-            nc.vector.tensor_copy(picked2_s[:], tab2_s[:].indirect(list2[:]))
+        def gather_tab2_scales(c):
+            nc.vector.tensor_copy(picked2_s[c][:], tab2_s[:].indirect(list2[:, list_cols(c)]))
 
         def gather_tab2_words(c):
             nc.vector.tensor_copy(picked2_w[c][:], tab2_w[:].bitcast(U32).indirect(list2[:, list_cols(c)]))
@@ -182,7 +186,7 @@ def tile_list_gmu_relu_none_kernel(
             cols = slice(t * P, (t + 1) * P)
             nc.tensor.matmul_mx(
                 out=new_sum("ht", c, t)[:], lhsT=wt_w[:, cols].bitcast(FP8X4), lhsT_scale=wt_s[:, cols],
-                rhs=picked2_w[c][:].bitcast(FP8X4), rhs_scale=picked2_s[:, chunk_cols(c)], start=True, stop=True,
+                rhs=picked2_w[c][:].bitcast(FP8X4), rhs_scale=picked2_s[c][:], start=True, stop=True,
             )
 
         def sum_hv(c, t):
@@ -209,7 +213,7 @@ def tile_list_gmu_relu_none_kernel(
             cols = slice(t * P, (t + 1) * P)
             nc.tensor.matmul_mx(
                 out=sums["z", c, t][0][:], lhsT=zt_w[:, 2 * t * P : 2 * (t + 1) * P].bitcast(FP4X4), lhsT_scale=zt_s[:, cols],
-                rhs=picked2_w[c][:].bitcast(FP8X4), rhs_scale=picked2_s[:, chunk_cols(c)], start=False, stop=True,
+                rhs=picked2_w[c][:].bitcast(FP8X4), rhs_scale=picked2_s[c][:], start=False, stop=True,
             )
 
         def sum_z(c, t):
@@ -282,9 +286,10 @@ def tile_list_gmu_relu_none_kernel(
         negate_bias()
         round_wv(0, 0)
         round_wv(0, 1)
-        gather_tab2_scales()
         gather_tab2_words(0)
         gather_tab2_words(1)
+        gather_tab2_scales(0)
+        gather_tab2_scales(1)
         quantise_wv(0)
         close_z(0, 0)
         sum_ht(0, 0)

@@ -49,7 +49,7 @@ def tile_list_gmu_relu_none_kernel(
         tab_w = kept("tab_w", [P, T], I32)
         tab2_w = kept("tab2_w", [P, T], I32)
         tab_s = kept("tab_s", [P, T], U8)
-        tab2_s = placed("tab2_s", [P, T], U8, 8 * 4 * CHUNK)
+        tab2_s = kept("tab2_s", [P, T], U8)
         zv_w = kept("zv_w", [P, PASSES, 2 * N], U8)
         zt_w = kept("zt_w", [P, 2 * N], U8)
         wt_w = kept("wt_w", [P, N], I32)
@@ -60,34 +60,27 @@ def tile_list_gmu_relu_none_kernel(
         early_bias = kept("early_bias", [P, 2, N_TILES], F32)
         warm_in = kept("warm_in", [P, 8], F32)
         warm_out = kept("warm_out", [P, 8], F32)
-        wv_w = [placed("wv_w0", [P, PASSES, HALF], U32, 8 * 4 * CHUNK), kept("wv_w1", [P, PASSES, HALF], U32)]
+        wv_w = [kept("wv_w0", [P, PASSES, HALF], U32), kept("wv_w1", [P, PASSES, HALF], U32)]
         wv_s = [kept("wv_s%d" % h, [P, PASSES, HALF], U8) for h in range(2)]
-        wv_bf = [kept("wv_bf%d" % h, [P, PASSES, HALF, 4], BF16) for h in range(2)]
+        wv_bf = [kept("wv_bf0", [P, PASSES, HALF, 4], BF16), kept("wv_bf1", [P, PASSES, HALF, 4], BF16)]
         picked_s = kept("picked_s", [P, J], U8)
         planes = kept("planes", [P, PASSES, J], U8)
-        picked2_s = [kept("picked2_s%d" % c, [P, CHUNK], U8) for c in range(2)]
+        picked2_s = [kept("picked2_s0", [P, CHUNK], U8), kept("picked2_s1", [P, CHUNK], U8)]
         parted = [kept("parted%d" % c, [P, PASSES, 2 * CHUNK], U8) for c in range(2)]
-        word_bytes = 4 * CHUNK
 
-        picked_w = [
-            [(0, CHUNK // 2, placed("picked_w0a", [P, CHUNK // 2], U32, word_bytes - 256)),
-             (CHUNK // 2, CHUNK // 2, kept("picked_w0b", [P, CHUNK // 2], U32))],
-            [(CHUNK, CHUNK, placed("picked_w1", [P, CHUNK], U32, word_bytes))],
-        ]
-        picked2_w = [kept("picked2_w%d" % c, [P, CHUNK], U32) for c in range(2)]
+        picked_w = [[(c * CHUNK, CHUNK, kept("picked_w%d" % c, [P, CHUNK], U32))] for c in range(2)]
+        picked2_w = [kept("picked2_w0", [P, CHUNK], U32), kept("picked2_w1", [P, CHUNK], U32)]
 
-        raw_at = 2 * word_bytes
-        wv_raw = [[kept("wv_raw%d0" % h, [P, 4, HALF], F32), placed("wv_raw%d1" % h, [P, 4, HALF], F32, raw_at * (h + 1))]
-                  for h in range(2)]
-        late_bias = placed("late_bias", [P, 2, N_TILES], F32, 2 * raw_at)
-        held_rest = placed("held_rest", [P, CHUNK], F32, raw_at)
+        wv_raw = [[kept("wv_raw00", [P, 4, HALF], F32), kept("wv_raw01", [P, 4, HALF], F32)],
+                  [kept("wv_raw10", [P, 4, HALF], F32), kept("wv_raw11", [P, 4, HALF], F32)]]
+        late_bias = kept("late_bias", [P, 2, N_TILES], F32)
 
         nc.gpsimd.memset(weight_s[:].bitcast(I32), 0)
-        nc.vector.memset(zv_s[:].rearrange("p a n -> p (a n)").bitcast(I32), 0)
-        nc.vector.memset(tab_s[0:96, :].bitcast(I32), 0)
-        nc.vector.memset(tab2_s[:].bitcast(I32), 0)
         nc.vector.memset(warm_in[:], 0.0)
         nc.scalar.activation(out=warm_out[:], in_=warm_in[:], func=ACT.Sigmoid)
+        nc.vector.memset(zv_s[:].rearrange("p a n -> p (a n)").bitcast(I32), 0)
+        nc.vector.memset(tab_s[0:96, :].bitcast(I32), 0)
+        nc.gpsimd.memset(planes[:].rearrange("p a j -> p (a j)").bitcast(I32), 0)
 
         def load_bytes(dst, src, queue):
             queue.dma_start(out=dst.bitcast(I32), in_=src.bitcast(I32))
@@ -102,34 +95,37 @@ def tile_list_gmu_relu_none_kernel(
         def chunk_cols(c):
             return slice(c * CHUNK, (c + 1) * CHUNK)
 
-        def load_tab2_scales(r):
-            load_bytes(tab2_s[r : P : 32, :], tab2_scales[0, r : 16 : 4, :], nc.sync)
-
         load_bytes(zt_s[0:16, :], zt_scales[0], nc.gpsimd)
         load_bytes(wt_s[0:16, :], wt_scales[0], nc.gpsimd)
-        nc.gpsimd.memset(planes[:].rearrange("p a j -> p (a j)").bitcast(I32), 0)
+        nc.gpsimd.memset(tab2_s[:].bitcast(I32), 0)
         with nc.allow_non_contiguous_dma(reason="one bias value to a partition"):
             nc.gpsimd.dma_start(out=early_bias[:, 0, :], in_=b.rearrange("(t p) -> p t", p=P))
         nc.sync.dma_start(list1[:], offs)
         load_bytes(tab_s[96:128, :], tab_scales.rearrange("a q t -> q a t"), nc.sync)
         load_bytes(tab_w[:], tab_words[0].rearrange("p t i -> p (t i)"), nc.sync)
-        for r in range(4):
-            load_bytes(zv_s[r : P : 32, :, :], zv_scales[:, r : 16 : 4, :].rearrange("a q n -> q a n"), nc.sync)
-        nc.sync.dma_start(list2[:], offs2)
-        load_bytes(tab2_w[:], tab2_words[0].rearrange("p t i -> p (t i)"), nc.sync)
+        load_bytes(zv_s[0 : P : 32, :, :], zv_scales[:, 0 : 16 : 4, :].rearrange("a q n -> q a n"), nc.sync)
+        load_bytes(zv_s[1 : P : 32, :, :], zv_scales[:, 1 : 16 : 4, :].rearrange("a q n -> q a n"), nc.sync)
+        load_bytes(zv_s[2 : P : 32, :, :], zv_scales[:, 2 : 16 : 4, :].rearrange("a q n -> q a n"), nc.sync)
+        load_bytes(zv_s[3 : P : 32, :, :], zv_scales[:, 3 : 16 : 4, :].rearrange("a q n -> q a n"), nc.sync)
         load_bytes(zv_w[:], zv_words.rearrange("a p n -> p a n"), nc.sync)
+        load_bytes(tab2_w[:], tab2_words[0].rearrange("p t i -> p (t i)"), nc.sync)
+        nc.sync.dma_start(list2[:], offs2)
         nc.vector.tensor_copy(picked_s[:], tab_s[:].indirect(list1[:]))
-        for g in (0, 2, 1, 3):
-            load_bytes(planes[32 * g : 32 * g + 4, :, :], picked_s[96 + 8 * g : 104 + 8 * g, :], nc.sync)
+        load_bytes(planes[0 : 4, :, :], picked_s[96 : 104, :], nc.sync)
+        load_bytes(planes[64 : 68, :, :], picked_s[112 : 120, :], nc.sync)
+        load_bytes(planes[32 : 36, :, :], picked_s[104 : 112, :], nc.sync)
+        load_bytes(planes[96 : 100, :, :], picked_s[120 : 128, :], nc.sync)
         load_wv(0, 0)
-        load_tab2_scales(0)
+        load_bytes(tab2_s[0 : P : 32, :], tab2_scales[0, 0 : 16 : 4, :], nc.sync)
+        load_bytes(tab2_s[1 : P : 32, :], tab2_scales[0, 1 : 16 : 4, :], nc.sync)
+        load_bytes(tab2_s[2 : P : 32, :], tab2_scales[0, 2 : 16 : 4, :], nc.sync)
+        load_bytes(tab2_s[3 : P : 32, :], tab2_scales[0, 3 : 16 : 4, :], nc.sync)
         load_wv(0, 1)
-        for r in range(1, 4):
-            load_tab2_scales(r)
         load_bytes(zt_w[:], zt_words[0], nc.sync)
+        load_bytes(weight_s[64 : 68, :], weight_s[8 : 12, :], nc.sync)
+        load_bytes(weight_s[32 : 36, :], weight_s[4 : 8, :], nc.sync)
+        load_bytes(weight_s[96 : 100, :], weight_s[12 : 16, :], nc.sync)
         load_bytes(wt_w[:], wt_words[0].rearrange("p n i -> p (n i)"), nc.sync)
-        for g in (2, 1, 3):
-            load_bytes(weight_s[32 * g : 32 * g + 4, :], weight_s[4 * g : 4 * g + 4, :], nc.sync)
         load_wv(1, 0)
         load_wv(1, 1)
 
@@ -182,6 +178,14 @@ def tile_list_gmu_relu_none_kernel(
         def release(kind, c, t):
             free_banks.append(sums[kind, c, t][1])
 
+        def warm_tensor(passes):
+            acc = psum.tile([P, CHUNK], F32, name="warm_sum", tag="bank%d" % (BANKS - 1))
+            for repeat in range(passes):
+                nc.tensor.matmul_mx(
+                    out=acc[:], lhsT=zv_w[:, 0, 0 : 2 * P].bitcast(FP4X4), lhsT_scale=zv_s[:, 0, 0:P],
+                    rhs=zv_w[:, 1, :].bitcast(FP4X4), rhs_scale=zv_s[:, 1, :], start=True, stop=True,
+                )
+
         def sum_ht(c, t):
             cols = slice(t * P, (t + 1) * P)
             nc.tensor.matmul_mx(
@@ -220,13 +224,13 @@ def tile_list_gmu_relu_none_kernel(
             open_z(c, t)
             close_z(c, t)
 
-        def make_gate(c, t):
+        def make_gate(c, t, biases):
             gate[c, t] = work.tile([P, CHUNK], F32, name="gate")
-            nc.scalar.activation(out=gate[c, t][:], in_=sums["z", c, t][0][:], func=ACT.Sigmoid, bias=early_bias[:, 0, t : t + 1], scale=1.0)
+            nc.scalar.activation(out=gate[c, t][:], in_=sums["z", c, t][0][:], func=ACT.Sigmoid, bias=biases[:, 0, t : t + 1], scale=1.0)
             release("z", c, t)
 
-        def make_rest(c, t, last, biases=late_bias, into=None):
-            rest[c, t] = work.tile([P, CHUNK], F32, name="rest") if into is None else into
+        def make_rest(c, t, last, biases):
+            rest[c, t] = work.tile([P, CHUNK], F32, name="rest")
             nc.scalar.activation(out=rest[c, t][:], in_=sums["z", c, t][0][:], func=ACT.Sigmoid, bias=biases[:, 1, t : t + 1], scale=-1.0)
             if last:
                 release("z", c, t)
@@ -273,16 +277,17 @@ def tile_list_gmu_relu_none_kernel(
                 )
                 nc.sync.dma_start(out=out[t * P : (t + 1) * P, chunk_cols(c)][:, s], in_=result[:, s])
 
+        warm_tensor(4)
         gather_tab_words(0)
-        part_passes(0)
         gather_tab_words(1)
+        part_passes(0)
         part_passes(1)
         open_z(0, 0)
         open_z(0, 1)
-        open_z(0, 2)
-        open_z(0, 3)
         open_z(1, 0)
         open_z(1, 1)
+        open_z(0, 2)
+        open_z(0, 3)
         negate_bias()
         round_wv(0, 0)
         round_wv(0, 1)
@@ -292,19 +297,19 @@ def tile_list_gmu_relu_none_kernel(
         gather_tab2_scales(1)
         quantise_wv(0)
         close_z(0, 0)
-        sum_ht(0, 0)
         close_z(0, 1)
+        sum_ht(0, 0)
         sum_ht(0, 1)
-        close_z(0, 2)
-        close_z(0, 3)
-        close_z(1, 0)
-        close_z(1, 1)
         make_rest(0, 0, True, early_bias)
         gate_from_rest(0, 0)
+        sum_hv(0, 0)
         make_rest(0, 1, True, early_bias)
         gate_from_rest(0, 1)
-        sum_hv(0, 0)
         sum_hv(0, 1)
+        close_z(1, 0)
+        close_z(1, 1)
+        close_z(0, 2)
+        close_z(0, 3)
         t_by_rest(0, 0)
         sum_ht(1, 0)
         t_by_rest(0, 1)
@@ -315,12 +320,11 @@ def tile_list_gmu_relu_none_kernel(
         v_by_gate(0, 1)
         join_on_gpsimd(0, 1)
         sum_hv(1, 1)
+        make_rest(1, 0, True, early_bias)
+        gate_from_rest(1, 0)
         round_wv(1, 0)
-        make_rest(1, 0, False, early_bias)
-        make_gate(1, 0)
-        open_z(1, 2)
-        close_z(1, 2)
         round_wv(1, 1)
+        sum_z(1, 2)
         t_by_rest(1, 0)
         sum_ht(0, 2)
         v_by_gate(1, 0)
@@ -328,7 +332,7 @@ def tile_list_gmu_relu_none_kernel(
         quantise_wv(1)
         sum_hv(0, 2)
         make_rest(1, 1, False, early_bias)
-        make_gate(1, 1)
+        make_gate(1, 1, early_bias)
         sum_z(1, 3)
         t_by_rest(1, 1)
         sum_ht(0, 3)
@@ -336,17 +340,17 @@ def tile_list_gmu_relu_none_kernel(
         join_on_gpsimd(1, 1)
         sum_hv(0, 3)
         make_rest(0, 2, False, early_bias)
-        make_gate(0, 2)
+        make_gate(0, 2, early_bias)
         sum_ht(1, 2)
         t_by_rest(0, 2)
         sum_hv(1, 2)
         v_by_gate(0, 2)
         join_on_gpsimd(0, 2)
-        sum_ht(1, 3)
         make_rest(0, 3, False, early_bias)
-        make_gate(0, 3)
-        sum_hv(1, 3)
+        make_gate(0, 3, early_bias)
+        sum_ht(1, 3)
         t_by_rest(0, 3)
+        sum_hv(1, 3)
         v_by_gate(0, 3)
         join_on_gpsimd(0, 3)
         make_rest(1, 2, True, early_bias)
@@ -354,6 +358,6 @@ def tile_list_gmu_relu_none_kernel(
         t_by_rest(1, 2)
         v_by_rest(1, 2)
         t_by_rest(1, 3)
-        v_by_rest(1, 3, parts=2)
         join_on_vector(1, 2)
+        v_by_rest(1, 3, parts=2)
         join_on_vector(1, 3, parts=2)

@@ -62,7 +62,8 @@ def tile_list_gmu_relu_none_kernel(
         warm_out = kept("warm_out", [P, 8], F32)
         wv_w = [kept("wv_w0", [P, PASSES, HALF], U32), kept("wv_w1", [P, PASSES, HALF], U32)]
         wv_s = [kept("wv_s%d" % h, [P, PASSES, HALF], U8) for h in range(2)]
-        wv_bf = [kept("wv_bf0", [P, PASSES, HALF, 4], BF16), kept("wv_bf1", [P, PASSES, HALF, 4], BF16)]
+        wv_bf = [kept("wv_bf0", [P, PASSES, HALF, 4], BF16), placed("wv_bf1", [P, PASSES, HALF, 4], BF16, 0)]
+        after_quantise = placed("after_quantise", [P, CHUNK], F32, 0)
         picked_s = kept("picked_s", [P, J], U8)
         planes = kept("planes", [P, PASSES, J], U8)
         picked2_s = [kept("picked2_s0", [P, CHUNK], U8), kept("picked2_s1", [P, CHUNK], U8)]
@@ -75,12 +76,13 @@ def tile_list_gmu_relu_none_kernel(
                   [kept("wv_raw10", [P, 4, HALF], F32), kept("wv_raw11", [P, 4, HALF], F32)]]
         late_bias = kept("late_bias", [P, 2, N_TILES], F32)
 
-        nc.gpsimd.memset(weight_s[:].bitcast(I32), 0)
         nc.vector.memset(warm_in[:], 0.0)
         nc.scalar.activation(out=warm_out[:], in_=warm_in[:], func=ACT.Sigmoid)
         nc.vector.memset(zv_s[:].rearrange("p a n -> p (a n)").bitcast(I32), 0)
         nc.vector.memset(tab_s[0:96, :].bitcast(I32), 0)
-        nc.gpsimd.memset(planes[:].rearrange("p a j -> p (a j)").bitcast(I32), 0)
+        nc.vector.memset(planes[:].rearrange("p a j -> p (a j)").bitcast(I32), 0)
+        nc.vector.memset(tab2_s[:].bitcast(I32), 0)
+        nc.vector.memset(weight_s[:].bitcast(I32), 0)
 
         def load_bytes(dst, src, queue):
             queue.dma_start(out=dst.bitcast(I32), in_=src.bitcast(I32))
@@ -97,9 +99,6 @@ def tile_list_gmu_relu_none_kernel(
 
         load_bytes(zt_s[0:16, :], zt_scales[0], nc.gpsimd)
         load_bytes(wt_s[0:16, :], wt_scales[0], nc.gpsimd)
-        nc.gpsimd.memset(tab2_s[:].bitcast(I32), 0)
-        with nc.allow_non_contiguous_dma(reason="one bias value to a partition"):
-            nc.gpsimd.dma_start(out=early_bias[:, 0, :], in_=b.rearrange("(t p) -> p t", p=P))
         nc.sync.dma_start(list1[:], offs)
         load_bytes(tab_s[96:128, :], tab_scales.rearrange("a q t -> q a t"), nc.sync)
         load_bytes(tab_w[:], tab_words[0].rearrange("p t i -> p (t i)"), nc.sync)
@@ -121,6 +120,8 @@ def tile_list_gmu_relu_none_kernel(
         load_bytes(tab2_s[2 : P : 32, :], tab2_scales[0, 2 : 16 : 4, :], nc.sync)
         load_bytes(tab2_s[3 : P : 32, :], tab2_scales[0, 3 : 16 : 4, :], nc.sync)
         load_wv(0, 1)
+        with nc.allow_non_contiguous_dma(reason="one bias value to a partition"):
+            nc.sync.dma_start(out=early_bias[:, 0, :], in_=b.rearrange("(t p) -> p t", p=P))
         load_bytes(zt_w[:], zt_words[0], nc.sync)
         load_bytes(weight_s[64 : 68, :], weight_s[8 : 12, :], nc.sync)
         load_bytes(weight_s[32 : 36, :], weight_s[4 : 8, :], nc.sync)
@@ -256,8 +257,9 @@ def tile_list_gmu_relu_none_kernel(
             )
             release("hv", c, t)
 
-        def join_on_gpsimd(c, t):
-            result = work.tile([P, CHUNK], F32, name="result")
+        def join_on_gpsimd(c, t, result=None):
+            if result is None:
+                result = work.tile([P, CHUNK], F32, name="result")
             nc.gpsimd.tensor_tensor(out=result[:], in0=from_t[c, t][:], in1=from_v[c, t][:], op=ALU.subtract)
             nc.sync.dma_start(out=out[t * P : (t + 1) * P, chunk_cols(c)], in_=result[:])
 
@@ -304,7 +306,6 @@ def tile_list_gmu_relu_none_kernel(
         gate_from_rest(0, 0)
         sum_hv(0, 0)
         make_rest(0, 1, True, early_bias)
-        gate_from_rest(0, 1)
         sum_hv(0, 1)
         close_z(1, 0)
         close_z(1, 1)
@@ -317,19 +318,19 @@ def tile_list_gmu_relu_none_kernel(
         v_by_gate(0, 0)
         join_on_gpsimd(0, 0)
         sum_ht(1, 1)
-        v_by_gate(0, 1)
-        join_on_gpsimd(0, 1)
+        v_by_rest(0, 1)
         sum_hv(1, 1)
-        make_rest(1, 0, True, early_bias)
-        gate_from_rest(1, 0)
+        make_rest(1, 0, False, early_bias)
+        make_gate(1, 0, early_bias)
         round_wv(1, 0)
         round_wv(1, 1)
         sum_z(1, 2)
         t_by_rest(1, 0)
         sum_ht(0, 2)
         v_by_gate(1, 0)
-        join_on_gpsimd(1, 0)
+        join_on_vector(0, 1)
         quantise_wv(1)
+        join_on_gpsimd(1, 0, after_quantise)
         sum_hv(0, 2)
         make_rest(1, 1, False, early_bias)
         make_gate(1, 1, early_bias)
@@ -358,6 +359,6 @@ def tile_list_gmu_relu_none_kernel(
         t_by_rest(1, 2)
         v_by_rest(1, 2)
         t_by_rest(1, 3)
-        join_on_vector(1, 2)
         v_by_rest(1, 3, parts=2)
+        join_on_vector(1, 2)
         join_on_vector(1, 3, parts=2)

@@ -77,7 +77,6 @@ def tile_list_gmu_relu_none_kernel(
         late_bias = kept("late_bias", [P, 2, N_TILES], F32)
 
         nc.vector.memset(warm_in[:], 0.0)
-        nc.scalar.activation(out=warm_out[:], in_=warm_in[:], func=ACT.Sigmoid)
         nc.vector.memset(zv_s[:].rearrange("p a n -> p (a n)").bitcast(I32), 0)
         nc.vector.memset(tab_s[0:96, :].bitcast(I32), 0)
         nc.vector.memset(planes[:].rearrange("p a j -> p (a j)").bitcast(I32), 0)
@@ -99,8 +98,9 @@ def tile_list_gmu_relu_none_kernel(
 
         load_bytes(zt_s[0:16, :], zt_scales[0], nc.gpsimd)
         load_bytes(wt_s[0:16, :], wt_scales[0], nc.gpsimd)
+        load_bytes(tab_s[96:128, :], tab_scales.rearrange("a q t -> q a t"), nc.scalar)
+        nc.scalar.activation(out=warm_out[:], in_=warm_in[:], func=ACT.Sigmoid)
         nc.sync.dma_start(list1[:], offs)
-        load_bytes(tab_s[96:128, :], tab_scales.rearrange("a q t -> q a t"), nc.sync)
         load_bytes(tab_w[:], tab_words[0].rearrange("p t i -> p (t i)"), nc.sync)
         load_bytes(zv_s[0 : P : 32, :, :], zv_scales[:, 0 : 16 : 4, :].rearrange("a q n -> q a n"), nc.sync)
         load_bytes(zv_s[1 : P : 32, :, :], zv_scales[:, 1 : 16 : 4, :].rearrange("a q n -> q a n"), nc.sync)
@@ -320,8 +320,8 @@ def tile_list_gmu_relu_none_kernel(
         sum_ht(1, 1)
         v_by_rest(0, 1)
         sum_hv(1, 1)
-        make_rest(1, 0, False, early_bias)
-        make_gate(1, 0, early_bias)
+        make_rest(1, 0, True, early_bias)
+        gate_from_rest(1, 0)
         round_wv(1, 0)
         round_wv(1, 1)
         sum_z(1, 2)
@@ -359,6 +359,6 @@ def tile_list_gmu_relu_none_kernel(
         t_by_rest(1, 2)
         v_by_rest(1, 2)
         t_by_rest(1, 3)
-        v_by_rest(1, 3, parts=2)
-        join_on_vector(1, 2)
+        v_by_rest(1, 3)
+        join_on_vector(1, 2, parts=2)
         join_on_vector(1, 3, parts=2)

@@ -17,14 +17,21 @@ ACT = mybir.ActivationFunctionType
 ALU = mybir.AluOpType
 
 P = 128
-K_PASS = 512
+PACK = 4
+K_PASS = P * PACK
 PASSES = K // K_PASS
+BLOCKS = K_PASS // 32
+QUAD = 32
+ROWS = 4
 CHUNK = 512
+CHUNKS = J // CHUNK
 N_TILES = N // P
 HALF = N // 2
-QUADS = 4
-PASS1_SHIFT = 16
+TAB_ROWS_AT = P - PASSES * BLOCKS
+QUADS_BY_PORT = (0, 2, 1, 3)
 BANKS = 8
+WARM_PASSES = 4
+PLUS, MINUS = 0, 1
 
 
 def tile_list_gmu_relu_none_kernel(
@@ -34,15 +41,12 @@ def tile_list_gmu_relu_none_kernel(
     nc = tc.nc
     with ExitStack() as ctx:
         keep = ctx.enter_context(tc.tile_pool(name="keep", bufs=1))
-        lapped = ctx.enter_context(tc.tile_pool(name="lapped", bufs=1))
-        work = ctx.enter_context(tc.tile_pool(name="work", bufs=2 * N_TILES))
+        reused = ctx.enter_context(tc.tile_pool(name="reused", bufs=1))
+        work = ctx.enter_context(tc.tile_pool(name="work", bufs=CHUNKS * N_TILES))
         psum = ctx.enter_context(tc.psum_pool(name="psum", bufs=1))
 
         def kept(name, shape, dtype):
             return keep.tile(shape, dtype, name=name, align_bytes=64)
-
-        def placed(name, shape, dtype, offset):
-            return lapped.tile(shape, dtype, name=name, align_bytes=64, offset=offset)
 
         list1 = kept("list1", [P, J // 16], U16)
         list2 = kept("list2", [P, J // 16], U16)
@@ -57,38 +61,39 @@ def tile_list_gmu_relu_none_kernel(
         weight_s = kept("weight_s", [P, 2 * N], U8)
         zt_s = weight_s[:, 0:N]
         wt_s = weight_s[:, N : 2 * N]
-        early_bias = kept("early_bias", [P, 2, N_TILES], F32)
+        bias = kept("bias", [P, 2, N_TILES], F32)
         warm_in = kept("warm_in", [P, 8], F32)
         warm_out = kept("warm_out", [P, 8], F32)
-        wv_w = [kept("wv_w0", [P, PASSES, HALF], U32), kept("wv_w1", [P, PASSES, HALF], U32)]
+        wv_w = [kept("wv_w%d" % h, [P, PASSES, HALF], U32) for h in range(2)]
         wv_s = [kept("wv_s%d" % h, [P, PASSES, HALF], U8) for h in range(2)]
-        wv_bf = [kept("wv_bf0", [P, PASSES, HALF, 4], BF16), placed("wv_bf1", [P, PASSES, HALF, 4], BF16, 0)]
-        after_quantise = placed("after_quantise", [P, CHUNK], F32, 0)
+        wv_bf = [
+            kept("wv_bf0", [P, PASSES, HALF, PACK], BF16),
+            reused.tile([P, PASSES, HALF, PACK], BF16, name="wv_bf1", align_bytes=64, offset=0),
+        ]
+        after_quantise = reused.tile([P, CHUNK], F32, name="after_quantise", align_bytes=64, offset=0)
         picked_s = kept("picked_s", [P, J], U8)
         planes = kept("planes", [P, PASSES, J], U8)
-        picked2_s = [kept("picked2_s0", [P, CHUNK], U8), kept("picked2_s1", [P, CHUNK], U8)]
-        parted = [kept("parted%d" % c, [P, PASSES, 2 * CHUNK], U8) for c in range(2)]
-
-        picked_w = [[(c * CHUNK, CHUNK, kept("picked_w%d" % c, [P, CHUNK], U32))] for c in range(2)]
-        picked2_w = [kept("picked2_w0", [P, CHUNK], U32), kept("picked2_w1", [P, CHUNK], U32)]
-
-        wv_raw = [[kept("wv_raw00", [P, 4, HALF], F32), kept("wv_raw01", [P, 4, HALF], F32)],
-                  [kept("wv_raw10", [P, 4, HALF], F32), kept("wv_raw11", [P, 4, HALF], F32)]]
-        late_bias = kept("late_bias", [P, 2, N_TILES], F32)
+        picked2_s = [kept("picked2_s%d" % c, [P, CHUNK], U8) for c in range(CHUNKS)]
+        parted = [kept("parted%d" % c, [P, PASSES, 2 * CHUNK], U8) for c in range(CHUNKS)]
+        picked_w = [kept("picked_w%d" % c, [P, CHUNK], U32) for c in range(CHUNKS)]
+        picked2_w = [kept("picked2_w%d" % c, [P, CHUNK], U32) for c in range(CHUNKS)]
+        wv_raw = [[kept("wv_raw%d%d" % (h, a), [P, PACK, HALF], F32) for a in range(PASSES)] for h in range(2)]
 
         nc.vector.memset(warm_in[:], 0.0)
+        nc.scalar.activation(out=warm_out[:], in_=warm_in[:], func=ACT.Sigmoid)
+
         nc.vector.memset(zv_s[:].rearrange("p a n -> p (a n)").bitcast(I32), 0)
-        nc.vector.memset(tab_s[0:96, :].bitcast(I32), 0)
+        nc.vector.memset(tab_s[0:TAB_ROWS_AT, :].bitcast(I32), 0)
         nc.vector.memset(planes[:].rearrange("p a j -> p (a j)").bitcast(I32), 0)
         nc.vector.memset(tab2_s[:].bitcast(I32), 0)
         nc.vector.memset(weight_s[:].bitcast(I32), 0)
 
-        def load_bytes(dst, src, queue):
+        def move_bytes(dst, src, queue=nc.sync):
             queue.dma_start(out=dst.bitcast(I32), in_=src.bitcast(I32))
 
         def load_wv(h, a):
             rows = wv[K_PASS * a : K_PASS * (a + 1), HALF * h : HALF * (h + 1)]
-            nc.sync.dma_start(out=wv_raw[h][a][:], in_=rows.rearrange("(p i) n -> p i n", i=4))
+            nc.sync.dma_start(out=wv_raw[h][a][:], in_=rows.rearrange("(p i) n -> p i n", i=PACK))
 
         def list_cols(c):
             return slice(c * CHUNK // 16, (c + 1) * CHUNK // 16)
@@ -96,56 +101,36 @@ def tile_list_gmu_relu_none_kernel(
         def chunk_cols(c):
             return slice(c * CHUNK, (c + 1) * CHUNK)
 
-        load_bytes(zt_s[0:16, :], zt_scales[0], nc.gpsimd)
-        load_bytes(wt_s[0:16, :], wt_scales[0], nc.gpsimd)
-        load_bytes(tab_s[96:128, :], tab_scales.rearrange("a q t -> q a t"), nc.scalar)
-        nc.scalar.activation(out=warm_out[:], in_=warm_in[:], func=ACT.Sigmoid)
+        move_bytes(zt_s[0:BLOCKS, :], zt_scales[0], nc.gpsimd)
+        move_bytes(wt_s[0:BLOCKS, :], wt_scales[0], nc.gpsimd)
+
         nc.sync.dma_start(list1[:], offs)
-        load_bytes(tab_w[:], tab_words[0].rearrange("p t i -> p (t i)"), nc.sync)
-        load_bytes(zv_s[0 : P : 32, :, :], zv_scales[:, 0 : 16 : 4, :].rearrange("a q n -> q a n"), nc.sync)
-        load_bytes(zv_s[1 : P : 32, :, :], zv_scales[:, 1 : 16 : 4, :].rearrange("a q n -> q a n"), nc.sync)
-        load_bytes(zv_s[2 : P : 32, :, :], zv_scales[:, 2 : 16 : 4, :].rearrange("a q n -> q a n"), nc.sync)
-        load_bytes(zv_s[3 : P : 32, :, :], zv_scales[:, 3 : 16 : 4, :].rearrange("a q n -> q a n"), nc.sync)
-        load_bytes(zv_w[:], zv_words.rearrange("a p n -> p a n"), nc.sync)
-        load_bytes(tab2_w[:], tab2_words[0].rearrange("p t i -> p (t i)"), nc.sync)
+        move_bytes(tab_s[TAB_ROWS_AT:P, :], tab_scales.rearrange("a q t -> q a t"))
+        move_bytes(tab_w[:], tab_words[0].rearrange("p t i -> p (t i)"))
+        for r in range(ROWS):
+            move_bytes(zv_s[r:P:QUAD, :, :], zv_scales[:, r:BLOCKS:ROWS, :].rearrange("a q n -> q a n"))
+        move_bytes(zv_w[:], zv_words.rearrange("a p n -> p a n"))
+        move_bytes(tab2_w[:], tab2_words[0].rearrange("p t i -> p (t i)"))
         nc.sync.dma_start(list2[:], offs2)
         nc.vector.tensor_copy(picked_s[:], tab_s[:].indirect(list1[:]))
-        load_bytes(planes[0 : 4, :, :], picked_s[96 : 104, :], nc.sync)
-        load_bytes(planes[64 : 68, :, :], picked_s[112 : 120, :], nc.sync)
-        load_bytes(planes[32 : 36, :, :], picked_s[104 : 112, :], nc.sync)
-        load_bytes(planes[96 : 100, :, :], picked_s[120 : 128, :], nc.sync)
+        for g in QUADS_BY_PORT:
+            first = TAB_ROWS_AT + PASSES * ROWS * g
+            move_bytes(planes[QUAD * g : QUAD * g + ROWS, :, :], picked_s[first : first + PASSES * ROWS, :])
         load_wv(0, 0)
-        load_bytes(tab2_s[0 : P : 32, :], tab2_scales[0, 0 : 16 : 4, :], nc.sync)
-        load_bytes(tab2_s[1 : P : 32, :], tab2_scales[0, 1 : 16 : 4, :], nc.sync)
-        load_bytes(tab2_s[2 : P : 32, :], tab2_scales[0, 2 : 16 : 4, :], nc.sync)
-        load_bytes(tab2_s[3 : P : 32, :], tab2_scales[0, 3 : 16 : 4, :], nc.sync)
+        for r in range(ROWS):
+            move_bytes(tab2_s[r:P:QUAD, :], tab2_scales[0, r:BLOCKS:ROWS, :])
         load_wv(0, 1)
         with nc.allow_non_contiguous_dma(reason="one bias value to a partition"):
-            nc.sync.dma_start(out=early_bias[:, 0, :], in_=b.rearrange("(t p) -> p t", p=P))
-        load_bytes(zt_w[:], zt_words[0], nc.sync)
-        load_bytes(weight_s[64 : 68, :], weight_s[8 : 12, :], nc.sync)
-        load_bytes(weight_s[32 : 36, :], weight_s[4 : 8, :], nc.sync)
-        load_bytes(weight_s[96 : 100, :], weight_s[12 : 16, :], nc.sync)
-        load_bytes(wt_w[:], wt_words[0].rearrange("p n i -> p (n i)"), nc.sync)
+            nc.sync.dma_start(out=bias[:, PLUS, :], in_=b.rearrange("(t p) -> p t", p=P))
+        move_bytes(zt_w[:], zt_words[0])
+        for g in QUADS_BY_PORT[1:]:
+            move_bytes(weight_s[QUAD * g : QUAD * g + ROWS, :], weight_s[ROWS * g : ROWS * (g + 1), :])
+        move_bytes(wt_w[:], wt_words[0].rearrange("p n i -> p (n i)"))
         load_wv(1, 0)
         load_wv(1, 1)
 
-        def gather_tab2_scales(c):
-            nc.vector.tensor_copy(picked2_s[c][:], tab2_s[:].indirect(list2[:, list_cols(c)]))
-
-        def gather_tab2_words(c):
-            nc.vector.tensor_copy(picked2_w[c][:], tab2_w[:].bitcast(U32).indirect(list2[:, list_cols(c)]))
-
-        def gather_tab_words(c):
-            for first, entries, tile in picked_w[c]:
-                nc.vector.tensor_copy(tile[:], tab_w[:].bitcast(U32).indirect(list1[:, first // 16 : (first + entries) // 16]))
-
         def part_passes(c):
-            for first, entries, tile in picked_w[c]:
-                at = first % CHUNK
-                nc.vector.tensor_copy(
-                    parted[c][:].bitcast(U16)[:, :, at : at + entries], tile[:].bitcast(U16).rearrange("p (j a) -> p a j", a=PASSES)
-                )
+            nc.vector.tensor_copy(parted[c][:].bitcast(U16), picked_w[c][:].bitcast(U16).rearrange("p (j a) -> p a j", a=PASSES))
 
         def round_wv(h, a):
             nc.scalar.activation(
@@ -153,12 +138,6 @@ def tile_list_gmu_relu_none_kernel(
                 in_=wv_raw[h][a][:].rearrange("p i (n m) -> p n i m", m=4),
                 func=ACT.Copy, scale=-1.0,
             )
-
-        def negate_bias():
-            nc.scalar.activation(out=early_bias[:, 1, :], in_=early_bias[:, 0, :], func=ACT.Copy, scale=-1.0)
-
-        def carry_bias():
-            nc.scalar.activation(out=late_bias[:], in_=early_bias[:], func=ACT.Copy)
 
         def quantise_wv(h):
             nc.vector.quantize_mx(
@@ -179,13 +158,27 @@ def tile_list_gmu_relu_none_kernel(
         def release(kind, c, t):
             free_banks.append(sums[kind, c, t][1])
 
-        def warm_tensor(passes):
-            acc = psum.tile([P, CHUNK], F32, name="warm_sum", tag="bank%d" % (BANKS - 1))
-            for repeat in range(passes):
+        def fp4_columns(words, t):
+            return words[:, 2 * t * P : 2 * (t + 1) * P].bitcast(FP4X4)
+
+        def open_z(c, t):
+            acc = new_sum("z", c, t)
+            for a in range(PASSES):
                 nc.tensor.matmul_mx(
-                    out=acc[:], lhsT=zv_w[:, 0, 0 : 2 * P].bitcast(FP4X4), lhsT_scale=zv_s[:, 0, 0:P],
-                    rhs=zv_w[:, 1, :].bitcast(FP4X4), rhs_scale=zv_s[:, 1, :], start=True, stop=True,
+                    out=acc[:], lhsT=fp4_columns(zv_w[:, a, :], t), lhsT_scale=zv_s[:, a, t * P : (t + 1) * P],
+                    rhs=parted[c][:, a, :].bitcast(FP4X4), rhs_scale=planes[:, a, chunk_cols(c)],
+                    start=(a == 0), stop=False,
                 )
+
+        def close_z(c, t):
+            nc.tensor.matmul_mx(
+                out=sums["z", c, t][0][:], lhsT=fp4_columns(zt_w, t), lhsT_scale=zt_s[:, t * P : (t + 1) * P],
+                rhs=picked2_w[c][:].bitcast(FP8X4), rhs_scale=picked2_s[c][:], start=False, stop=True,
+            )
+
+        def sum_z(c, t):
+            open_z(c, t)
+            close_z(c, t)
 
         def sum_ht(c, t):
             cols = slice(t * P, (t + 1) * P)
@@ -204,44 +197,23 @@ def tile_list_gmu_relu_none_kernel(
                     start=(a == 0), stop=(a == PASSES - 1),
                 )
 
-        def open_z(c, t):
-            cols = slice(t * P, (t + 1) * P)
-            acc = new_sum("z", c, t)
-            for a in range(PASSES):
-                nc.tensor.matmul_mx(
-                    out=acc[:], lhsT=zv_w[:, a, 2 * t * P : 2 * (t + 1) * P].bitcast(FP4X4), lhsT_scale=zv_s[:, a, cols],
-                    rhs=parted[c][:, a, :].bitcast(FP4X4), rhs_scale=planes[:, a, chunk_cols(c)],
-                    start=(a == 0), stop=False,
-                )
+        def sigmoid_of_z(name, c, t, side, scale):
+            result = work.tile([P, CHUNK], F32, name=name)
+            nc.scalar.activation(out=result[:], in_=sums["z", c, t][0][:], func=ACT.Sigmoid, bias=bias[:, side, t : t + 1], scale=scale)
+            return result
 
-        def close_z(c, t):
-            cols = slice(t * P, (t + 1) * P)
-            nc.tensor.matmul_mx(
-                out=sums["z", c, t][0][:], lhsT=zt_w[:, 2 * t * P : 2 * (t + 1) * P].bitcast(FP4X4), lhsT_scale=zt_s[:, cols],
-                rhs=picked2_w[c][:].bitcast(FP8X4), rhs_scale=picked2_s[c][:], start=False, stop=True,
-            )
-
-        def sum_z(c, t):
-            open_z(c, t)
-            close_z(c, t)
-
-        def make_gate(c, t, biases):
-            gate[c, t] = work.tile([P, CHUNK], F32, name="gate")
-            nc.scalar.activation(out=gate[c, t][:], in_=sums["z", c, t][0][:], func=ACT.Sigmoid, bias=biases[:, 0, t : t + 1], scale=1.0)
+        def make_rest(c, t):
+            rest[c, t] = sigmoid_of_z("rest", c, t, MINUS, -1.0)
             release("z", c, t)
 
-        def make_rest(c, t, last, biases):
-            rest[c, t] = work.tile([P, CHUNK], F32, name="rest")
-            nc.scalar.activation(out=rest[c, t][:], in_=sums["z", c, t][0][:], func=ACT.Sigmoid, bias=biases[:, 1, t : t + 1], scale=-1.0)
-            if last:
-                release("z", c, t)
+        def make_rest_and_gate(c, t):
+            rest[c, t] = sigmoid_of_z("rest", c, t, MINUS, -1.0)
+            gate[c, t] = sigmoid_of_z("gate", c, t, PLUS, 1.0)
+            release("z", c, t)
 
         def gate_from_rest(c, t):
             gate[c, t] = work.tile([P, CHUNK], F32, name="gate")
             nc.gpsimd.tensor_scalar(out=gate[c, t][:], in0=rest[c, t][:], scalar1=-1.0, scalar2=1.0, op0=ALU.mult, op1=ALU.add)
-
-        def spans(parts):
-            return [slice(i * CHUNK // parts, (i + 1) * CHUNK // parts) for i in range(parts)]
 
         def t_by_rest(c, t):
             from_t[c, t] = work.tile([P, CHUNK], F32, name="from_t")
@@ -257,108 +229,104 @@ def tile_list_gmu_relu_none_kernel(
             )
             release("hv", c, t)
 
-        def join_on_gpsimd(c, t, result=None):
-            if result is None:
-                result = work.tile([P, CHUNK], F32, name="result")
+        def join_on_gpsimd(c, t, result):
             nc.gpsimd.tensor_tensor(out=result[:], in0=from_t[c, t][:], in1=from_v[c, t][:], op=ALU.subtract)
             nc.sync.dma_start(out=out[t * P : (t + 1) * P, chunk_cols(c)], in_=result[:])
 
-        def v_by_rest(c, t, parts=1):
+        def new_result():
+            return work.tile([P, CHUNK], F32, name="result")
+
+        def v_by_rest(c, t):
             from_v[c, t] = work.tile([P, CHUNK], F32, name="from_v")
-            for s in spans(parts):
-                nc.vector.scalar_tensor_tensor(
-                    out=from_v[c, t][:, s], in0=rest[c, t][:, s], scalar=1.0, in1=sums["hv", c, t][0][:, s], op0=ALU.subtract, op1=ALU.mult
-                )
+            nc.vector.scalar_tensor_tensor(
+                out=from_v[c, t][:], in0=rest[c, t][:], scalar=1.0, in1=sums["hv", c, t][0][:], op0=ALU.subtract, op1=ALU.mult
+            )
             release("hv", c, t)
 
-        def join_on_vector(c, t, parts=1):
-            result = work.tile([P, CHUNK], F32, name="result")
-            for s in spans(parts):
+        def join_on_vector(c, t, parts):
+            result = new_result()
+            for i in range(parts):
+                s = slice(i * CHUNK // parts, (i + 1) * CHUNK // parts)
                 nc.vector.scalar_tensor_tensor(
                     out=result[:, s], in0=from_v[c, t][:, s], scalar=0.0, in1=from_t[c, t][:, s], op0=ALU.max, op1=ALU.add
                 )
                 nc.sync.dma_start(out=out[t * P : (t + 1) * P, chunk_cols(c)][:, s], in_=result[:, s])
 
-        warm_tensor(4)
-        gather_tab_words(0)
-        gather_tab_words(1)
-        part_passes(0)
-        part_passes(1)
-        open_z(0, 0)
-        open_z(0, 1)
-        open_z(1, 0)
-        open_z(1, 1)
-        open_z(0, 2)
-        open_z(0, 3)
-        negate_bias()
-        round_wv(0, 0)
-        round_wv(0, 1)
-        gather_tab2_words(0)
-        gather_tab2_words(1)
-        gather_tab2_scales(0)
-        gather_tab2_scales(1)
+        warm_sum = psum.tile([P, CHUNK], F32, name="warm_sum", tag="bank%d" % (BANKS - 1))
+        for repeat in range(WARM_PASSES):
+            nc.tensor.matmul_mx(
+                out=warm_sum[:], lhsT=fp4_columns(zv_w[:, 0, :], 0), lhsT_scale=zv_s[:, 0, 0:P],
+                rhs=zv_w[:, 1, :].bitcast(FP4X4), rhs_scale=zv_s[:, 1, :], start=True, stop=True,
+            )
+
+        for c in range(CHUNKS):
+            nc.vector.tensor_copy(picked_w[c][:], tab_w[:].bitcast(U32).indirect(list1[:, list_cols(c)]))
+        for c in range(CHUNKS):
+            part_passes(c)
+        for c, t in ((0, 0), (0, 1), (1, 0), (1, 1), (0, 2), (0, 3)):
+            open_z(c, t)
+        nc.scalar.activation(out=bias[:, MINUS, :], in_=bias[:, PLUS, :], func=ACT.Copy, scale=-1.0)
+        for a in range(PASSES):
+            round_wv(0, a)
+        for c in range(CHUNKS):
+            nc.vector.tensor_copy(picked2_w[c][:], tab2_w[:].bitcast(U32).indirect(list2[:, list_cols(c)]))
+        for c in range(CHUNKS):
+            nc.vector.tensor_copy(picked2_s[c][:], tab2_s[:].indirect(list2[:, list_cols(c)]))
         quantise_wv(0)
-        close_z(0, 0)
-        close_z(0, 1)
-        sum_ht(0, 0)
-        sum_ht(0, 1)
-        make_rest(0, 0, True, early_bias)
+
+        for t in range(2):
+            close_z(0, t)
+        for t in range(2):
+            sum_ht(0, t)
+        make_rest(0, 0)
         gate_from_rest(0, 0)
         sum_hv(0, 0)
-        make_rest(0, 1, True, early_bias)
+        make_rest(0, 1)
         sum_hv(0, 1)
-        close_z(1, 0)
-        close_z(1, 1)
-        close_z(0, 2)
-        close_z(0, 3)
+        for c, t in ((0, 2), (1, 0), (1, 1), (0, 3)):
+            close_z(c, t)
         t_by_rest(0, 0)
         sum_ht(1, 0)
         t_by_rest(0, 1)
         sum_hv(1, 0)
         v_by_gate(0, 0)
-        join_on_gpsimd(0, 0)
+        join_on_gpsimd(0, 0, new_result())
         sum_ht(1, 1)
         v_by_rest(0, 1)
         sum_hv(1, 1)
-        make_rest(1, 0, True, early_bias)
+        make_rest(1, 0)
         gate_from_rest(1, 0)
-        round_wv(1, 0)
-        round_wv(1, 1)
+        for a in range(PASSES):
+            round_wv(1, a)
         sum_z(1, 2)
         t_by_rest(1, 0)
         sum_ht(0, 2)
         v_by_gate(1, 0)
-        join_on_vector(0, 1)
+        join_on_vector(0, 1, parts=1)
         quantise_wv(1)
         join_on_gpsimd(1, 0, after_quantise)
         sum_hv(0, 2)
-        make_rest(1, 1, False, early_bias)
-        make_gate(1, 1, early_bias)
-        sum_z(1, 3)
-        t_by_rest(1, 1)
-        sum_ht(0, 3)
-        v_by_gate(1, 1)
-        join_on_gpsimd(1, 1)
-        sum_hv(0, 3)
-        make_rest(0, 2, False, early_bias)
-        make_gate(0, 2, early_bias)
-        sum_ht(1, 2)
-        t_by_rest(0, 2)
-        sum_hv(1, 2)
-        v_by_gate(0, 2)
-        join_on_gpsimd(0, 2)
-        make_rest(0, 3, False, early_bias)
-        make_gate(0, 3, early_bias)
-        sum_ht(1, 3)
-        t_by_rest(0, 3)
-        sum_hv(1, 3)
-        v_by_gate(0, 3)
-        join_on_gpsimd(0, 3)
-        make_rest(1, 2, True, early_bias)
-        make_rest(1, 3, True, early_bias)
-        t_by_rest(1, 2)
-        v_by_rest(1, 2)
-        t_by_rest(1, 3)
-        v_by_rest(1, 3)
-        join_on_vector(1, 2, parts=2)
-        join_on_vector(1, 3, parts=2)
+
+        refills = {
+            (1, 1): ((sum_z, 1, 3), (sum_ht, 0, 3), (sum_hv, 0, 3)),
+            (0, 2): ((sum_ht, 1, 2), (sum_hv, 1, 2)),
+            (0, 3): ((sum_ht, 1, 3), (sum_hv, 1, 3)),
+        }
+        for (c, t), later in refills.items():
+            make_rest_and_gate(c, t)
+            later[0][0](*later[0][1:])
+            t_by_rest(c, t)
+            later[1][0](*later[1][1:])
+            v_by_gate(c, t)
+            join_on_gpsimd(c, t, new_result())
+            for step, c2, t2 in later[2:]:
+                step(c2, t2)
+
+        last = ((1, 2), (1, 3))
+        for c, t in last:
+            make_rest(c, t)
+        for c, t in last:
+            t_by_rest(c, t)
+            v_by_rest(c, t)
+        for c, t in last:
+            join_on_vector(c, t, parts=2)

@@ -95,6 +95,14 @@ def tile_list_gmu_relu_none_kernel(
             rows = wv[K_PASS * a : K_PASS * (a + 1), HALF * h : HALF * (h + 1)]
             nc.sync.dma_start(out=wv_raw[h][a][:], in_=rows.rearrange("(p i) n -> p i n", i=PACK))
 
+        def load_zt(h):
+            cols = slice(2 * HALF * h, 2 * HALF * (h + 1))
+            move_bytes(zt_w[:, cols], zt_words[0][:, cols])
+
+        def load_wt(h):
+            cols = slice(HALF * h, HALF * (h + 1))
+            move_bytes(wt_w[:, cols], wt_words[0][:, cols, :].rearrange("p n i -> p (n i)"))
+
         def list_cols(c):
             return slice(c * CHUNK // 16, (c + 1) * CHUNK // 16)
 
@@ -103,6 +111,8 @@ def tile_list_gmu_relu_none_kernel(
 
         move_bytes(zt_s[0:BLOCKS, :], zt_scales[0], nc.gpsimd)
         move_bytes(wt_s[0:BLOCKS, :], wt_scales[0], nc.gpsimd)
+        with nc.allow_non_contiguous_dma(reason="one bias value to a partition"):
+            nc.gpsimd.dma_start(out=bias[:, PLUS, :], in_=b.rearrange("(t p) -> p t", p=P))
 
         nc.sync.dma_start(list1[:], offs)
         move_bytes(tab_s[TAB_ROWS_AT:P, :], tab_scales.rearrange("a q t -> q a t"))
@@ -120,14 +130,14 @@ def tile_list_gmu_relu_none_kernel(
         for r in range(ROWS):
             move_bytes(tab2_s[r:P:QUAD, :], tab2_scales[0, r:BLOCKS:ROWS, :])
         load_wv(0, 1)
-        with nc.allow_non_contiguous_dma(reason="one bias value to a partition"):
-            nc.sync.dma_start(out=bias[:, PLUS, :], in_=b.rearrange("(t p) -> p t", p=P))
-        move_bytes(zt_w[:], zt_words[0])
+        load_zt(0)
         for g in QUADS_BY_PORT[1:]:
             move_bytes(weight_s[QUAD * g : QUAD * g + ROWS, :], weight_s[ROWS * g : ROWS * (g + 1), :])
-        move_bytes(wt_w[:], wt_words[0].rearrange("p n i -> p (n i)"))
+        load_wt(0)
+        load_zt(1)
         load_wv(1, 0)
         load_wv(1, 1)
+        load_wt(1)
 
         def part_passes(c):
             nc.vector.tensor_copy(parted[c][:].bitcast(U16), picked_w[c][:].bitcast(U16).rearrange("p (j a) -> p a j", a=PASSES))
@@ -283,8 +293,8 @@ def tile_list_gmu_relu_none_kernel(
         sum_hv(0, 0)
         make_rest(0, 1)
         sum_hv(0, 1)
-        for c, t in ((0, 2), (1, 0), (1, 1), (0, 3)):
-            close_z(c, t)
+        for t in range(2):
+            close_z(1, t)
         t_by_rest(0, 0)
         sum_ht(1, 0)
         t_by_rest(0, 1)
@@ -294,6 +304,8 @@ def tile_list_gmu_relu_none_kernel(
         sum_ht(1, 1)
         v_by_rest(0, 1)
         sum_hv(1, 1)
+        for t in range(2, N_TILES):
+            close_z(0, t)
         make_rest(1, 0)
         gate_from_rest(1, 0)
         for a in range(PASSES):

@@ -54,7 +54,7 @@ def tile_list_gmu_relu_none_kernel(
         tab2_w = kept("tab2_w", [P, T], I32)
         tab_s = kept("tab_s", [P, T], U8)
         tab2_s = kept("tab2_s", [P, T], U8)
-        zv_w = kept("zv_w", [P, PASSES, 2 * N], U8)
+        zv_w = [kept("zv_w%d" % h, [P, PASSES, 2 * HALF], U8) for h in range(2)]
         zt_w = kept("zt_w", [P, 2 * N], U8)
         wt_w = kept("wt_w", [P, N], I32)
         zv_s = kept("zv_s", [P, PASSES, N], U8)
@@ -95,6 +95,9 @@ def tile_list_gmu_relu_none_kernel(
             rows = wv[K_PASS * a : K_PASS * (a + 1), HALF * h : HALF * (h + 1)]
             nc.sync.dma_start(out=wv_raw[h][a][:], in_=rows.rearrange("(p i) n -> p i n", i=PACK))
 
+        def load_zv(h):
+            move_bytes(zv_w[h][:], zv_words[:, :, 2 * HALF * h : 2 * HALF * (h + 1)].rearrange("a p n -> p a n"))
+
         def load_zt(h):
             cols = slice(2 * HALF * h, 2 * HALF * (h + 1))
             move_bytes(zt_w[:, cols], zt_words[0][:, cols])
@@ -119,7 +122,7 @@ def tile_list_gmu_relu_none_kernel(
         move_bytes(tab_w[:], tab_words[0].rearrange("p t i -> p (t i)"))
         for r in range(ROWS):
             move_bytes(zv_s[r:P:QUAD, :, :], zv_scales[:, r:BLOCKS:ROWS, :].rearrange("a q n -> q a n"))
-        move_bytes(zv_w[:], zv_words.rearrange("a p n -> p a n"))
+        load_zv(0)
         move_bytes(tab2_w[:], tab2_words[0].rearrange("p t i -> p (t i)"))
         nc.sync.dma_start(list2[:], offs2)
         nc.vector.tensor_copy(picked_s[:], tab_s[:].indirect(list1[:]))
@@ -127,6 +130,7 @@ def tile_list_gmu_relu_none_kernel(
             first = TAB_ROWS_AT + PASSES * ROWS * g
             move_bytes(planes[QUAD * g : QUAD * g + ROWS, :, :], picked_s[first : first + PASSES * ROWS, :])
         load_wv(0, 0)
+        load_zv(1)
         for r in range(ROWS):
             move_bytes(tab2_s[r:P:QUAD, :], tab2_scales[0, r:BLOCKS:ROWS, :])
         load_wv(0, 1)
@@ -134,9 +138,9 @@ def tile_list_gmu_relu_none_kernel(
         for g in QUADS_BY_PORT[1:]:
             move_bytes(weight_s[QUAD * g : QUAD * g + ROWS, :], weight_s[ROWS * g : ROWS * (g + 1), :])
         load_wt(0)
-        load_zt(1)
         load_wv(1, 0)
         load_wv(1, 1)
+        load_zt(1)
         load_wt(1)
 
         def part_passes(c):
@@ -175,7 +179,7 @@ def tile_list_gmu_relu_none_kernel(
             acc = new_sum("z", c, t)
             for a in range(PASSES):
                 nc.tensor.matmul_mx(
-                    out=acc[:], lhsT=fp4_columns(zv_w[:, a, :], t), lhsT_scale=zv_s[:, a, t * P : (t + 1) * P],
+                    out=acc[:], lhsT=fp4_columns(zv_w[t // 2][:, a, :], t % 2), lhsT_scale=zv_s[:, a, t * P : (t + 1) * P],
                     rhs=parted[c][:, a, :].bitcast(FP4X4), rhs_scale=planes[:, a, chunk_cols(c)],
                     start=(a == 0), stop=False,
                 )
@@ -265,8 +269,8 @@ def tile_list_gmu_relu_none_kernel(
         warm_sum = psum.tile([P, CHUNK], F32, name="warm_sum", tag="bank%d" % (BANKS - 1))
         for repeat in range(WARM_PASSES):
             nc.tensor.matmul_mx(
-                out=warm_sum[:], lhsT=fp4_columns(zv_w[:, 0, :], 0), lhsT_scale=zv_s[:, 0, 0:P],
-                rhs=zv_w[:, 1, :].bitcast(FP4X4), rhs_scale=zv_s[:, 1, :], start=True, stop=True,
+                out=warm_sum[:], lhsT=fp4_columns(zv_w[0][:, 0, :], 0), lhsT_scale=zv_s[:, 0, 0:P],
+                rhs=zv_w[0][:].rearrange("p a n -> p (a n)").bitcast(FP4X4), rhs_scale=zv_s[:, 1, :], start=True, stop=True,
             )
 
         for c in range(CHUNKS):

@@ -130,9 +130,9 @@ def tile_list_gmu_relu_none_kernel(
             first = TAB_ROWS_AT + PASSES * ROWS * g
             move_bytes(planes[QUAD * g : QUAD * g + ROWS, :, :], picked_s[first : first + PASSES * ROWS, :])
         load_wv(0, 0)
-        load_zv(1)
         for r in range(ROWS):
             move_bytes(tab2_s[r:P:QUAD, :], tab2_scales[0, r:BLOCKS:ROWS, :])
+        load_zv(1)
         load_wv(0, 1)
         load_zt(0)
         for g in QUADS_BY_PORT[1:]:

@@ -122,8 +122,8 @@ def tile_list_gmu_relu_none_kernel(
         move_bytes(tab_w[:], tab_words[0].rearrange("p t i -> p (t i)"))
         for r in range(ROWS):
             move_bytes(zv_s[r:P:QUAD, :, :], zv_scales[:, r:BLOCKS:ROWS, :].rearrange("a q n -> q a n"))
-        load_zv(0)
         move_bytes(tab2_w[:], tab2_words[0].rearrange("p t i -> p (t i)"))
+        load_zv(0)
         nc.sync.dma_start(list2[:], offs2)
         nc.vector.tensor_copy(picked_s[:], tab_s[:].indirect(list1[:]))
         for g in QUADS_BY_PORT:
@@ -269,8 +269,8 @@ def tile_list_gmu_relu_none_kernel(
         warm_sum = psum.tile([P, CHUNK], F32, name="warm_sum", tag="bank%d" % (BANKS - 1))
         for repeat in range(WARM_PASSES):
             nc.tensor.matmul_mx(
-                out=warm_sum[:], lhsT=fp4_columns(zv_w[0][:, 0, :], 0), lhsT_scale=zv_s[:, 0, 0:P],
-                rhs=zv_w[0][:].rearrange("p a n -> p (a n)").bitcast(FP4X4), rhs_scale=zv_s[:, 1, :], start=True, stop=True,
+                out=warm_sum[:], lhsT=fp4_columns(zv_s[:, 0, :], 0), lhsT_scale=zv_s[:, 0, 0:P],
+                rhs=zv_s[:].rearrange("p a n -> p (a n)").bitcast(FP4X4), rhs_scale=zv_s[:, 1, :], start=True, stop=True,
             )
 
         for c in range(CHUNKS):

@@ -31,6 +31,7 @@ TAB_ROWS_AT = P - PASSES * BLOCKS
 QUADS_BY_PORT = (0, 2, 1, 3)
 BANKS = 8
 WARM_PASSES = 4
+SCALAR_COLS = 160
 PLUS, MINUS = 0, 1
 
 
@@ -66,18 +67,32 @@ def tile_list_gmu_relu_none_kernel(
         warm_out = kept("warm_out", [P, 8], F32)
         wv_w = [kept("wv_w%d" % h, [P, PASSES, HALF], U32) for h in range(2)]
         wv_s = [kept("wv_s%d" % h, [P, PASSES, HALF], U8) for h in range(2)]
-        wv_bf = [
-            kept("wv_bf0", [P, PASSES, HALF, PACK], BF16),
-            reused.tile([P, PASSES, HALF, PACK], BF16, name="wv_bf1", align_bytes=64, offset=0),
-        ]
-        after_quantise = reused.tile([P, CHUNK], F32, name="after_quantise", align_bytes=64, offset=0)
+        def shared(name, shape, dtype, kib):
+            return reused.tile(shape, dtype, name=name, align_bytes=64, offset=kib * 1024)
+
+        wv_bf = [shared("wv_bf%d" % h, [P, PASSES, HALF, PACK], BF16, 4 * h) for h in range(2)]
+        second_raw = [shared("second_raw%d" % h, [P, PACK, HALF], F32, kib) for h, kib in enumerate((16, 9))]
+        held = {
+            key: shared("%s%d%d" % key, [P, CHUNK], F32, kib)
+            for key, kib in (
+                (("result", 0, 1), 4), (("gate", 1, 1), 6), (("rest", 1, 0), 8), (("gate", 1, 0), 10), (("rest", 1, 1), 12),
+                (("gate", 0, 3), 6), (("rest", 0, 2), 8), (("gate", 0, 2), 10), (("rest", 0, 3), 12),
+                (("rest", 1, 2), 8), (("rest", 1, 3), 10),
+                (("rest", 0, 0), 14), (("from_t", 0, 1), 14),
+            )
+        }
         picked_s = kept("picked_s", [P, J], U8)
         planes = kept("planes", [P, PASSES, J], U8)
-        picked2_s = [kept("picked2_s%d" % c, [P, CHUNK], U8) for c in range(CHUNKS)]
+        picked2_s = [kept("picked2_s0", [P, CHUNK], U8), shared("picked2_s1", [P, CHUNK], U8, 16)]
         parted = [kept("parted%d" % c, [P, PASSES, 2 * CHUNK], U8) for c in range(CHUNKS)]
         picked_w = [kept("picked_w%d" % c, [P, CHUNK], U32) for c in range(CHUNKS)]
         picked2_w = [kept("picked2_w%d" % c, [P, CHUNK], U32) for c in range(CHUNKS)]
-        wv_raw = [[kept("wv_raw%d%d" % (h, a), [P, PACK, HALF], F32) for a in range(PASSES)] for h in range(2)]
+        wv_raw = [[kept("wv_raw%d" % h, [P, PACK, HALF], F32), second_raw[h]] for h in range(2)]
+
+        def work_tile(kind, c, t):
+            if (kind, c, t) in held:
+                return held[kind, c, t]
+            return work.tile([P, CHUNK], F32, name=kind)
 
         nc.vector.memset(warm_in[:], 0.0)
         nc.scalar.activation(out=warm_out[:], in_=warm_in[:], func=ACT.Sigmoid)
@@ -97,10 +112,6 @@ def tile_list_gmu_relu_none_kernel(
 
         def load_zv(h):
             move_bytes(zv_w[h][:], zv_words[:, :, 2 * HALF * h : 2 * HALF * (h + 1)].rearrange("a p n -> p a n"))
-
-        def load_zt(h):
-            cols = slice(2 * HALF * h, 2 * HALF * (h + 1))
-            move_bytes(zt_w[:, cols], zt_words[0][:, cols])
 
         def load_wt(h):
             cols = slice(HALF * h, HALF * (h + 1))
@@ -134,23 +145,28 @@ def tile_list_gmu_relu_none_kernel(
             move_bytes(tab2_s[r:P:QUAD, :], tab2_scales[0, r:BLOCKS:ROWS, :])
         load_zv(1)
         load_wv(0, 1)
-        load_zt(0)
+        move_bytes(zt_w[:], zt_words[0])
         for g in QUADS_BY_PORT[1:]:
             move_bytes(weight_s[QUAD * g : QUAD * g + ROWS, :], weight_s[ROWS * g : ROWS * (g + 1), :])
         load_wt(0)
         load_wv(1, 0)
         load_wv(1, 1)
-        load_zt(1)
         load_wt(1)
 
         def part_passes(c):
             nc.vector.tensor_copy(parted[c][:].bitcast(U16), picked_w[c][:].bitcast(U16).rearrange("p (j a) -> p a j", a=PASSES))
 
-        def round_wv(h, a):
+        def round_wv(h, a, cols=slice(0, HALF)):
             nc.scalar.activation(
-                out=wv_bf[h][:, a].rearrange("p (n m) i -> p n i m", m=4),
-                in_=wv_raw[h][a][:].rearrange("p i (n m) -> p n i m", m=4),
+                out=wv_bf[h][:, a, cols].rearrange("p (n m) i -> p n i m", m=4),
+                in_=wv_raw[h][a][:, :, cols].rearrange("p i (n m) -> p n i m", m=4),
                 func=ACT.Copy, scale=-1.0,
+            )
+
+        def round_wv_on_gpsimd(h, a, cols):
+            nc.gpsimd.tensor_scalar(
+                out=wv_bf[h][:, a, cols], in0=wv_raw[h][a][:, :, cols].rearrange("p i n -> p n i"),
+                scalar1=-1.0, scalar2=0.0, op0=ALU.mult, op1=ALU.add,
             )
 
         def quantise_wv(h):
@@ -212,53 +228,48 @@ def tile_list_gmu_relu_none_kernel(
                 )
 
         def sigmoid_of_z(name, c, t, side, scale):
-            result = work.tile([P, CHUNK], F32, name=name)
+            result = work_tile(name, c, t)
             nc.scalar.activation(out=result[:], in_=sums["z", c, t][0][:], func=ACT.Sigmoid, bias=bias[:, side, t : t + 1], scale=scale)
             return result
 
         def make_rest(c, t):
             rest[c, t] = sigmoid_of_z("rest", c, t, MINUS, -1.0)
-            release("z", c, t)
 
-        def make_rest_and_gate(c, t):
-            rest[c, t] = sigmoid_of_z("rest", c, t, MINUS, -1.0)
+        def make_gate(c, t):
             gate[c, t] = sigmoid_of_z("gate", c, t, PLUS, 1.0)
-            release("z", c, t)
 
         def gate_from_rest(c, t):
-            gate[c, t] = work.tile([P, CHUNK], F32, name="gate")
+            gate[c, t] = work_tile("gate", c, t)
             nc.gpsimd.tensor_scalar(out=gate[c, t][:], in0=rest[c, t][:], scalar1=-1.0, scalar2=1.0, op0=ALU.mult, op1=ALU.add)
 
         def t_by_rest(c, t):
-            from_t[c, t] = work.tile([P, CHUNK], F32, name="from_t")
+            from_t[c, t] = work_tile("from_t", c, t)
             nc.vector.scalar_tensor_tensor(
                 out=from_t[c, t][:], in0=sums["ht", c, t][0][:], scalar=0.0, in1=rest[c, t][:], op0=ALU.max, op1=ALU.mult
             )
             release("ht", c, t)
 
         def v_by_gate(c, t):
-            from_v[c, t] = work.tile([P, CHUNK], F32, name="from_v")
+            from_v[c, t] = work_tile("from_v", c, t)
             nc.vector.scalar_tensor_tensor(
                 out=from_v[c, t][:], in0=sums["hv", c, t][0][:], scalar=0.0, in1=gate[c, t][:], op0=ALU.min, op1=ALU.mult
             )
             release("hv", c, t)
 
-        def join_on_gpsimd(c, t, result):
+        def join_on_gpsimd(c, t):
+            result = work_tile("result", c, t)
             nc.gpsimd.tensor_tensor(out=result[:], in0=from_t[c, t][:], in1=from_v[c, t][:], op=ALU.subtract)
             nc.sync.dma_start(out=out[t * P : (t + 1) * P, chunk_cols(c)], in_=result[:])
 
-        def new_result():
-            return work.tile([P, CHUNK], F32, name="result")
-
         def v_by_rest(c, t):
-            from_v[c, t] = work.tile([P, CHUNK], F32, name="from_v")
+            from_v[c, t] = work_tile("from_v", c, t)
             nc.vector.scalar_tensor_tensor(
                 out=from_v[c, t][:], in0=rest[c, t][:], scalar=1.0, in1=sums["hv", c, t][0][:], op0=ALU.subtract, op1=ALU.mult
             )
             release("hv", c, t)
 
         def join_on_vector(c, t, parts):
-            result = new_result()
+            result = work_tile("result", c, t)
             for i in range(parts):
                 s = slice(i * CHUNK // parts, (i + 1) * CHUNK // parts)
                 nc.vector.scalar_tensor_tensor(
@@ -277,66 +288,65 @@ def tile_list_gmu_relu_none_kernel(
             nc.vector.tensor_copy(picked_w[c][:], tab_w[:].bitcast(U32).indirect(list1[:, list_cols(c)]))
         for c in range(CHUNKS):
             part_passes(c)
-        for c, t in ((0, 0), (0, 1), (1, 0), (1, 1), (0, 2), (0, 3)):
+        for c, t in ((0, 0), (0, 1), (1, 0), (1, 1), (0, 2), (0, 3), (1, 2)):
             open_z(c, t)
         nc.scalar.activation(out=bias[:, MINUS, :], in_=bias[:, PLUS, :], func=ACT.Copy, scale=-1.0)
-        for a in range(PASSES):
-            round_wv(0, a)
+        round_wv(0, 0)
+        round_wv(0, 1, slice(0, SCALAR_COLS))
+        round_wv_on_gpsimd(0, 1, slice(SCALAR_COLS, HALF))
         for c in range(CHUNKS):
             nc.vector.tensor_copy(picked2_w[c][:], tab2_w[:].bitcast(U32).indirect(list2[:, list_cols(c)]))
-        for c in range(CHUNKS):
+
+        def gather_scales2(c):
             nc.vector.tensor_copy(picked2_s[c][:], tab2_s[:].indirect(list2[:, list_cols(c)]))
+
+        gather_scales2(0)
         quantise_wv(0)
+        gather_scales2(1)
 
         for t in range(2):
             close_z(0, t)
-        for t in range(2):
-            sum_ht(0, t)
-        make_rest(0, 0)
-        gate_from_rest(0, 0)
-        sum_hv(0, 0)
-        make_rest(0, 1)
+        sum_ht(0, 0)
+        for t in range(2, N_TILES):
+            close_z(0, t)
+        for t, refill in enumerate((sum_hv, sum_ht)):
+            make_rest(0, t)
+            release("z", 0, t)
+            gate_from_rest(0, t)
+            refill(0, t)
+        for a in range(PASSES):
+            round_wv(1, a)
+        t_by_rest(0, 0)
         sum_hv(0, 1)
         for t in range(2):
             close_z(1, t)
-        t_by_rest(0, 0)
+        v_by_gate(0, 0)
+        join_on_gpsimd(0, 0)
         sum_ht(1, 0)
         t_by_rest(0, 1)
         sum_hv(1, 0)
-        v_by_gate(0, 0)
-        join_on_gpsimd(0, 0, new_result())
+        v_by_gate(0, 1)
         sum_ht(1, 1)
-        v_by_rest(0, 1)
-        sum_hv(1, 1)
-        for t in range(2, N_TILES):
-            close_z(0, t)
-        make_rest(1, 0)
-        gate_from_rest(1, 0)
-        for a in range(PASSES):
-            round_wv(1, a)
-        sum_z(1, 2)
-        t_by_rest(1, 0)
-        sum_ht(0, 2)
-        v_by_gate(1, 0)
-        join_on_vector(0, 1, parts=1)
+        close_z(1, 2)
         quantise_wv(1)
-        join_on_gpsimd(1, 0, after_quantise)
-        sum_hv(0, 2)
+        join_on_gpsimd(0, 1)
 
         refills = {
-            (1, 1): ((sum_z, 1, 3), (sum_ht, 0, 3), (sum_hv, 0, 3)),
-            (0, 2): ((sum_ht, 1, 2), (sum_hv, 1, 2)),
-            (0, 3): ((sum_ht, 1, 3), (sum_hv, 1, 3)),
+            (1, 0): ((sum_hv, 1, 1), (sum_ht, 0, 2), (sum_hv, 0, 2)),
+            (1, 1): ((sum_ht, 0, 3), (sum_hv, 0, 3), (sum_z, 1, 3)),
+            (0, 2): ((sum_ht, 1, 2), (sum_hv, 1, 2), (sum_ht, 1, 3)),
+            (0, 3): ((sum_hv, 1, 3),),
         }
         for (c, t), later in refills.items():
-            make_rest_and_gate(c, t)
-            later[0][0](*later[0][1:])
-            t_by_rest(c, t)
-            later[1][0](*later[1][1:])
-            v_by_gate(c, t)
-            join_on_gpsimd(c, t, new_result())
-            for step, c2, t2 in later[2:]:
-                step(c2, t2)
+            make_rest(c, t)
+            make_gate(c, t)
+            release("z", c, t)
+            for reader, refill in zip((None, t_by_rest, v_by_gate), later + (None, None)):
+                if reader:
+                    reader(c, t)
+                if refill:
+                    refill[0](*refill[1:])
+            join_on_gpsimd(c, t)
 
         last = ((1, 2), (1, 3))
         for c, t in last:

@@ -31,7 +31,6 @@ TAB_ROWS_AT = P - PASSES * BLOCKS
 QUADS_BY_PORT = (0, 2, 1, 3)
 BANKS = 8
 WARM_PASSES = 4
-SCALAR_COLS = 160
 PLUS, MINUS = 0, 1
 
 
@@ -71,23 +70,23 @@ def tile_list_gmu_relu_none_kernel(
             return reused.tile(shape, dtype, name=name, align_bytes=64, offset=kib * 1024)
 
         wv_bf = [shared("wv_bf%d" % h, [P, PASSES, HALF, PACK], BF16, 4 * h) for h in range(2)]
-        second_raw = [shared("second_raw%d" % h, [P, PACK, HALF], F32, kib) for h, kib in enumerate((16, 9))]
+        last_raw = shared("last_raw", [P, PACK, HALF], F32, 9)
         held = {
             key: shared("%s%d%d" % key, [P, CHUNK], F32, kib)
             for key, kib in (
-                (("result", 0, 1), 4), (("gate", 1, 1), 6), (("rest", 1, 0), 8), (("gate", 1, 0), 10), (("rest", 1, 1), 12),
-                (("gate", 0, 3), 6), (("rest", 0, 2), 8), (("gate", 0, 2), 10), (("rest", 0, 3), 12),
-                (("rest", 1, 2), 8), (("rest", 1, 3), 10),
-                (("rest", 0, 0), 14), (("from_t", 0, 1), 14),
+                (("gate", 0, 0), 0), (("result", 1, 0), 4), (("from_t", 0, 0), 14), (("result", 0, 1), 14),
+                (("rest", 1, 1), 8), (("gate", 1, 1), 10), (("rest", 0, 2), 12), (("gate", 0, 2), 6),
+                (("rest", 0, 3), 8), (("gate", 0, 3), 10), (("rest", 1, 2), 12), (("rest", 1, 3), 6),
             )
         }
         picked_s = kept("picked_s", [P, J], U8)
         planes = kept("planes", [P, PASSES, J], U8)
-        picked2_s = [kept("picked2_s0", [P, CHUNK], U8), shared("picked2_s1", [P, CHUNK], U8, 16)]
+        picked2_s = [kept("picked2_s%d" % c, [P, CHUNK], U8) for c in range(CHUNKS)]
         parted = [kept("parted%d" % c, [P, PASSES, 2 * CHUNK], U8) for c in range(CHUNKS)]
         picked_w = [kept("picked_w%d" % c, [P, CHUNK], U32) for c in range(CHUNKS)]
         picked2_w = [kept("picked2_w%d" % c, [P, CHUNK], U32) for c in range(CHUNKS)]
-        wv_raw = [[kept("wv_raw%d" % h, [P, PACK, HALF], F32), second_raw[h]] for h in range(2)]
+        wv_raw = [[kept("wv_raw%d%d" % (h, a), [P, PACK, HALF], F32) for a in range(PASSES - h)] for h in range(2)]
+        wv_raw[1].append(last_raw)
 
         def work_tile(kind, c, t):
             if (kind, c, t) in held:
@@ -156,17 +155,11 @@ def tile_list_gmu_relu_none_kernel(
         def part_passes(c):
             nc.vector.tensor_copy(parted[c][:].bitcast(U16), picked_w[c][:].bitcast(U16).rearrange("p (j a) -> p a j", a=PASSES))
 
-        def round_wv(h, a, cols=slice(0, HALF)):
+        def round_wv(h, a):
             nc.scalar.activation(
-                out=wv_bf[h][:, a, cols].rearrange("p (n m) i -> p n i m", m=4),
-                in_=wv_raw[h][a][:, :, cols].rearrange("p i (n m) -> p n i m", m=4),
+                out=wv_bf[h][:, a].rearrange("p (n m) i -> p n i m", m=4),
+                in_=wv_raw[h][a][:].rearrange("p i (n m) -> p n i m", m=4),
                 func=ACT.Copy, scale=-1.0,
-            )
-
-        def round_wv_on_gpsimd(h, a, cols):
-            nc.gpsimd.tensor_scalar(
-                out=wv_bf[h][:, a, cols], in0=wv_raw[h][a][:, :, cols].rearrange("p i n -> p n i"),
-                scalar1=-1.0, scalar2=0.0, op0=ALU.mult, op1=ALU.add,
             )
 
         def quantise_wv(h):
@@ -288,52 +281,55 @@ def tile_list_gmu_relu_none_kernel(
             nc.vector.tensor_copy(picked_w[c][:], tab_w[:].bitcast(U32).indirect(list1[:, list_cols(c)]))
         for c in range(CHUNKS):
             part_passes(c)
-        for c, t in ((0, 0), (0, 1), (1, 0), (1, 1), (0, 2), (0, 3), (1, 2)):
+        for c, t in ((0, 0), (0, 1), (1, 0), (1, 1), (0, 2), (0, 3)):
             open_z(c, t)
         nc.scalar.activation(out=bias[:, MINUS, :], in_=bias[:, PLUS, :], func=ACT.Copy, scale=-1.0)
-        round_wv(0, 0)
-        round_wv(0, 1, slice(0, SCALAR_COLS))
-        round_wv_on_gpsimd(0, 1, slice(SCALAR_COLS, HALF))
+        for a in range(PASSES):
+            round_wv(0, a)
         for c in range(CHUNKS):
             nc.vector.tensor_copy(picked2_w[c][:], tab2_w[:].bitcast(U32).indirect(list2[:, list_cols(c)]))
-
-        def gather_scales2(c):
+        for c in range(CHUNKS):
             nc.vector.tensor_copy(picked2_s[c][:], tab2_s[:].indirect(list2[:, list_cols(c)]))
-
-        gather_scales2(0)
         quantise_wv(0)
-        gather_scales2(1)
 
         for t in range(2):
             close_z(0, t)
-        sum_ht(0, 0)
-        for t in range(2, N_TILES):
-            close_z(0, t)
-        for t, refill in enumerate((sum_hv, sum_ht)):
+        for t in range(2):
+            sum_ht(0, t)
+        close_z(0, 2)
+        close_z(1, 0)
+        for t in range(2):
             make_rest(0, t)
             release("z", 0, t)
-            gate_from_rest(0, t)
-            refill(0, t)
+            sum_hv(0, t)
+        gate_from_rest(0, 0)
+        make_rest(1, 0)
+        gate_from_rest(1, 0)
         for a in range(PASSES):
             round_wv(1, a)
         t_by_rest(0, 0)
-        sum_hv(0, 1)
-        for t in range(2):
-            close_z(1, t)
-        v_by_gate(0, 0)
-        join_on_gpsimd(0, 0)
         sum_ht(1, 0)
         t_by_rest(0, 1)
         sum_hv(1, 0)
-        v_by_gate(0, 1)
+        close_z(1, 1)
+        close_z(0, 3)
+        v_by_gate(0, 0)
+        join_on_gpsimd(0, 0)
         sum_ht(1, 1)
-        close_z(1, 2)
+        v_by_rest(0, 1)
+        sum_hv(1, 1)
+        release("z", 1, 0)
+        sum_z(1, 2)
+        t_by_rest(1, 0)
+        sum_ht(0, 2)
+        v_by_gate(1, 0)
+        join_on_vector(0, 1, parts=1)
         quantise_wv(1)
-        join_on_gpsimd(0, 1)
+        join_on_gpsimd(1, 0)
+        sum_hv(0, 2)
 
         refills = {
-            (1, 0): ((sum_hv, 1, 1), (sum_ht, 0, 2), (sum_hv, 0, 2)),
-            (1, 1): ((sum_ht, 0, 3), (sum_hv, 0, 3), (sum_z, 1, 3)),
+            (1, 1): ((sum_z, 1, 3), (sum_ht, 0, 3), (sum_hv, 0, 3)),
             (0, 2): ((sum_ht, 1, 2), (sum_hv, 1, 2), (sum_ht, 1, 3)),
             (0, 3): ((sum_hv, 1, 3),),
         }

@@ -31,6 +31,7 @@ TAB_ROWS_AT = P - PASSES * BLOCKS
 QUADS_BY_PORT = (0, 2, 1, 3)
 BANKS = 8
 WARM_PASSES = 4
+GPSIMD_COLS = 96
 PLUS, MINUS = 0, 1
 
 
@@ -74,7 +75,7 @@ def tile_list_gmu_relu_none_kernel(
         held = {
             key: shared("%s%d%d" % key, [P, CHUNK], F32, kib)
             for key, kib in (
-                (("gate", 0, 0), 0), (("result", 1, 0), 4), (("from_t", 0, 0), 14), (("result", 0, 1), 14),
+                (("result", 1, 0), 4), (("from_t", 0, 0), 14), (("result", 0, 1), 14),
                 (("rest", 1, 1), 8), (("gate", 1, 1), 10), (("rest", 0, 2), 12), (("gate", 0, 2), 6),
                 (("rest", 0, 3), 8), (("gate", 0, 3), 10), (("rest", 1, 2), 12), (("rest", 1, 3), 6),
             )
@@ -155,11 +156,17 @@ def tile_list_gmu_relu_none_kernel(
         def part_passes(c):
             nc.vector.tensor_copy(parted[c][:].bitcast(U16), picked_w[c][:].bitcast(U16).rearrange("p (j a) -> p a j", a=PASSES))
 
-        def round_wv(h, a):
+        def round_wv(h, a, cols=slice(0, HALF)):
             nc.scalar.activation(
-                out=wv_bf[h][:, a].rearrange("p (n m) i -> p n i m", m=4),
-                in_=wv_raw[h][a][:].rearrange("p i (n m) -> p n i m", m=4),
+                out=wv_bf[h][:, a, cols].rearrange("p (n m) i -> p n i m", m=4),
+                in_=wv_raw[h][a][:, :, cols].rearrange("p i (n m) -> p n i m", m=4),
                 func=ACT.Copy, scale=-1.0,
+            )
+
+        def round_wv_on_gpsimd(h, a, cols):
+            nc.gpsimd.tensor_scalar(
+                out=wv_bf[h][:, a, cols], in0=wv_raw[h][a][:, :, cols].rearrange("p i n -> p n i"),
+                scalar1=-1.0, scalar2=0.0, op0=ALU.mult, op1=ALU.add,
             )
 
         def quantise_wv(h):
@@ -303,10 +310,11 @@ def tile_list_gmu_relu_none_kernel(
             release("z", 0, t)
             sum_hv(0, t)
         gate_from_rest(0, 0)
+        round_wv_on_gpsimd(1, 0, slice(0, GPSIMD_COLS))
         make_rest(1, 0)
-        gate_from_rest(1, 0)
-        for a in range(PASSES):
-            round_wv(1, a)
+        make_gate(1, 0)
+        round_wv(1, 0, slice(GPSIMD_COLS, HALF))
+        round_wv(1, 1)
         t_by_rest(0, 0)
         sum_ht(1, 0)
         t_by_rest(0, 1)

from contextlib import ExitStack

import concourse.mybir as mybir

K, L, N, T, J = 1024, 512, 512, 2048, 1024
FLOPS = 2 * N * J * (2 * K + 2 * L)

F32 = mybir.dt.float32
BF16 = mybir.dt.bfloat16
I32 = mybir.dt.int32
U32 = mybir.dt.uint32
U16 = mybir.dt.uint16
U8 = mybir.dt.uint8
FP8X4 = mybir.dt.float8_e4m3fn_x4
FP4X4 = mybir.dt.float4_e2m1fn_x4
ACT = mybir.ActivationFunctionType
ALU = mybir.AluOpType

P = 128
PACK = 4
K_PASS = P * PACK
PASSES = K // K_PASS
BLOCKS = K_PASS // 32
QUAD = 32
ROWS = 4
CHUNK = 512
CHUNKS = J // CHUNK
N_TILES = N // P
HALF = N // 2
TAB_ROWS_AT = P - PASSES * BLOCKS
QUADS_BY_PORT = (0, 2, 1, 3)
BANKS = 8
WARM_PASSES = 4
GPSIMD_COLS = 96
PLUS, MINUS = 0, 1


def tile_list_gmu_relu_none_kernel(
    tc, tab_words, tab_scales, tab2_words, tab2_scales, zv_words, zv_scales, zt_words, zt_scales,
    b, wv, wt_words, wt_scales, offs, offs2, out,
):
    nc = tc.nc
    with ExitStack() as ctx:
        keep = ctx.enter_context(tc.tile_pool(name="keep", bufs=1))
        reused = ctx.enter_context(tc.tile_pool(name="reused", bufs=1))
        work = ctx.enter_context(tc.tile_pool(name="work", bufs=CHUNKS * N_TILES))
        psum = ctx.enter_context(tc.psum_pool(name="psum", bufs=1))

        def kept(name, shape, dtype):
            return keep.tile(shape, dtype, name=name, align_bytes=64)

        list1 = kept("list1", [P, J // 16], U16)
        list2 = kept("list2", [P, J // 16], U16)
        tab_w = kept("tab_w", [P, T], I32)
        tab2_w = kept("tab2_w", [P, T], I32)
        tab_s = kept("tab_s", [P, T], U8)
        tab2_s = kept("tab2_s", [P, T], U8)
        zv_w = [kept("zv_w%d" % h, [P, PASSES, 2 * HALF], U8) for h in range(2)]
        zt_w = kept("zt_w", [P, 2 * N], U8)
        wt_w = kept("wt_w", [P, N], I32)
        zv_s = kept("zv_s", [P, PASSES, N], U8)
        weight_s = kept("weight_s", [P, 2 * N], U8)
        zt_s = weight_s[:, 0:N]
        wt_s = weight_s[:, N : 2 * N]
        bias = kept("bias", [P, 2, N_TILES], F32)
        warm_in = kept("warm_in", [P, 8], F32)
        warm_out = kept("warm_out", [P, 8], F32)
        wv_w = [kept("wv_w%d" % h, [P, PASSES, HALF], U32) for h in range(2)]
        wv_s = [kept("wv_s%d" % h, [P, PASSES, HALF], U8) for h in range(2)]
        def shared(name, shape, dtype, kib):
            return reused.tile(shape, dtype, name=name, align_bytes=64, offset=kib * 1024)

        wv_bf = [shared("wv_bf%d" % h, [P, PASSES, HALF, PACK], BF16, 4 * h) for h in range(2)]
        last_raw = shared("last_raw", [P, PACK, HALF], F32, 9)
        held = {
            key: shared("%s%d%d" % key, [P, CHUNK], F32, kib)
            for key, kib in (
                (("result", 1, 0), 4), (("from_t", 0, 0), 14), (("result", 0, 1), 14),
                (("rest", 1, 1), 8), (("gate", 1, 1), 10), (("rest", 0, 2), 12), (("gate", 0, 2), 6),
                (("rest", 0, 3), 8), (("gate", 0, 3), 10), (("rest", 1, 2), 12), (("rest", 1, 3), 6),
            )
        }
        picked_s = kept("picked_s", [P, J], U8)
        planes = kept("planes", [P, PASSES, J], U8)
        picked2_s = [kept("picked2_s%d" % c, [P, CHUNK], U8) for c in range(CHUNKS)]
        parted = [kept("parted%d" % c, [P, PASSES, 2 * CHUNK], U8) for c in range(CHUNKS)]
        picked_w = [kept("picked_w%d" % c, [P, CHUNK], U32) for c in range(CHUNKS)]
        picked2_w = [kept("picked2_w%d" % c, [P, CHUNK], U32) for c in range(CHUNKS)]
        wv_raw = [[kept("wv_raw%d%d" % (h, a), [P, PACK, HALF], F32) for a in range(PASSES - h)] for h in range(2)]
        wv_raw[1].append(last_raw)

        def work_tile(kind, c, t):
            if (kind, c, t) in held:
                return held[kind, c, t]
            return work.tile([P, CHUNK], F32, name=kind)

        nc.vector.memset(warm_in[:], 0.0)
        nc.scalar.activation(out=warm_out[:], in_=warm_in[:], func=ACT.Sigmoid)

        nc.vector.memset(zv_s[:].rearrange("p a n -> p (a n)").bitcast(I32), 0)
        nc.vector.memset(tab_s[0:TAB_ROWS_AT, :].bitcast(I32), 0)
        nc.vector.memset(planes[:].rearrange("p a j -> p (a j)").bitcast(I32), 0)
        nc.vector.memset(tab2_s[:].bitcast(I32), 0)
        nc.vector.memset(weight_s[:].bitcast(I32), 0)

        def move_bytes(dst, src, queue=nc.sync):
            queue.dma_start(out=dst.bitcast(I32), in_=src.bitcast(I32))

        def load_wv(h, a):
            rows = wv[K_PASS * a : K_PASS * (a + 1), HALF * h : HALF * (h + 1)]
            nc.sync.dma_start(out=wv_raw[h][a][:], in_=rows.rearrange("(p i) n -> p i n", i=PACK))

        def load_zv(h):
            move_bytes(zv_w[h][:], zv_words[:, :, 2 * HALF * h : 2 * HALF * (h + 1)].rearrange("a p n -> p a n"))

        def load_wt(h):
            cols = slice(HALF * h, HALF * (h + 1))
            move_bytes(wt_w[:, cols], wt_words[0][:, cols, :].rearrange("p n i -> p (n i)"))

        def list_cols(c):
            return slice(c * CHUNK // 16, (c + 1) * CHUNK // 16)

        def chunk_cols(c):
            return slice(c * CHUNK, (c + 1) * CHUNK)

        move_bytes(zt_s[0:BLOCKS, :], zt_scales[0], nc.gpsimd)
        move_bytes(wt_s[0:BLOCKS, :], wt_scales[0], nc.gpsimd)
        with nc.allow_non_contiguous_dma(reason="one bias value to a partition"):
            nc.gpsimd.dma_start(out=bias[:, PLUS, :], in_=b.rearrange("(t p) -> p t", p=P))

        nc.sync.dma_start(list1[:], offs)
        move_bytes(tab_s[TAB_ROWS_AT:P, :], tab_scales.rearrange("a q t -> q a t"))
        move_bytes(tab_w[:], tab_words[0].rearrange("p t i -> p (t i)"))
        for r in range(ROWS):
            move_bytes(zv_s[r:P:QUAD, :, :], zv_scales[:, r:BLOCKS:ROWS, :].rearrange("a q n -> q a n"))
        move_bytes(tab2_w[:], tab2_words[0].rearrange("p t i -> p (t i)"))
        load_zv(0)
        nc.sync.dma_start(list2[:], offs2)
        nc.vector.tensor_copy(picked_s[:], tab_s[:].indirect(list1[:]))
        for g in QUADS_BY_PORT:
            first = TAB_ROWS_AT + PASSES * ROWS * g
            move_bytes(planes[QUAD * g : QUAD * g + ROWS, :, :], picked_s[first : first + PASSES * ROWS, :])
        load_wv(0, 0)
        for r in range(ROWS):
            move_bytes(tab2_s[r:P:QUAD, :], tab2_scales[0, r:BLOCKS:ROWS, :])
        load_zv(1)
        load_wv(0, 1)
        move_bytes(zt_w[:], zt_words[0])
        for g in QUADS_BY_PORT[1:]:
            move_bytes(weight_s[QUAD * g : QUAD * g + ROWS, :], weight_s[ROWS * g : ROWS * (g + 1), :])
        load_wt(0)
        load_wv(1, 0)
        load_wv(1, 1)
        load_wt(1)

        def part_passes(c):
            nc.vector.tensor_copy(parted[c][:].bitcast(U16), picked_w[c][:].bitcast(U16).rearrange("p (j a) -> p a j", a=PASSES))

        def round_wv(h, a, cols=slice(0, HALF)):
            nc.scalar.activation(
                out=wv_bf[h][:, a, cols].rearrange("p (n m) i -> p n i m", m=4),
                in_=wv_raw[h][a][:, :, cols].rearrange("p i (n m) -> p n i m", m=4),
                func=ACT.Copy, scale=-1.0,
            )

        def round_wv_on_gpsimd(h, a, cols):
            nc.gpsimd.tensor_scalar(
                out=wv_bf[h][:, a, cols], in0=wv_raw[h][a][:, :, cols].rearrange("p i n -> p n i"),
                scalar1=-1.0, scalar2=0.0, op0=ALU.mult, op1=ALU.add,
            )

        def quantise_wv(h):
            nc.vector.quantize_mx(
                out=wv_w[h][:].rearrange("p a n -> p (a n)").bitcast(FP8X4),
                scales=wv_s[h][:].rearrange("p a n -> p (a n)"),
                in_=wv_bf[h][:].rearrange("p a n i -> p (a n i)"),
            )

        free_banks = list(range(BANKS))
        sums, gate, rest, from_v, from_t = {}, {}, {}, {}, {}

        def new_sum(kind, c, t):
            bank = free_banks.pop(0)
            acc = psum.tile([P, CHUNK], F32, name=kind, tag="bank%d" % bank)
            sums[kind, c, t] = (acc, bank)
            return acc

        def release(kind, c, t):
            free_banks.append(sums[kind, c, t][1])

        def fp4_columns(words, t):
            return words[:, 2 * t * P : 2 * (t + 1) * P].bitcast(FP4X4)

        def open_z(c, t):
            acc = new_sum("z", c, t)
            for a in range(PASSES):
                nc.tensor.matmul_mx(
                    out=acc[:], lhsT=fp4_columns(zv_w[t // 2][:, a, :], t % 2), lhsT_scale=zv_s[:, a, t * P : (t + 1) * P],
                    rhs=parted[c][:, a, :].bitcast(FP4X4), rhs_scale=planes[:, a, chunk_cols(c)],
                    start=(a == 0), stop=False,
                )

        def close_z(c, t):
            nc.tensor.matmul_mx(
                out=sums["z", c, t][0][:], lhsT=fp4_columns(zt_w, t), lhsT_scale=zt_s[:, t * P : (t + 1) * P],
                rhs=picked2_w[c][:].bitcast(FP8X4), rhs_scale=picked2_s[c][:], start=False, stop=True,
            )

        def sum_z(c, t):
            open_z(c, t)
            close_z(c, t)

        def sum_ht(c, t):
            cols = slice(t * P, (t + 1) * P)
            nc.tensor.matmul_mx(
                out=new_sum("ht", c, t)[:], lhsT=wt_w[:, cols].bitcast(FP8X4), lhsT_scale=wt_s[:, cols],
                rhs=picked2_w[c][:].bitcast(FP8X4), rhs_scale=picked2_s[c][:], start=True, stop=True,
            )

        def sum_hv(c, t):
            h, cols = t // 2, slice(t % 2 * P, (t % 2 + 1) * P)
            acc = new_sum("hv", c, t)
            for a in range(PASSES):
                nc.tensor.matmul_mx(
                    out=acc[:], lhsT=wv_w[h][:, a, cols].bitcast(FP8X4), lhsT_scale=wv_s[h][:, a, cols],
                    rhs=parted[c][:, a, :].bitcast(FP4X4), rhs_scale=planes[:, a, chunk_cols(c)],
                    start=(a == 0), stop=(a == PASSES - 1),
                )

        def sigmoid_of_z(name, c, t, side, scale):
            result = work_tile(name, c, t)
            nc.scalar.activation(out=result[:], in_=sums["z", c, t][0][:], func=ACT.Sigmoid, bias=bias[:, side, t : t + 1], scale=scale)
            return result

        def make_rest(c, t):
            rest[c, t] = sigmoid_of_z("rest", c, t, MINUS, -1.0)

        def make_gate(c, t):
            gate[c, t] = sigmoid_of_z("gate", c, t, PLUS, 1.0)

        def gate_from_rest(c, t):
            gate[c, t] = work_tile("gate", c, t)
            nc.gpsimd.tensor_scalar(out=gate[c, t][:], in0=rest[c, t][:], scalar1=-1.0, scalar2=1.0, op0=ALU.mult, op1=ALU.add)

        def t_by_rest(c, t):
            from_t[c, t] = work_tile("from_t", c, t)
            nc.vector.scalar_tensor_tensor(
                out=from_t[c, t][:], in0=sums["ht", c, t][0][:], scalar=0.0, in1=rest[c, t][:], op0=ALU.max, op1=ALU.mult
            )
            release("ht", c, t)

        def v_by_gate(c, t):
            from_v[c, t] = work_tile("from_v", c, t)
            nc.vector.scalar_tensor_tensor(
                out=from_v[c, t][:], in0=sums["hv", c, t][0][:], scalar=0.0, in1=gate[c, t][:], op0=ALU.min, op1=ALU.mult
            )
            release("hv", c, t)

        def join_on_gpsimd(c, t):
            result = work_tile("result", c, t)
            nc.gpsimd.tensor_tensor(out=result[:], in0=from_t[c, t][:], in1=from_v[c, t][:], op=ALU.subtract)
            nc.sync.dma_start(out=out[t * P : (t + 1) * P, chunk_cols(c)], in_=result[:])

        def v_by_rest(c, t):
            from_v[c, t] = work_tile("from_v", c, t)
            nc.vector.scalar_tensor_tensor(
                out=from_v[c, t][:], in0=rest[c, t][:], scalar=1.0, in1=sums["hv", c, t][0][:], op0=ALU.subtract, op1=ALU.mult
            )
            release("hv", c, t)

        def join_on_vector(c, t, parts):
            result = work_tile("result", c, t)
            for i in range(parts):
                s = slice(i * CHUNK // parts, (i + 1) * CHUNK // parts)
                nc.vector.scalar_tensor_tensor(
                    out=result[:, s], in0=from_v[c, t][:, s], scalar=0.0, in1=from_t[c, t][:, s], op0=ALU.max, op1=ALU.add
                )
                nc.sync.dma_start(out=out[t * P : (t + 1) * P, chunk_cols(c)][:, s], in_=result[:, s])

        warm_sum = psum.tile([P, CHUNK], F32, name="warm_sum", tag="bank%d" % (BANKS - 1))
        for repeat in range(WARM_PASSES):
            nc.tensor.matmul_mx(
                out=warm_sum[:], lhsT=fp4_columns(zv_s[:, 0, :], 0), lhsT_scale=zv_s[:, 0, 0:P],
                rhs=zv_s[:].rearrange("p a n -> p (a n)").bitcast(FP4X4), rhs_scale=zv_s[:, 1, :], start=True, stop=True,
            )

        for c in range(CHUNKS):
            nc.vector.tensor_copy(picked_w[c][:], tab_w[:].bitcast(U32).indirect(list1[:, list_cols(c)]))
        for c in range(CHUNKS):
            part_passes(c)
        for c, t in ((0, 0), (0, 1), (1, 0), (1, 1), (0, 2), (0, 3)):
            open_z(c, t)
        nc.scalar.activation(out=bias[:, MINUS, :], in_=bias[:, PLUS, :], func=ACT.Copy, scale=-1.0)
        for a in range(PASSES):
            round_wv(0, a)
        for c in range(CHUNKS):
            nc.vector.tensor_copy(picked2_w[c][:], tab2_w[:].bitcast(U32).indirect(list2[:, list_cols(c)]))
        for c in range(CHUNKS):
            nc.vector.tensor_copy(picked2_s[c][:], tab2_s[:].indirect(list2[:, list_cols(c)]))
        quantise_wv(0)

        for t in range(2):
            close_z(0, t)
        for t in range(2):
            sum_ht(0, t)
        close_z(0, 2)
        close_z(1, 0)
        for t in range(2):
            make_rest(0, t)
            release("z", 0, t)
            sum_hv(0, t)
        gate_from_rest(0, 0)
        round_wv_on_gpsimd(1, 0, slice(0, GPSIMD_COLS))
        make_rest(1, 0)
        make_gate(1, 0)
        round_wv(1, 0, slice(GPSIMD_COLS, HALF))
        round_wv(1, 1)
        t_by_rest(0, 0)
        sum_ht(1, 0)
        t_by_rest(0, 1)
        sum_hv(1, 0)
        close_z(1, 1)
        close_z(0, 3)
        v_by_gate(0, 0)
        join_on_gpsimd(0, 0)
        sum_ht(1, 1)
        v_by_rest(0, 1)
        sum_hv(1, 1)
        release("z", 1, 0)
        sum_z(1, 2)
        t_by_rest(1, 0)
        sum_ht(0, 2)
        v_by_gate(1, 0)
        join_on_vector(0, 1, parts=1)
        quantise_wv(1)
        join_on_gpsimd(1, 0)
        sum_hv(0, 2)

        refills = {
            (1, 1): ((sum_z, 1, 3), (sum_ht, 0, 3), (sum_hv, 0, 3)),
            (0, 2): ((sum_ht, 1, 2), (sum_hv, 1, 2), (sum_ht, 1, 3)),
            (0, 3): ((sum_hv, 1, 3),),
        }
        for (c, t), later in refills.items():
            make_rest(c, t)
            make_gate(c, t)
            release("z", c, t)
            for reader, refill in zip((None, t_by_rest, v_by_gate), later + (None, None)):
                if reader:
                    reader(c, t)
                if refill:
                    refill[0](*refill[1:])
            join_on_gpsimd(c, t)

        last = ((1, 2), (1, 3))
        for c, t in last:
            make_rest(c, t)
        for c, t in last:
            t_by_rest(c, t)
            v_by_rest(c, t)
        for c, t in last:
            join_on_vector(c, t, parts=2)
